import numpy as np
import ml_dtypes


def mxq(x, axis, fmt="e4m3"):
    dtype, down = {"e4m3": (ml_dtypes.float8_e4m3fn, 7), "e5m2": (ml_dtypes.float8_e5m2, 14)}[fmt]
    v = np.moveaxis(np.asarray(x, np.float32).astype(ml_dtypes.bfloat16).astype(np.float64), axis, -1)
    blocks = v.reshape(v.shape[:-1] + (-1, 32))
    amax = np.abs(blocks).max(-1, keepdims=True)
    byte = np.maximum(np.where(amax > 0, np.frexp(amax)[1] - 1 + 127, 0) - down, 1)
    scale = np.exp2(byte - 127.0)
    codes = (blocks / scale).astype(np.float32).astype(dtype).astype(np.float64)
    return np.moveaxis((codes * scale).reshape(v.shape), -1, axis)


WIDE = False


def mx_kscale(k):
    if not WIDE:
        return np.ones(k)
    levels = np.array([10, -10, 5, -5, 0])
    if k % 512:
        return np.exp2(np.random.permutation(np.resize(levels, k // 32))).repeat(32)
    a = np.empty((k // 512, 16))
    for p in range(k // 512):
        a[p, :8] = np.random.permutation(np.resize(levels, 8))
        for g in range(8):
            far = levels[np.abs(levels - a[p, g]) >= 10]
            a[p, g + 8] = far[np.random.randint(len(far))]
    return np.exp2(a.ravel()).repeat(32)


def f64(x):
    return np.asarray(x).astype(np.float64)


def striped(idx):
    return np.tile(idx.reshape(-1, 16).T, (8, 1)).astype(np.uint16)


def unstriped(offs):
    return offs[:16].T.reshape(-1).astype(np.int64)


def pack_weight(w):
    k, n = w.shape
    w = f64(np.asarray(w, np.float32).astype(ml_dtypes.bfloat16)).reshape(k // 32, 32, n)
    amax = np.abs(w).max(1)
    byte = np.clip(np.where(amax > 0, np.frexp(amax)[1] - 1 + 127 - 7, 1), 1, 254)
    scaled = (w * np.exp2(127.0 - byte)[:, None, :]).reshape(k, n).astype(np.float32)
    words = np.ascontiguousarray(scaled.reshape(k // 512, 128, 4, n).transpose(0, 1, 3, 2)).astype(ml_dtypes.float8_e4m3fn).view(np.uint8)
    return words, np.ascontiguousarray(byte.astype(np.uint8).reshape(k // 512, 16, n))


def unpack_weight(words, scales):
    g, p, n, _ = words.shape
    vals = np.ascontiguousarray(words).view(ml_dtypes.float8_e4m3fn).astype(np.float64) * np.repeat(np.exp2(scales.astype(np.float64) - 127.0), 8, axis=1)[..., None]
    return vals.transpose(0, 1, 3, 2).reshape(g * 512, n)


def silu(v):
    return v / (1.0 + np.exp(-np.maximum(v, -700.0)))


K, T, S, H, N, U = 512, 4096, 1024, 512, 256, 2048
P = 2 ** 7


def setup_inputs():
    n = np.random.standard_normal
    s = mx_kscale(K)[:, None]
    u = mx_kscale(H)
    packed_xT = pack_weight(n((K, T)) * s)
    return {
        "x_words": packed_xT[0],
        "x_scales": packed_xT[1],
        "gate": np.tile(np.random.uniform(0.5, 1.5, S), (P, 1)).astype(np.float32),
        "w1": (n((K, H)) / np.sqrt(K) / s).astype(np.float32),
        "w3": (n((K, H)) / np.sqrt(K) / s * u).astype(np.float32),
        "w2": (n((H, N)) / np.sqrt(H) / u[:, None]).astype(np.float32),
        "offs": striped(np.random.permutation(T)[:S]),
        "dst": striped(np.random.permutation(U)[:S]),
    }


def reference(x_words, x_scales, gate, w1, w3, w2, offs, dst):
    xq = unpack_weight(x_words, x_scales)[:, unstriped(offs)]
    h = (silu(mxq(f64(w1), 0, "e4m3").T @ xq)) * ((mxq(f64(w3), 0, "e4m3").T @ xq))
    y = mxq(f64(w2), 0, "e4m3").T @ mxq(h, 0, "e4m3")
    out = np.zeros((N, U))
    out[:, unstriped(dst)] = y * f64(gate)[:1]
    return out

@@ -1,0 +1,181 @@
+from contextlib import ExitStack
+
+import concourse.mybir as mybir
+
+K, T, S, H, N, U = 512, 4096, 1024, 512, 256, 2048
+FLOPS = 2 * K * H * S * 2 + 2 * H * N * S
+
+F32 = mybir.dt.float32
+BF16 = mybir.dt.bfloat16
+I32 = mybir.dt.int32
+U32 = mybir.dt.uint32
+U16 = mybir.dt.uint16
+U8 = mybir.dt.uint8
+FP8X4 = mybir.dt.float8_e4m3fn_x4
+SILU = mybir.ActivationFunctionType.Silu
+MULT = mybir.AluOpType.mult
+
+P = 128
+PACK = 4
+RUN = 4
+LIST = 16
+HALF = H // 2
+GATHER = 512
+BANK_TOKENS = 128
+CHUNKS = (256, 256, 512)
+
+
+def tile_picked_route2_glusilu_p_kernel(
+    tc, x_words, x_scales, gate, w1, w3, w2, offs, dst, out
+):
+    nc = tc.nc
+    with ExitStack() as ctx:
+        keep = ctx.enter_context(tc.tile_pool(name="keep", bufs=1))
+        psum = ctx.enter_context(tc.psum_pool(name="psum", bufs=1))
+
+        offs_sb = keep.tile([P, S // LIST], U16, name="offs_sb")
+        dst_sb = keep.tile([P, S // LIST], U16, name="dst_sb")
+        words = keep.tile([P, T], I32, name="words")
+        planes = keep.tile([P, T], U8, name="planes")
+        gate_sb = keep.tile([P, S], F32, name="gate_sb")
+        windows = [keep.tile([P, U], F32, name=f"window{b}") for b in range(N // P)]
+
+        warm = keep.tile([P, 8], F32, name="warm")
+        warm_out = keep.tile([P, 8], F32, name="warm_out")
+
+        nc.gpsimd.memset(warm[:], 0.0)
+        nc.gpsimd.memset(planes[:].bitcast(I32), 0)
+        nc.sync.dma_start(offs_sb[:], offs)
+        nc.sync.dma_start(words[:], x_words[0].rearrange("p c r -> p (c r)").bitcast(I32))
+        for q in range(4):
+            nc.scalar.dma_start(
+                planes[32 * q : 32 * q + 4, :].bitcast(I32), x_scales[0, 4 * q : 4 * q + 4, :].bitcast(I32)
+            )
+        nc.scalar.activation(warm_out[:], warm[:], SILU)
+        for window in windows:
+            nc.gpsimd.memset(window[:], 0.0)
+
+        def load_halves(w, name):
+            rows = w.rearrange("(p j) c -> p j c", j=PACK)
+            halves = []
+            for hf in range(2):
+                raw = keep.tile([P, PACK, HALF], F32, name=f"{name}_raw{hf}")
+                nc.sync.dma_start(raw[:], rows[:, :, hf * HALF : (hf + 1) * HALF])
+                halves.append(raw)
+            return halves
+
+        w1_raw = load_halves(w1, "w1")
+        w3_raw = load_halves(w3, "w3")
+        w2_raw = keep.tile([P, PACK, N], F32, name="w2_raw")
+        w2_rows = w2.rearrange("(u t e) n -> e u t n", t=PACK, e=RUN)
+        for e in range(RUN):
+            nc.sync.dma_start(w2_raw[e:P:RUN], w2_rows[e])
+        nc.sync.dma_start(gate_sb[:], gate)
+        nc.sync.dma_start(dst_sb[:], dst)
+
+        x_planes = keep.tile([P, S], U8, name="x_planes", align_bytes=64)
+        nc.vector.tensor_copy(x_planes[:], planes[:].indirect(offs_sb[:]))
+        x_codes = []
+        for g in range(S // GATHER):
+            picked = keep.tile([P, GATHER], U32, name=f"x_codes{g}", align_bytes=64)
+            cols = slice(g * GATHER // LIST, (g + 1) * GATHER // LIST)
+            nc.vector.tensor_copy(picked[:], words[:].bitcast(U32).indirect(offs_sb[:, cols]))
+            x_codes.append(picked)
+
+        def quantize_first(halves, copy, name):
+            grouped = keep.tile([P, PACK, P, PACK], BF16, name=f"{name}_grouped", align_bytes=64)
+            for hf, raw in enumerate(halves):
+                part = grouped[:, :, hf * (P // 2) : (hf + 1) * (P // 2), :]
+                copy(
+                    part.rearrange("p t (u e) j -> p t u j e", e=RUN),
+                    raw[:].rearrange("p j (u t e) -> p t u j e", t=PACK, e=RUN),
+                )
+            codes = keep.tile([P, H], U32, name=f"{name}_codes", align_bytes=64)
+            scales = keep.tile([P, H], U8, name=f"{name}_scales", align_bytes=64)
+            nc.vector.quantize_mx(
+                out=codes[:].bitcast(FP8X4), scales=scales[:], in_=grouped[:].rearrange("p t m j -> p (t m j)")
+            )
+            return codes, scales
+
+        w1_q = quantize_first(w1_raw, nc.scalar.copy, "w1")
+        w3_q = quantize_first(w3_raw, nc.vector.tensor_copy, "w3")
+
+        def first_product(w_q, j0, tag):
+            codes, scales = w_q
+            bank = psum.tile([P, PACK, BANK_TOKENS], F32, name=tag, tag=tag, bufs=3)
+            picked = x_codes[j0 // GATHER]
+            c0 = j0 % GATHER
+            for t in range(PACK):
+                nc.tensor.matmul_mx(
+                    out=bank[:, t, :],
+                    lhsT=codes[:, t * P : (t + 1) * P].bitcast(FP8X4),
+                    lhsT_scale=scales[:, t * P : (t + 1) * P],
+                    rhs=picked[:, c0 : c0 + BANK_TOKENS].bitcast(FP8X4),
+                    rhs_scale=x_planes[:, j0 : j0 + BANK_TOKENS],
+                    start=True,
+                    stop=True,
+                )
+            return bank[:].rearrange("p t n -> p n t")
+
+        def hidden(j0, width):
+            h = keep.tile([P, width, PACK], BF16, name=f"h{j0}", align_bytes=64)
+            for c0 in range(0, width, BANK_TOKENS):
+                act = keep.tile([P, BANK_TOKENS, PACK], F32, name=f"act{j0 + c0}")
+                nc.scalar.activation(act[:], first_product(w1_q, j0 + c0, "up1"), SILU)
+                nc.vector.tensor_tensor(
+                    h[:, c0 : c0 + BANK_TOKENS, :], first_product(w3_q, j0 + c0, "up3"), act[:], MULT
+                )
+            codes = keep.tile([P, width], U32, name=f"h_codes{j0}", align_bytes=64)
+            scales = keep.tile([P, width], U8, name=f"h_scales{j0}", align_bytes=64)
+            nc.vector.quantize_mx(
+                out=codes[:].bitcast(FP8X4), scales=scales[:], in_=h[:].rearrange("p n t -> p (n t)")
+            )
+            return codes, scales
+
+        def quantize_w2():
+            grouped = keep.tile([P, N, PACK], BF16, name="w2_grouped", align_bytes=64)
+            nc.scalar.copy(
+                grouped[:].rearrange("p (c i) t -> p c t i", i=RUN),
+                w2_raw[:].rearrange("p t (c i) -> p c t i", i=RUN),
+            )
+            codes = keep.tile([P, N], U32, name="w2_codes", align_bytes=64)
+            scales = keep.tile([P, N], U8, name="w2_scales", align_bytes=64)
+            nc.vector.quantize_mx(
+                out=codes[:].bitcast(FP8X4), scales=scales[:], in_=grouped[:].rearrange("p n t -> p (n t)")
+            )
+            return codes, scales
+
+        def second_product(h_q, j0, width):
+            ys = []
+            for b in range(N // P):
+                bank = psum.tile([P, width], F32, name="down", tag="down", bufs=2)
+                nc.tensor.matmul_mx(
+                    out=bank[:],
+                    lhsT=w2_q[0][:, b * P : (b + 1) * P].bitcast(FP8X4),
+                    lhsT_scale=w2_q[1][:, b * P : (b + 1) * P],
+                    rhs=h_q[0][:].bitcast(FP8X4),
+                    rhs_scale=h_q[1][:],
+                    start=True,
+                    stop=True,
+                )
+                y = keep.tile([P, width], F32, name=f"y{j0}_{b}")
+                nc.scalar.copy(y[:], bank[:])
+                ys.append(y)
+            return ys
+
+        def scatter(ys, j0, width):
+            places = dst_sb[:, j0 // LIST : (j0 + width) // LIST]
+            for window, y in zip(windows, ys):
+                nc.vector.tensor_tensor(window[:].indirect(places), y[:], gate_sb[:, j0 : j0 + width], MULT)
+
+        starts = [sum(CHUNKS[:c]) for c in range(len(CHUNKS))]
+        h_q = hidden(starts[0], CHUNKS[0])
+        w2_q = quantize_w2()
+        ys = second_product(h_q, starts[0], CHUNKS[0])
+        for c in range(1, len(CHUNKS)):
+            h_q = hidden(starts[c], CHUNKS[c])
+            scatter(ys, starts[c - 1], CHUNKS[c - 1])
+            ys = second_product(h_q, starts[c], CHUNKS[c])
+        scatter(ys, starts[-1], CHUNKS[-1])
+        for b, window in enumerate(windows):
+            nc.sync.dma_start(out[b * P : (b + 1) * P, :], window[:])

@@ -22,7 +22,10 @@ LIST = 16
 HALF = H // 2
 GATHER = 512
 BANK_TOKENS = 128
-CHUNKS = (256, 256, 512)
+EDGE = 8
+CHUNK = 256
+SCATTERS = (256, 384, 384)
+AHEAD = 3
 
 
 def tile_picked_route2_glusilu_p_kernel(
@@ -35,43 +38,34 @@ def tile_picked_route2_glusilu_p_kernel(
 
         offs_sb = keep.tile([P, S // LIST], U16, name="offs_sb")
         dst_sb = keep.tile([P, S // LIST], U16, name="dst_sb")
-        words = keep.tile([P, T], I32, name="words")
-        planes = keep.tile([P, T], U8, name="planes")
-        gate_sb = keep.tile([P, S], F32, name="gate_sb")
+        planes = keep.tile([P, T], U8, name="planes", tag="planes", align_bytes=64)
         windows = [keep.tile([P, U], F32, name=f"window{b}") for b in range(N // P)]
+        zeros_a = keep.tile([P, EDGE], F32, name="zeros_a", tag="words")
+        zeros_b = keep.tile([P, EDGE], F32, name="zeros_b", tag="held")
 
-        warm = keep.tile([P, 8], F32, name="warm")
-        warm_out = keep.tile([P, 8], F32, name="warm_out")
+        nc.vector.memset(zeros_a[:], 0.0)
+        nc.vector.memset(zeros_b[:], 0.0)
+        nc.vector.memset(planes[:].bitcast(I32), 0)
+        nc.vector.tensor_tensor(windows[0][:, :EDGE], zeros_a[:], zeros_b[:], MULT)
+        nc.scalar.activation(windows[1][:, :EDGE], windows[0][:, :EDGE], SILU)
+        for window in windows:
+            nc.vector.memset(window[:, EDGE:], 0.0)
 
-        nc.gpsimd.memset(warm[:], 0.0)
-        nc.gpsimd.memset(planes[:].bitcast(I32), 0)
         nc.sync.dma_start(offs_sb[:], offs)
-        nc.sync.dma_start(words[:], x_words[0].rearrange("p c r -> p (c r)").bitcast(I32))
+        nc.sync.dma_start(dst_sb[:], dst)
+        w1_rows = w1.rearrange("(p j) c -> p j c", j=PACK)
+        w3_rows = w3.rearrange("(p j) c -> p j c", j=PACK)
+        w1_raw = keep.tile([P, PACK, H], F32, name="w1_raw", tag="w1_raw")
+        nc.sync.dma_start(w1_raw[:], w1_rows)
         for q in range(4):
-            nc.scalar.dma_start(
+            nc.sync.dma_start(
                 planes[32 * q : 32 * q + 4, :].bitcast(I32), x_scales[0, 4 * q : 4 * q + 4, :].bitcast(I32)
             )
-        nc.scalar.activation(warm_out[:], warm[:], SILU)
-        for window in windows:
-            nc.gpsimd.memset(window[:], 0.0)
-
-        def load_halves(w, name):
-            rows = w.rearrange("(p j) c -> p j c", j=PACK)
-            halves = []
-            for hf in range(2):
-                raw = keep.tile([P, PACK, HALF], F32, name=f"{name}_raw{hf}")
-                nc.sync.dma_start(raw[:], rows[:, :, hf * HALF : (hf + 1) * HALF])
-                halves.append(raw)
-            return halves
-
-        w1_raw = load_halves(w1, "w1")
-        w3_raw = load_halves(w3, "w3")
-        w2_raw = keep.tile([P, PACK, N], F32, name="w2_raw")
-        w2_rows = w2.rearrange("(u t e) n -> e u t n", t=PACK, e=RUN)
-        for e in range(RUN):
-            nc.sync.dma_start(w2_raw[e:P:RUN], w2_rows[e])
-        nc.sync.dma_start(gate_sb[:], gate)
-        nc.sync.dma_start(dst_sb[:], dst)
+        words = keep.tile([P, T], I32, name="words", tag="words")
+        nc.sync.dma_start(words[:], x_words[0].rearrange("p c r -> p (c r)").bitcast(I32))
+        held = keep.tile([P, 2, PACK, HALF], F32, name="held", tag="held")
+        for i, rows in enumerate((w3_rows[:, :, :HALF], w3_rows[:, :, HALF:])):
+            nc.sync.dma_start(held[:, i], rows)
 
         x_planes = keep.tile([P, S], U8, name="x_planes", align_bytes=64)
         nc.vector.tensor_copy(x_planes[:], planes[:].indirect(offs_sb[:]))
@@ -82,27 +76,52 @@ def tile_picked_route2_glusilu_p_kernel(
             nc.vector.tensor_copy(picked[:], words[:].bitcast(U32).indirect(offs_sb[:, cols]))
             x_codes.append(picked)
 
-        def quantize_first(halves, copy, name):
+        def quantize_first(pieces, calls, name, codes_tag):
             grouped = keep.tile([P, PACK, P, PACK], BF16, name=f"{name}_grouped", align_bytes=64)
-            for hf, raw in enumerate(halves):
-                part = grouped[:, :, hf * (P // 2) : (hf + 1) * (P // 2), :]
+            for raw, c0, slots, copy in pieces:
+                m = slice(c0 // PACK, (c0 + raw.shape[2]) // PACK)
                 copy(
-                    part.rearrange("p t (u e) j -> p t u j e", e=RUN),
-                    raw[:].rearrange("p j (u t e) -> p t u j e", t=PACK, e=RUN),
+                    grouped[:, slots, m, :].rearrange("p t (u e) j -> p t u j e", e=RUN),
+                    raw.rearrange("p j (u t e) -> p t u j e", t=PACK, e=RUN)[:, slots],
                 )
-            codes = keep.tile([P, H], U32, name=f"{name}_codes", align_bytes=64)
+            codes = keep.tile([P, H], U32, name=f"{name}_codes", tag=codes_tag, align_bytes=64)
             scales = keep.tile([P, H], U8, name=f"{name}_scales", align_bytes=64)
-            nc.vector.quantize_mx(
-                out=codes[:].bitcast(FP8X4), scales=scales[:], in_=grouped[:].rearrange("p t m j -> p (t m j)")
-            )
+            step = PACK // calls
+            for t in range(0, PACK, step):
+                cols = slice(t * P, (t + step) * P)
+                nc.vector.quantize_mx(
+                    out=codes[:, cols].bitcast(FP8X4),
+                    scales=scales[:, cols],
+                    in_=grouped[:, t : t + step].rearrange("p t m j -> p (t m j)"),
+                )
             return codes, scales
 
-        w1_q = quantize_first(w1_raw, nc.scalar.copy, "w1")
-        w3_q = quantize_first(w3_raw, nc.vector.tensor_copy, "w3")
+        w1_q = quantize_first([(w1_raw[:], 0, slice(0, PACK), nc.scalar.copy)], 1, "w1", "planes")
 
-        def first_product(w_q, j0, tag):
+        late = keep.tile([P, PACK * N + S], F32, name="late", tag="w1_raw")
+        w2_raw = late[:, : PACK * N].rearrange("p (t n) -> p t n", t=PACK)
+        gate_sb = late[:, PACK * N :]
+        w2_rows = w2.rearrange("(u t e) n -> e u t n", t=PACK, e=RUN)
+        for e in range(RUN):
+            nc.sync.dma_start(w2_raw[e:P:RUN], w2_rows[e])
+        nc.sync.dma_start(gate_sb, gate)
+
+        w3_q = quantize_first(
+            [
+                (held[:, 0], 0, slice(0, PACK), nc.scalar.copy),
+                (held[:, 1], HALF, slice(0, 2), nc.vector.tensor_copy),
+                (held[:, 1], HALF, slice(2, PACK), nc.scalar.copy),
+            ],
+            2,
+            "w3",
+            "w3_codes",
+        )
+
+        def first_product(w_q, j0, side):
             codes, scales = w_q
-            bank = psum.tile([P, PACK, BANK_TOKENS], F32, name=tag, tag=tag, bufs=3)
+            k = j0 // BANK_TOKENS
+            tag = f"up{k % AHEAD}_{(k // AHEAD + side) % 2}"
+            bank = psum.tile([P, PACK, BANK_TOKENS], F32, name="up", tag=tag)
             picked = x_codes[j0 // GATHER]
             c0 = j0 % GATHER
             for t in range(PACK):
@@ -117,13 +136,14 @@ def tile_picked_route2_glusilu_p_kernel(
                 )
             return bank[:].rearrange("p t n -> p n t")
 
-        def hidden(j0, width):
-            h = keep.tile([P, width, PACK], BF16, name=f"h{j0}", align_bytes=64)
+        def hidden(j0, h_tag):
+            width = CHUNK
+            h = keep.tile([P, width, PACK], BF16, name="h", tag=h_tag, align_bytes=64)
             for c0 in range(0, width, BANK_TOKENS):
                 act = keep.tile([P, BANK_TOKENS, PACK], F32, name=f"act{j0 + c0}")
-                nc.scalar.activation(act[:], first_product(w1_q, j0 + c0, "up1"), SILU)
+                nc.scalar.activation(act[:], first_product(w1_q, j0 + c0, 0), SILU)
                 nc.vector.tensor_tensor(
-                    h[:, c0 : c0 + BANK_TOKENS, :], first_product(w3_q, j0 + c0, "up3"), act[:], MULT
+                    h[:, c0 : c0 + BANK_TOKENS, :], first_product(w3_q, j0 + c0, 1), act[:], MULT
                 )
             codes = keep.tile([P, width], U32, name=f"h_codes{j0}", align_bytes=64)
             scales = keep.tile([P, width], U8, name=f"h_scales{j0}", align_bytes=64)
@@ -133,10 +153,10 @@ def tile_picked_route2_glusilu_p_kernel(
             return codes, scales
 
         def quantize_w2():
-            grouped = keep.tile([P, N, PACK], BF16, name="w2_grouped", align_bytes=64)
+            grouped = keep.tile([P, N, PACK], BF16, name="w2_grouped", tag="w2_grouped", align_bytes=64)
             nc.scalar.copy(
                 grouped[:].rearrange("p (c i) t -> p c t i", i=RUN),
-                w2_raw[:].rearrange("p t (c i) -> p c t i", i=RUN),
+                w2_raw.rearrange("p t (c i) -> p c t i", i=RUN),
             )
             codes = keep.tile([P, N], U32, name="w2_codes", align_bytes=64)
             scales = keep.tile([P, N], U8, name="w2_scales", align_bytes=64)
@@ -145,10 +165,11 @@ def tile_picked_route2_glusilu_p_kernel(
             )
             return codes, scales
 
-        def second_product(h_q, j0, width):
-            ys = []
-            for b in range(N // P):
-                bank = psum.tile([P, width], F32, name="down", tag="down", bufs=2)
+        ys = [keep.tile([P, S], F32, name=f"y{b}") for b in range(N // P)]
+
+        def second_product(h_q, j0):
+            for b, y in enumerate(ys):
+                bank = psum.tile([P, CHUNK], F32, name="down", tag="down", bufs=2)
                 nc.tensor.matmul_mx(
                     out=bank[:],
                     lhsT=w2_q[0][:, b * P : (b + 1) * P].bitcast(FP8X4),
@@ -158,24 +179,19 @@ def tile_picked_route2_glusilu_p_kernel(
                     start=True,
                     stop=True,
                 )
-                y = keep.tile([P, width], F32, name=f"y{j0}_{b}")
-                nc.scalar.copy(y[:], bank[:])
-                ys.append(y)
-            return ys
+                nc.scalar.copy(y[:, j0 : j0 + CHUNK], bank[:])
 
-        def scatter(ys, j0, width):
+        h_q = hidden(0, "h_a")
+        w2_q = quantize_w2()
+        second_product(h_q, 0)
+        for c, h_tag in enumerate(("h_b", "h_a", "w2_grouped"), 1):
+            second_product(hidden(c * CHUNK, h_tag), c * CHUNK)
+        j0 = 0
+        for width in SCATTERS:
+            cols = slice(j0, j0 + width)
             places = dst_sb[:, j0 // LIST : (j0 + width) // LIST]
             for window, y in zip(windows, ys):
-                nc.vector.tensor_tensor(window[:].indirect(places), y[:], gate_sb[:, j0 : j0 + width], MULT)
-
-        starts = [sum(CHUNKS[:c]) for c in range(len(CHUNKS))]
-        h_q = hidden(starts[0], CHUNKS[0])
-        w2_q = quantize_w2()
-        ys = second_product(h_q, starts[0], CHUNKS[0])
-        for c in range(1, len(CHUNKS)):
-            h_q = hidden(starts[c], CHUNKS[c])
-            scatter(ys, starts[c - 1], CHUNKS[c - 1])
-            ys = second_product(h_q, starts[c], CHUNKS[c])
-        scatter(ys, starts[-1], CHUNKS[-1])
+                nc.vector.tensor_tensor(window[:].indirect(places), y[:, cols], gate_sb[:, cols], MULT)
+            j0 += width
         for b, window in enumerate(windows):
             nc.sync.dma_start(out[b * P : (b + 1) * P, :], window[:])

@@ -24,8 +24,8 @@ GATHER = 512
 BANK_TOKENS = 128
 EDGE = 8
 CHUNK = 256
-SCATTERS = (256, 384, 384)
 AHEAD = 3
+ON_GPSIMD = 3
 
 
 def tile_picked_route2_glusilu_p_kernel(
@@ -63,9 +63,8 @@ def tile_picked_route2_glusilu_p_kernel(
             )
         words = keep.tile([P, T], I32, name="words", tag="words")
         nc.sync.dma_start(words[:], x_words[0].rearrange("p c r -> p (c r)").bitcast(I32))
-        held = keep.tile([P, 2, PACK, HALF], F32, name="held", tag="held")
-        for i, rows in enumerate((w3_rows[:, :, :HALF], w3_rows[:, :, HALF:])):
-            nc.sync.dma_start(held[:, i], rows)
+        w3_raw = keep.tile([P, PACK, H], F32, name="w3_raw", tag="held")
+        nc.sync.dma_start(w3_raw[:], w3_rows)
 
         x_planes = keep.tile([P, S], U8, name="x_planes", align_bytes=64)
         nc.vector.tensor_copy(x_planes[:], planes[:].indirect(offs_sb[:]))
@@ -81,8 +80,8 @@ def tile_picked_route2_glusilu_p_kernel(
             for raw, c0, slots, copy in pieces:
                 m = slice(c0 // PACK, (c0 + raw.shape[2]) // PACK)
                 copy(
-                    grouped[:, slots, m, :].rearrange("p t (u e) j -> p t u j e", e=RUN),
-                    raw.rearrange("p j (u t e) -> p t u j e", t=PACK, e=RUN)[:, slots],
+                    grouped[:, slots, m, :].rearrange("p t m j -> p m j t"),
+                    raw.rearrange("p j (m t) -> p m j t", t=PACK)[:, :, :, slots],
                 )
             codes = keep.tile([P, H], U32, name=f"{name}_codes", tag=codes_tag, align_bytes=64)
             scales = keep.tile([P, H], U8, name=f"{name}_scales", align_bytes=64)
@@ -96,30 +95,26 @@ def tile_picked_route2_glusilu_p_kernel(
                 )
             return codes, scales
 
-        w1_q = quantize_first([(w1_raw[:], 0, slice(0, PACK), nc.scalar.copy)], 1, "w1", "planes")
+        w1_q = quantize_first([(w1_raw[:], 0, slice(0, 2), nc.scalar.copy), (w1_raw[:], 0, slice(2, PACK), nc.scalar.copy)], 1, "w1", "planes")
 
         late = keep.tile([P, PACK * N + S], F32, name="late", tag="w1_raw")
         w2_raw = late[:, : PACK * N].rearrange("p (t n) -> p t n", t=PACK)
         gate_sb = late[:, PACK * N :]
-        w2_rows = w2.rearrange("(u t e) n -> e u t n", t=PACK, e=RUN)
-        for e in range(RUN):
-            nc.sync.dma_start(w2_raw[e:P:RUN], w2_rows[e])
+        nc.sync.dma_start(w2_raw, w2.rearrange("(p t) n -> p t n", t=PACK))
         nc.sync.dma_start(gate_sb, gate)
 
         w3_q = quantize_first(
             [
-                (held[:, 0], 0, slice(0, PACK), nc.scalar.copy),
-                (held[:, 1], HALF, slice(0, 2), nc.vector.tensor_copy),
-                (held[:, 1], HALF, slice(2, PACK), nc.scalar.copy),
+                (w3_raw[:], 0, slice(0, 2), nc.vector.tensor_copy),
+                (w3_raw[:], 0, slice(2, PACK), nc.scalar.copy),
             ],
             2,
             "w3",
             "w3_codes",
         )
 
-        def first_product(w_q, j0, side):
+        def first_product(w_q, j0, k, side):
             codes, scales = w_q
-            k = j0 // BANK_TOKENS
             tag = f"up{k % AHEAD}_{(k // AHEAD + side) % 2}"
             bank = psum.tile([P, PACK, BANK_TOKENS], F32, name="up", tag=tag)
             picked = x_codes[j0 // GATHER]
@@ -136,62 +131,82 @@ def tile_picked_route2_glusilu_p_kernel(
                 )
             return bank[:].rearrange("p t n -> p n t")
 
-        def hidden(j0, h_tag):
-            width = CHUNK
-            h = keep.tile([P, width, PACK], BF16, name="h", tag=h_tag, align_bytes=64)
-            for c0 in range(0, width, BANK_TOKENS):
-                act = keep.tile([P, BANK_TOKENS, PACK], F32, name=f"act{j0 + c0}")
-                nc.scalar.activation(act[:], first_product(w1_q, j0 + c0, 0), SILU)
-                nc.vector.tensor_tensor(
-                    h[:, c0 : c0 + BANK_TOKENS, :], first_product(w3_q, j0 + c0, 1), act[:], MULT
-                )
-            codes = keep.tile([P, width], U32, name=f"h_codes{j0}", align_bytes=64)
-            scales = keep.tile([P, width], U8, name=f"h_scales{j0}", align_bytes=64)
+        def quantize_h(h, name):
+            width = h.shape[1]
+            codes = keep.tile([P, width], U32, name=f"{name}_codes", align_bytes=64)
+            scales = keep.tile([P, width], U8, name=f"{name}_scales", align_bytes=64)
             nc.vector.quantize_mx(
-                out=codes[:].bitcast(FP8X4), scales=scales[:], in_=h[:].rearrange("p n t -> p (n t)")
+                out=codes[:].bitcast(FP8X4), scales=scales[:], in_=h.rearrange("p n t -> p (n t)")
             )
             return codes, scales
 
-        def quantize_w2():
-            grouped = keep.tile([P, N, PACK], BF16, name="w2_grouped", tag="w2_grouped", align_bytes=64)
-            nc.scalar.copy(
-                grouped[:].rearrange("p (c i) t -> p c t i", i=RUN),
-                w2_raw.rearrange("p t (c i) -> p c t i", i=RUN),
+        first_acts = keep.tile([P, AHEAD, BANK_TOKENS, PACK], F32, name="first_acts", tag="held")
+        lin_sb = keep.tile([P, ON_GPSIMD * BANK_TOKENS * PACK], F32, name="lin_sb")
+        banks = S // BANK_TOKENS
+
+        def hidden(j0, h, order):
+            for i, c0 in enumerate(order):
+                k = j0 // BANK_TOKENS + i
+                if k < AHEAD:
+                    act = first_acts[:, k]
+                else:
+                    act = keep.tile([P, BANK_TOKENS, PACK], F32, name=f"act{k}")[:]
+                nc.scalar.activation(act, first_product(w1_q, j0 + c0, k, 0), SILU)
+                lin = first_product(w3_q, j0 + c0, k, 1)
+                h_part = h[:, c0 : c0 + BANK_TOKENS, :]
+                if k >= banks - ON_GPSIMD:
+                    lin_part = lin_sb[:, c0 * PACK : (c0 + BANK_TOKENS) * PACK].rearrange("p (n t) -> p n t", t=PACK)
+                    nc.scalar.copy(lin_part, lin)
+                    nc.gpsimd.tensor_tensor(h_part, lin_part, act, MULT)
+                else:
+                    nc.vector.tensor_tensor(h_part, lin, act, MULT)
+            return quantize_h(h, f"h{j0}")
+
+        def second_product(h_q, b):
+            bank = psum.tile([P, h_q[0].shape[1]], F32, name="down", tag=f"down{b}")
+            nc.tensor.matmul_mx(
+                out=bank[:],
+                lhsT=w2_q[0][:, b * P : (b + 1) * P].bitcast(FP8X4),
+                lhsT_scale=w2_q[1][:, b * P : (b + 1) * P],
+                rhs=h_q[0][:].bitcast(FP8X4),
+                rhs_scale=h_q[1][:],
+                start=True,
+                stop=True,
             )
-            codes = keep.tile([P, N], U32, name="w2_codes", align_bytes=64)
-            scales = keep.tile([P, N], U8, name="w2_scales", align_bytes=64)
-            nc.vector.quantize_mx(
-                out=codes[:].bitcast(FP8X4), scales=scales[:], in_=grouped[:].rearrange("p n t -> p (n t)")
-            )
-            return codes, scales
+            return bank
 
-        ys = [keep.tile([P, S], F32, name=f"y{b}") for b in range(N // P)]
+        def places(j0, width):
+            return dst_sb[:, j0 // LIST : (j0 + width) // LIST]
 
-        def second_product(h_q, j0):
-            for b, y in enumerate(ys):
-                bank = psum.tile([P, CHUNK], F32, name="down", tag="down", bufs=2)
-                nc.tensor.matmul_mx(
-                    out=bank[:],
-                    lhsT=w2_q[0][:, b * P : (b + 1) * P].bitcast(FP8X4),
-                    lhsT_scale=w2_q[1][:, b * P : (b + 1) * P],
-                    rhs=h_q[0][:].bitcast(FP8X4),
-                    rhs_scale=h_q[1][:],
-                    start=True,
-                    stop=True,
-                )
-                nc.scalar.copy(y[:, j0 : j0 + CHUNK], bank[:])
+        def gate_then_scatter(h_q, j0, b, gated):
+            nc.vector.tensor_tensor(gated, second_product(h_q, b)[:], gate_sb[:, j0 : j0 + CHUNK], MULT)
+            nc.vector.tensor_copy(windows[b][:].indirect(places(j0, CHUNK)), gated)
 
-        h_q = hidden(0, "h_a")
-        w2_q = quantize_w2()
-        second_product(h_q, 0)
-        for c, h_tag in enumerate(("h_b", "h_a", "w2_grouped"), 1):
-            second_product(hidden(c * CHUNK, h_tag), c * CHUNK)
-        j0 = 0
-        for width in SCATTERS:
-            cols = slice(j0, j0 + width)
-            places = dst_sb[:, j0 // LIST : (j0 + width) // LIST]
-            for window, y in zip(windows, ys):
-                nc.vector.tensor_tensor(window[:].indirect(places), y[:, cols], gate_sb[:, cols], MULT)
-            j0 += width
+        rest = S - 2 * CHUNK
+        work = keep.tile([P, 2 * CHUNK + 2 * rest], F32, name="work", align_bytes=64)
+        h0 = keep.tile([P, CHUNK, PACK], BF16, name="h0", align_bytes=64)
+        gated10 = keep.tile([P, CHUNK], F32, name="gated10")
+
+        def h_view(word0, tokens):
+            return work[:, word0 : word0 + 2 * tokens].bitcast(BF16).rearrange("p (n t) -> p n t", t=PACK)
+
+        h0_q = hidden(0, h0[:], (0, 128))
+        w2_grouped = keep.tile([P, N, PACK], BF16, name="w2_grouped", align_bytes=64)
+        nc.scalar.copy(
+            w2_grouped[:].rearrange("p (c i) t -> p c t i", i=RUN),
+            w2_raw.rearrange("p t (c i) -> p c t i", i=RUN),
+        )
+        w2_q = quantize_h(w2_grouped[:], "w2")
+        h1_q = hidden(CHUNK, h_view(CHUNK // 2, CHUNK), (0, 128))
+        gate_then_scatter(h0_q, 0, 0, work[:, :CHUNK])
+        gate_then_scatter(h0_q, 0, 1, work[:, CHUNK : 2 * CHUNK])
+        gate_then_scatter(h1_q, CHUNK, 0, gated10[:])
+        h2_q = hidden(2 * CHUNK, h_view(2 * CHUNK, rest), (384, 0, 128, 256))
+        y11 = lin_sb[:, ON_GPSIMD * BANK_TOKENS * PACK - CHUNK :]
+        nc.scalar.copy(y11, second_product(h1_q, 1)[:])
+        nc.vector.tensor_tensor(windows[1][:].indirect(places(CHUNK, CHUNK)), y11, gate_sb[:, CHUNK : 2 * CHUNK], MULT)
         for b, window in enumerate(windows):
+            y = keep.tile([P, rest], F32, name=f"y{b}")
+            nc.scalar.copy(y[:], second_product(h2_q, b)[:])
+            nc.vector.tensor_tensor(window[:].indirect(places(2 * CHUNK, rest)), y[:], gate_sb[:, 2 * CHUNK :], MULT)
             nc.sync.dma_start(out[b * P : (b + 1) * P, :], window[:])

@@ -34,19 +34,18 @@ def tile_picked_route2_glusilu_p_kernel(
     nc = tc.nc
     with ExitStack() as ctx:
         keep = ctx.enter_context(tc.tile_pool(name="keep", bufs=1))
+        shared = ctx.enter_context(tc.tile_pool(name="shared", bufs=1))
         psum = ctx.enter_context(tc.psum_pool(name="psum", bufs=1))
 
         offs_sb = keep.tile([P, S // LIST], U16, name="offs_sb")
         dst_sb = keep.tile([P, S // LIST], U16, name="dst_sb")
-        planes = keep.tile([P, T], U8, name="planes", tag="planes", align_bytes=64)
+        planes = shared.tile([P, T], U8, name="planes", align_bytes=64, offset=7168)
         windows = [keep.tile([P, U], F32, name=f"window{b}") for b in range(N // P)]
         zeros_a = keep.tile([P, EDGE], F32, name="zeros_a", tag="words")
-        zeros_b = keep.tile([P, EDGE], F32, name="zeros_b", tag="held")
 
         nc.vector.memset(zeros_a[:], 0.0)
-        nc.vector.memset(zeros_b[:], 0.0)
         nc.vector.memset(planes[:].bitcast(I32), 0)
-        nc.vector.tensor_tensor(windows[0][:, :EDGE], zeros_a[:], zeros_b[:], MULT)
+        nc.vector.tensor_copy(windows[0][:, :EDGE], zeros_a[:])
         nc.scalar.activation(windows[1][:, :EDGE], windows[0][:, :EDGE], SILU)
         for window in windows:
             nc.vector.memset(window[:, EDGE:], 0.0)
@@ -57,17 +56,19 @@ def tile_picked_route2_glusilu_p_kernel(
         w3_rows = w3.rearrange("(p j) c -> p j c", j=PACK)
         w1_raw = keep.tile([P, PACK, H], F32, name="w1_raw", tag="w1_raw")
         nc.sync.dma_start(w1_raw[:], w1_rows)
-        for q in range(4):
-            nc.sync.dma_start(
-                planes[32 * q : 32 * q + 4, :].bitcast(I32), x_scales[0, 4 * q : 4 * q + 4, :].bitcast(I32)
-            )
+        nc.sync.dma_start(planes[0:P:8, :].bitcast(I32), x_scales[0].bitcast(I32))
         words = keep.tile([P, T], I32, name="words", tag="words")
         nc.sync.dma_start(words[:], x_words[0].rearrange("p c r -> p (c r)").bitcast(I32))
-        w3_raw = keep.tile([P, PACK, H], F32, name="w3_raw", tag="held")
-        nc.sync.dma_start(w3_raw[:], w3_rows)
 
+        picked_planes = keep.tile([P, S], U8, name="picked_planes")
+        nc.vector.tensor_copy(picked_planes[:], planes[:].indirect(offs_sb[:]))
         x_planes = keep.tile([P, S], U8, name="x_planes", align_bytes=64)
-        nc.vector.tensor_copy(x_planes[:], planes[:].indirect(offs_sb[:]))
+        for q in range(4):
+            nc.sync.dma_start(
+                x_planes[32 * q : 32 * q + 4, :].bitcast(I32), picked_planes[32 * q : 32 * q + 32 : 8, :].bitcast(I32)
+            )
+        w3_raw = shared.tile([P, PACK, H], F32, name="w3_raw", align_bytes=64, offset=10240)
+        nc.sync.dma_start(w3_raw[:], w3_rows)
         x_codes = []
         for g in range(S // GATHER):
             picked = keep.tile([P, GATHER], U32, name=f"x_codes{g}", align_bytes=64)
@@ -75,7 +76,7 @@ def tile_picked_route2_glusilu_p_kernel(
             nc.vector.tensor_copy(picked[:], words[:].bitcast(U32).indirect(offs_sb[:, cols]))
             x_codes.append(picked)
 
-        def quantize_first(pieces, calls, name, codes_tag):
+        def quantize_first(pieces, calls, name, codes):
             grouped = keep.tile([P, PACK, P, PACK], BF16, name=f"{name}_grouped", align_bytes=64)
             for raw, c0, slots, copy in pieces:
                 m = slice(c0 // PACK, (c0 + raw.shape[2]) // PACK)
@@ -83,7 +84,6 @@ def tile_picked_route2_glusilu_p_kernel(
                     grouped[:, slots, m, :].rearrange("p t m j -> p m j t"),
                     raw.rearrange("p j (m t) -> p m j t", t=PACK)[:, :, :, slots],
                 )
-            codes = keep.tile([P, H], U32, name=f"{name}_codes", tag=codes_tag, align_bytes=64)
             scales = keep.tile([P, H], U8, name=f"{name}_scales", align_bytes=64)
             step = PACK // calls
             for t in range(0, PACK, step):
@@ -95,9 +95,9 @@ def tile_picked_route2_glusilu_p_kernel(
                 )
             return codes, scales
 
-        w1_q = quantize_first([(w1_raw[:], 0, slice(0, 2), nc.scalar.copy), (w1_raw[:], 0, slice(2, PACK), nc.scalar.copy)], 1, "w1", "planes")
+        w1_q = quantize_first([(w1_raw[:], 0, slice(0, 2), nc.scalar.copy), (w1_raw[:], 0, slice(2, PACK), nc.scalar.copy)], 1, "w1", shared.tile([P, H], U32, name="w1_codes", align_bytes=64, offset=8192))
 
-        late = keep.tile([P, PACK * N + S], F32, name="late", tag="w1_raw")
+        late = shared.tile([P, PACK * N + S], F32, name="late", align_bytes=64, offset=0)
         w2_raw = late[:, : PACK * N].rearrange("p (t n) -> p t n", t=PACK)
         gate_sb = late[:, PACK * N :]
         nc.sync.dma_start(w2_raw, w2.rearrange("(p t) n -> p t n", t=PACK))
@@ -110,7 +110,7 @@ def tile_picked_route2_glusilu_p_kernel(
             ],
             2,
             "w3",
-            "w3_codes",
+            keep.tile([P, H], U32, name="w3_codes", align_bytes=64),
         )
 
         def first_product(w_q, j0, k, side):
@@ -140,7 +140,7 @@ def tile_picked_route2_glusilu_p_kernel(
             )
             return codes, scales
 
-        first_acts = keep.tile([P, AHEAD, BANK_TOKENS, PACK], F32, name="first_acts", tag="held")
+        first_acts = shared.tile([P, AHEAD, BANK_TOKENS, PACK], F32, name="first_acts", align_bytes=64, offset=11264)
         lin_sb = keep.tile([P, ON_GPSIMD * BANK_TOKENS * PACK], F32, name="lin_sb")
         banks = S // BANK_TOKENS
 

@@ -19,13 +19,12 @@ P = 128
 PACK = 4
 RUN = 4
 LIST = 16
-HALF = H // 2
+ROWS = K // 32
 GATHER = 512
 BANK_TOKENS = 128
-EDGE = 8
-CHUNK = 256
-AHEAD = 3
-ON_GPSIMD = 3
+HALF = S // 2
+RING = 3
+W3_EXTRA = 24
 
 
 def tile_picked_route2_glusilu_p_kernel(
@@ -39,36 +38,66 @@ def tile_picked_route2_glusilu_p_kernel(
 
         offs_sb = keep.tile([P, S // LIST], U16, name="offs_sb")
         dst_sb = keep.tile([P, S // LIST], U16, name="dst_sb")
-        planes = shared.tile([P, T], U8, name="planes", align_bytes=64, offset=7168)
+        planes = shared.tile([P, T], U8, name="planes", align_bytes=64, offset=6144)
         windows = [keep.tile([P, U], F32, name=f"window{b}") for b in range(N // P)]
-        zeros_a = keep.tile([P, EDGE], F32, name="zeros_a", tag="words")
+        zeros = keep.tile([P, 8], F32, name="zeros")
 
-        nc.vector.memset(zeros_a[:], 0.0)
-        nc.vector.memset(planes[:].bitcast(I32), 0)
-        nc.vector.tensor_copy(windows[0][:, :EDGE], zeros_a[:])
-        nc.scalar.activation(windows[1][:, :EDGE], windows[0][:, :EDGE], SILU)
-        for window in windows:
-            nc.vector.memset(window[:, EDGE:], 0.0)
-
+        nc.sync.dma_start(planes[P - ROWS :, :].bitcast(I32), x_scales[0].bitcast(I32))
         nc.sync.dma_start(offs_sb[:], offs)
-        nc.sync.dma_start(dst_sb[:], dst)
-        w1_rows = w1.rearrange("(p j) c -> p j c", j=PACK)
-        w3_rows = w3.rearrange("(p j) c -> p j c", j=PACK)
-        w1_raw = keep.tile([P, PACK, H], F32, name="w1_raw", tag="w1_raw")
-        nc.sync.dma_start(w1_raw[:], w1_rows)
-        nc.sync.dma_start(planes[0:P:8, :].bitcast(I32), x_scales[0].bitcast(I32))
-        words = keep.tile([P, T], I32, name="words", tag="words")
+        w1_raw = keep.tile([P, PACK, H], F32, name="w1_raw")
+        nc.sync.dma_start(w1_raw[:], w1.rearrange("(p j) c -> p j c", j=PACK))
+        words = keep.tile([P, T], I32, name="words")
         nc.sync.dma_start(words[:], x_words[0].rearrange("p c r -> p (c r)").bitcast(I32))
+        nc.sync.dma_start(dst_sb[:], dst)
+
+        nc.vector.memset(zeros[:], 0.0)
+        nc.vector.memset(planes[: P - ROWS, :].bitcast(I32), 0)
+        nc.scalar.activation(windows[1][:], zeros[:, 0:1].to_broadcast([P, U]), SILU)
+        nc.vector.memset(windows[0][:], 0.0)
 
         picked_planes = keep.tile([P, S], U8, name="picked_planes")
         nc.vector.tensor_copy(picked_planes[:], planes[:].indirect(offs_sb[:]))
         x_planes = keep.tile([P, S], U8, name="x_planes", align_bytes=64)
         for q in range(4):
-            nc.sync.dma_start(
-                x_planes[32 * q : 32 * q + 4, :].bitcast(I32), picked_planes[32 * q : 32 * q + 32 : 8, :].bitcast(I32)
-            )
-        w3_raw = shared.tile([P, PACK, H], F32, name="w3_raw", align_bytes=64, offset=10240)
-        nc.sync.dma_start(w3_raw[:], w3_rows)
+            r0 = P - ROWS + 4 * q
+            nc.sync.dma_start(x_planes[32 * q : 32 * q + 4, :].bitcast(I32), picked_planes[r0 : r0 + 4, :].bitcast(I32))
+        w3_raw = shared.tile([P, PACK, H], F32, name="w3_raw", align_bytes=64, offset=8192)
+        nc.sync.dma_start(w3_raw[:], w3.rearrange("(p j) c -> p j c", j=PACK))
+        late = shared.tile([P, PACK * N + S], F32, name="late", align_bytes=64, offset=0)
+        w2_raw = late[:, : PACK * N].rearrange("p (t n) -> p t n", t=PACK)
+        gate_sb = late[:, PACK * N :]
+        nc.sync.dma_start(w2_raw, w2.rearrange("(p t) n -> p t n", t=PACK))
+        nc.sync.dma_start(gate_sb, gate)
+
+        def quantize(values, name):
+            width = values.shape[1] // PACK
+            codes = keep.tile([P, width], U32, name=f"{name}_codes", align_bytes=64)
+            scales = keep.tile([P, width], U8, name=f"{name}_scales", align_bytes=64)
+            nc.vector.quantize_mx(out=codes[:].bitcast(FP8X4), scales=scales[:], in_=values)
+            return codes, scales
+
+        def round_first(raw, name, pieces):
+            grouped = keep.tile([P, PACK, P, PACK], BF16, name=f"{name}_grouped", align_bytes=64)
+            for slots, m, copy in pieces:
+                copy(
+                    grouped[:, slots, m, :].rearrange("p t m j -> p m j t"),
+                    raw[:].rearrange("p j (m t) -> p m j t", t=PACK)[:, m, :, slots],
+                )
+            return grouped
+
+        def quantize_first(grouped, name, calls):
+            stationary = []
+            for t0, t1 in calls:
+                codes, scales = quantize(grouped[:, t0:t1].rearrange("p t m j -> p (t m j)"), f"{name}_{t0}")
+                for t in range(t1 - t0):
+                    stationary.append((codes[:, t * P : (t + 1) * P], scales[:, t * P : (t + 1) * P]))
+            return stationary
+
+        w1_grouped = round_first(
+            w1_raw, "w1", [(slice(0, 2), slice(0, P), nc.vector.tensor_copy), (slice(2, 4), slice(0, P), nc.scalar.copy)]
+        )
+        w1_q = quantize_first(w1_grouped, "w1", [(0, 4)])
+
         x_codes = []
         for g in range(S // GATHER):
             picked = keep.tile([P, GATHER], U32, name=f"x_codes{g}", align_bytes=64)
@@ -76,54 +105,27 @@ def tile_picked_route2_glusilu_p_kernel(
             nc.vector.tensor_copy(picked[:], words[:].bitcast(U32).indirect(offs_sb[:, cols]))
             x_codes.append(picked)
 
-        def quantize_first(pieces, calls, name, codes):
-            grouped = keep.tile([P, PACK, P, PACK], BF16, name=f"{name}_grouped", align_bytes=64)
-            for raw, c0, slots, copy in pieces:
-                m = slice(c0 // PACK, (c0 + raw.shape[2]) // PACK)
-                copy(
-                    grouped[:, slots, m, :].rearrange("p t m j -> p m j t"),
-                    raw.rearrange("p j (m t) -> p m j t", t=PACK)[:, :, :, slots],
-                )
-            scales = keep.tile([P, H], U8, name=f"{name}_scales", align_bytes=64)
-            step = PACK // calls
-            for t in range(0, PACK, step):
-                cols = slice(t * P, (t + step) * P)
-                nc.vector.quantize_mx(
-                    out=codes[:, cols].bitcast(FP8X4),
-                    scales=scales[:, cols],
-                    in_=grouped[:, t : t + step].rearrange("p t m j -> p (t m j)"),
-                )
-            return codes, scales
-
-        w1_q = quantize_first([(w1_raw[:], 0, slice(0, 2), nc.scalar.copy), (w1_raw[:], 0, slice(2, PACK), nc.scalar.copy)], 1, "w1", shared.tile([P, H], U32, name="w1_codes", align_bytes=64, offset=8192))
-
-        late = shared.tile([P, PACK * N + S], F32, name="late", align_bytes=64, offset=0)
-        w2_raw = late[:, : PACK * N].rearrange("p (t n) -> p t n", t=PACK)
-        gate_sb = late[:, PACK * N :]
-        nc.sync.dma_start(w2_raw, w2.rearrange("(p t) n -> p t n", t=PACK))
-        nc.sync.dma_start(gate_sb, gate)
-
-        w3_q = quantize_first(
-            [
-                (w3_raw[:], 0, slice(0, 2), nc.vector.tensor_copy),
-                (w3_raw[:], 0, slice(2, PACK), nc.scalar.copy),
-            ],
-            2,
+        w3_grouped = round_first(
+            w3_raw,
             "w3",
-            keep.tile([P, H], U32, name="w3_codes", align_bytes=64),
+            [
+                (slice(2, 4), slice(W3_EXTRA, P), nc.scalar.copy),
+                (slice(0, 2), slice(0, P), nc.vector.tensor_copy),
+                (slice(2, 4), slice(0, W3_EXTRA), nc.vector.tensor_copy),
+            ],
         )
+        w3_q = quantize_first(w3_grouped, "w3", [(0, 2), (2, 3), (3, 4)])
 
-        def first_product(w_q, j0, k, side):
-            codes, scales = w_q
-            tag = f"up{k % AHEAD}_{(k // AHEAD + side) % 2}"
+        def first_product(w_q, k, tag):
             bank = psum.tile([P, PACK, BANK_TOKENS], F32, name="up", tag=tag)
+            j0 = k * BANK_TOKENS
             picked = x_codes[j0 // GATHER]
             c0 = j0 % GATHER
             for t in range(PACK):
                 nc.tensor.matmul_mx(
                     out=bank[:, t, :],
-                    lhsT=codes[:, t * P : (t + 1) * P].bitcast(FP8X4),
-                    lhsT_scale=scales[:, t * P : (t + 1) * P],
+                    lhsT=w_q[t][0].bitcast(FP8X4),
+                    lhsT_scale=w_q[t][1],
                     rhs=picked[:, c0 : c0 + BANK_TOKENS].bitcast(FP8X4),
                     rhs_scale=x_planes[:, j0 : j0 + BANK_TOKENS],
                     start=True,
@@ -131,39 +133,18 @@ def tile_picked_route2_glusilu_p_kernel(
                 )
             return bank[:].rearrange("p t n -> p n t")
 
-        def quantize_h(h, name):
-            width = h.shape[1]
-            codes = keep.tile([P, width], U32, name=f"{name}_codes", align_bytes=64)
-            scales = keep.tile([P, width], U8, name=f"{name}_scales", align_bytes=64)
-            nc.vector.quantize_mx(
-                out=codes[:].bitcast(FP8X4), scales=scales[:], in_=h.rearrange("p n t -> p (n t)")
-            )
-            return codes, scales
-
-        first_acts = shared.tile([P, AHEAD, BANK_TOKENS, PACK], F32, name="first_acts", align_bytes=64, offset=11264)
-        lin_sb = keep.tile([P, ON_GPSIMD * BANK_TOKENS * PACK], F32, name="lin_sb")
         banks = S // BANK_TOKENS
+        acts = shared.tile([P, banks, BANK_TOKENS, PACK], F32, name="acts", align_bytes=64, offset=12288)
+        h = [keep.tile([P, HALF, PACK], BF16, name=f"h{c}", align_bytes=64) for c in range(2)]
 
-        def hidden(j0, h, order):
-            for i, c0 in enumerate(order):
-                k = j0 // BANK_TOKENS + i
-                if k < AHEAD:
-                    act = first_acts[:, k]
-                else:
-                    act = keep.tile([P, BANK_TOKENS, PACK], F32, name=f"act{k}")[:]
-                nc.scalar.activation(act, first_product(w1_q, j0 + c0, k, 0), SILU)
-                lin = first_product(w3_q, j0 + c0, k, 1)
-                h_part = h[:, c0 : c0 + BANK_TOKENS, :]
-                if k >= banks - ON_GPSIMD:
-                    lin_part = lin_sb[:, c0 * PACK : (c0 + BANK_TOKENS) * PACK].rearrange("p (n t) -> p n t", t=PACK)
-                    nc.scalar.copy(lin_part, lin)
-                    nc.gpsimd.tensor_tensor(h_part, lin_part, act, MULT)
-                else:
-                    nc.vector.tensor_tensor(h_part, lin, act, MULT)
-            return quantize_h(h, f"h{j0}")
+        def hidden(k):
+            nc.scalar.activation(acts[:, k], first_product(w1_q, k, f"act{k % RING}"), SILU)
+            lin = first_product(w3_q, k, f"lin{k % RING}")
+            c0 = k * BANK_TOKENS % HALF
+            nc.vector.tensor_tensor(h[k * BANK_TOKENS // HALF][:, c0 : c0 + BANK_TOKENS, :], lin, acts[:, k], MULT)
 
-        def second_product(h_q, b):
-            bank = psum.tile([P, h_q[0].shape[1]], F32, name="down", tag=f"down{b}")
+        def second_product(h_q, b, tag, name):
+            bank = psum.tile([P, HALF], F32, name="down", tag=tag)
             nc.tensor.matmul_mx(
                 out=bank[:],
                 lhsT=w2_q[0][:, b * P : (b + 1) * P].bitcast(FP8X4),
@@ -173,40 +154,34 @@ def tile_picked_route2_glusilu_p_kernel(
                 start=True,
                 stop=True,
             )
-            return bank
+            y = keep.tile([P, HALF], F32, name=name)
+            nc.scalar.copy(y[:], bank[:])
+            return y
 
-        def places(j0, width):
-            return dst_sb[:, j0 // LIST : (j0 + width) // LIST]
+        def scatter(y, c, b):
+            places = dst_sb[:, c * HALF // LIST : (c + 1) * HALF // LIST]
+            nc.vector.tensor_tensor(windows[b][:].indirect(places), y[:], gate_sb[:, c * HALF : (c + 1) * HALF], MULT)
 
-        def gate_then_scatter(h_q, j0, b, gated):
-            nc.vector.tensor_tensor(gated, second_product(h_q, b)[:], gate_sb[:, j0 : j0 + CHUNK], MULT)
-            nc.vector.tensor_copy(windows[b][:].indirect(places(j0, CHUNK)), gated)
-
-        rest = S - 2 * CHUNK
-        work = keep.tile([P, 2 * CHUNK + 2 * rest], F32, name="work", align_bytes=64)
-        h0 = keep.tile([P, CHUNK, PACK], BF16, name="h0", align_bytes=64)
-        gated10 = keep.tile([P, CHUNK], F32, name="gated10")
-
-        def h_view(word0, tokens):
-            return work[:, word0 : word0 + 2 * tokens].bitcast(BF16).rearrange("p (n t) -> p n t", t=PACK)
-
-        h0_q = hidden(0, h0[:], (0, 128))
+        for k in range(banks // 2):
+            hidden(k)
+        h0_q = quantize(h[0][:].rearrange("p n t -> p (n t)"), "h0")
         w2_grouped = keep.tile([P, N, PACK], BF16, name="w2_grouped", align_bytes=64)
         nc.scalar.copy(
             w2_grouped[:].rearrange("p (c i) t -> p c t i", i=RUN),
             w2_raw.rearrange("p t (c i) -> p c t i", i=RUN),
         )
-        w2_q = quantize_h(w2_grouped[:], "w2")
-        h1_q = hidden(CHUNK, h_view(CHUNK // 2, CHUNK), (0, 128))
-        gate_then_scatter(h0_q, 0, 0, work[:, :CHUNK])
-        gate_then_scatter(h0_q, 0, 1, work[:, CHUNK : 2 * CHUNK])
-        gate_then_scatter(h1_q, CHUNK, 0, gated10[:])
-        h2_q = hidden(2 * CHUNK, h_view(2 * CHUNK, rest), (384, 0, 128, 256))
-        y11 = lin_sb[:, ON_GPSIMD * BANK_TOKENS * PACK - CHUNK :]
-        nc.scalar.copy(y11, second_product(h1_q, 1)[:])
-        nc.vector.tensor_tensor(windows[1][:].indirect(places(CHUNK, CHUNK)), y11, gate_sb[:, CHUNK : 2 * CHUNK], MULT)
-        for b, window in enumerate(windows):
-            y = keep.tile([P, rest], F32, name=f"y{b}")
-            nc.scalar.copy(y[:], second_product(h2_q, b)[:])
-            nc.vector.tensor_tensor(window[:].indirect(places(2 * CHUNK, rest)), y[:], gate_sb[:, 2 * CHUNK :], MULT)
-            nc.sync.dma_start(out[b * P : (b + 1) * P, :], window[:])
+        hidden(banks // 2)
+        w2_q = quantize(w2_grouped[:].rearrange("p n t -> p (n t)"), "w2")
+        for k in range(banks // 2 + 1, banks):
+            hidden(k)
+        h1_q = quantize(h[1][:].rearrange("p n t -> p (n t)"), "h1")
+        y00 = second_product(h0_q, 0, "down0", "y00")
+        y01 = second_product(h0_q, 1, f"lin{(banks - 2) % RING}", "y01")
+        y10 = second_product(h1_q, 0, "down1", "y10")
+        y11 = second_product(h1_q, 1, "down0", "y11")
+        scatter(y00, 0, 0)
+        scatter(y01, 0, 1)
+        scatter(y10, 1, 0)
+        nc.sync.dma_start(out[0:P, :], windows[0][:])
+        scatter(y11, 1, 1)
+        nc.sync.dma_start(out[P : 2 * P, :], windows[1][:])

@@ -17,14 +17,12 @@ MULT = mybir.AluOpType.mult
 
 P = 128
 PACK = 4
-RUN = 4
 LIST = 16
 ROWS = K // 32
 GATHER = 512
 BANK_TOKENS = 128
 HALF = S // 2
 RING = 3
-W3_EXTRA = 24
 
 
 def tile_picked_route2_glusilu_p_kernel(
@@ -38,13 +36,13 @@ def tile_picked_route2_glusilu_p_kernel(
 
         offs_sb = keep.tile([P, S // LIST], U16, name="offs_sb")
         dst_sb = keep.tile([P, S // LIST], U16, name="dst_sb")
-        planes = shared.tile([P, T], U8, name="planes", align_bytes=64, offset=6144)
+        planes = shared.tile([P, T], U8, name="planes", align_bytes=64, offset=20352)
         windows = [keep.tile([P, U], F32, name=f"window{b}") for b in range(N // P)]
         zeros = keep.tile([P, 8], F32, name="zeros")
 
         nc.sync.dma_start(planes[P - ROWS :, :].bitcast(I32), x_scales[0].bitcast(I32))
         nc.sync.dma_start(offs_sb[:], offs)
-        w1_raw = keep.tile([P, PACK, H], F32, name="w1_raw")
+        w1_raw = shared.tile([P, PACK, H], F32, name="w1_raw", align_bytes=64, offset=28480)
         nc.sync.dma_start(w1_raw[:], w1.rearrange("(p j) c -> p j c", j=PACK))
         words = keep.tile([P, T], I32, name="words")
         nc.sync.dma_start(words[:], x_words[0].rearrange("p c r -> p (c r)").bitcast(I32))
@@ -61,9 +59,13 @@ def tile_picked_route2_glusilu_p_kernel(
         for q in range(4):
             r0 = P - ROWS + 4 * q
             nc.sync.dma_start(x_planes[32 * q : 32 * q + 4, :].bitcast(I32), picked_planes[r0 : r0 + 4, :].bitcast(I32))
-        w3_raw = shared.tile([P, PACK, H], F32, name="w3_raw", align_bytes=64, offset=8192)
-        nc.sync.dma_start(w3_raw[:], w3.rearrange("(p j) c -> p j c", j=PACK))
-        late = shared.tile([P, PACK * N + S], F32, name="late", align_bytes=64, offset=0)
+        w3_rows = w3.rearrange("(p j) (u c) -> p u j c", j=PACK, u=2)
+        w3_raw = []
+        for u, offset in enumerate((16320, 24384)):
+            raw = shared.tile([P, PACK, H // 2], F32, name=f"w3_raw{u}", align_bytes=64, offset=offset)
+            nc.sync.dma_start(raw[:], w3_rows[:, u])
+            w3_raw.append(raw)
+        late = shared.tile([P, PACK * N + S], F32, name="late", align_bytes=64, offset=28480)
         w2_raw = late[:, : PACK * N].rearrange("p (t n) -> p t n", t=PACK)
         gate_sb = late[:, PACK * N :]
         nc.sync.dma_start(w2_raw, w2.rearrange("(p t) n -> p t n", t=PACK))
@@ -76,12 +78,13 @@ def tile_picked_route2_glusilu_p_kernel(
             nc.vector.quantize_mx(out=codes[:].bitcast(FP8X4), scales=scales[:], in_=values)
             return codes, scales
 
-        def round_first(raw, name, pieces):
+        def round_first(name, pieces):
             grouped = keep.tile([P, PACK, P, PACK], BF16, name=f"{name}_grouped", align_bytes=64)
-            for slots, m, copy in pieces:
+            for raw, m0, slots, copy in pieces:
+                m = slice(m0, m0 + raw.shape[2] // PACK)
                 copy(
                     grouped[:, slots, m, :].rearrange("p t m j -> p m j t"),
-                    raw[:].rearrange("p j (m t) -> p m j t", t=PACK)[:, m, :, slots],
+                    raw.rearrange("p j (m t) -> p m j t", t=PACK)[:, :, :, slots],
                 )
             return grouped
 
@@ -94,7 +97,7 @@ def tile_picked_route2_glusilu_p_kernel(
             return stationary
 
         w1_grouped = round_first(
-            w1_raw, "w1", [(slice(0, 2), slice(0, P), nc.vector.tensor_copy), (slice(2, 4), slice(0, P), nc.scalar.copy)]
+            "w1", [(w1_raw[:], 0, slice(0, 2), nc.vector.tensor_copy), (w1_raw[:], 0, slice(2, 4), nc.scalar.copy)]
         )
         w1_q = quantize_first(w1_grouped, "w1", [(0, 4)])
 
@@ -106,12 +109,10 @@ def tile_picked_route2_glusilu_p_kernel(
             x_codes.append(picked)
 
         w3_grouped = round_first(
-            w3_raw,
             "w3",
             [
-                (slice(2, 4), slice(W3_EXTRA, P), nc.scalar.copy),
-                (slice(0, 2), slice(0, P), nc.vector.tensor_copy),
-                (slice(2, 4), slice(0, W3_EXTRA), nc.vector.tensor_copy),
+                (w3_raw[0][:], 0, slice(0, 4), nc.scalar.copy),
+                (w3_raw[1][:], P // 2, slice(0, 4), nc.vector.tensor_copy),
             ],
         )
         w3_q = quantize_first(w3_grouped, "w3", [(0, 2), (2, 3), (3, 4)])
@@ -134,14 +135,22 @@ def tile_picked_route2_glusilu_p_kernel(
             return bank[:].rearrange("p t n -> p n t")
 
         banks = S // BANK_TOKENS
-        acts = shared.tile([P, banks, BANK_TOKENS, PACK], F32, name="acts", align_bytes=64, offset=12288)
-        h = [keep.tile([P, HALF, PACK], BF16, name=f"h{c}", align_bytes=64) for c in range(2)]
+        acts = shared.tile([P, banks, BANK_TOKENS, PACK], F32, name="acts", align_bytes=64, offset=0)
+        rounded = keep.tile([P, S, PACK], BF16, name="rounded", align_bytes=64)
+        w2_grouped = rounded[:, :N, :]
+        h = [rounded[:, BANK_TOKENS : BANK_TOKENS + HALF, :], rounded[:, HALF:, :]]
 
-        def hidden(k):
-            nc.scalar.activation(acts[:, k], first_product(w1_q, k, f"act{k % RING}"), SILU)
-            lin = first_product(w3_q, k, f"lin{k % RING}")
+        def hidden(k, turn, on_gpsimd):
+            nc.scalar.activation(acts[:, k], first_product(w1_q, k, f"act{turn % RING}"), SILU)
+            lin = first_product(w3_q, k, f"lin{turn % RING}")
             c0 = k * BANK_TOKENS % HALF
-            nc.vector.tensor_tensor(h[k * BANK_TOKENS // HALF][:, c0 : c0 + BANK_TOKENS, :], lin, acts[:, k], MULT)
+            h_part = h[k * BANK_TOKENS // HALF][:, c0 : c0 + BANK_TOKENS, :]
+            if on_gpsimd:
+                lin_sb = keep.tile([P, BANK_TOKENS, PACK], F32, name=f"lin_sb{k}")
+                nc.scalar.copy(lin_sb[:], lin)
+                nc.gpsimd.tensor_tensor(h_part, lin_sb[:], acts[:, k], MULT)
+            else:
+                nc.vector.tensor_tensor(h_part, lin, acts[:, k], MULT)
 
         def second_product(h_q, b, tag, name):
             bank = psum.tile([P, HALF], F32, name="down", tag=tag)
@@ -162,24 +171,22 @@ def tile_picked_route2_glusilu_p_kernel(
             places = dst_sb[:, c * HALF // LIST : (c + 1) * HALF // LIST]
             nc.vector.tensor_tensor(windows[b][:].indirect(places), y[:], gate_sb[:, c * HALF : (c + 1) * HALF], MULT)
 
-        for k in range(banks // 2):
-            hidden(k)
-        h0_q = quantize(h[0][:].rearrange("p n t -> p (n t)"), "h0")
-        w2_grouped = keep.tile([P, N, PACK], BF16, name="w2_grouped", align_bytes=64)
-        nc.scalar.copy(
-            w2_grouped[:].rearrange("p (c i) t -> p c t i", i=RUN),
-            w2_raw.rearrange("p t (c i) -> p c t i", i=RUN),
-        )
-        hidden(banks // 2)
-        w2_q = quantize(w2_grouped[:].rearrange("p n t -> p (n t)"), "w2")
-        for k in range(banks // 2 + 1, banks):
-            hidden(k)
-        h1_q = quantize(h[1][:].rearrange("p n t -> p (n t)"), "h1")
-        y00 = second_product(h0_q, 0, "down0", "y00")
+        nc.vector.tensor_copy(w2_grouped, w2_raw.rearrange("p t n -> p n t"))
+        hidden(1, 0, False)
+        w2_q = quantize(w2_grouped.rearrange("p n t -> p (n t)"), "w2")
+        hidden(0, 1, True)
+        hidden(2, 2, False)
+        hidden(3, 3, False)
+        hidden(5, 4, False)
+        h0_q = quantize(h[0].rearrange("p n t -> p (n t)"), "h0")
+        hidden(4, 5, True)
+        hidden(6, 6, False)
+        hidden(7, 7, False)
+        scatter(second_product(h0_q, 0, "down0", "y00"), 0, 0)
+        h1_q = quantize(h[1].rearrange("p n t -> p (n t)"), "h1")
         y01 = second_product(h0_q, 1, f"lin{(banks - 2) % RING}", "y01")
         y10 = second_product(h1_q, 0, "down1", "y10")
         y11 = second_product(h1_q, 1, "down0", "y11")
-        scatter(y00, 0, 0)
         scatter(y01, 0, 1)
         scatter(y10, 1, 0)
         nc.sync.dma_start(out[0:P, :], windows[0][:])

@@ -1,6 +1,7 @@
 from contextlib import ExitStack
 
 import concourse.mybir as mybir
+from concourse.masks import make_identity
 
 K, T, S, H, N, U = 512, 4096, 1024, 512, 256, 2048
 FLOPS = 2 * K * H * S * 2 + 2 * H * N * S
@@ -13,6 +14,7 @@ U16 = mybir.dt.uint16
 U8 = mybir.dt.uint8
 FP8X4 = mybir.dt.float8_e4m3fn_x4
 SILU = mybir.ActivationFunctionType.Silu
+COPY = mybir.ActivationFunctionType.Copy
 MULT = mybir.AluOpType.mult
 
 P = 128
@@ -22,7 +24,8 @@ ROWS = K // 32
 GATHER = 512
 BANK_TOKENS = 128
 HALF = S // 2
-RING = 3
+CHUNK = 256
+SHARE = 80
 
 
 def tile_picked_route2_glusilu_p_kernel(
@@ -65,11 +68,15 @@ def tile_picked_route2_glusilu_p_kernel(
             raw = shared.tile([P, PACK, H // 2], F32, name=f"w3_raw{u}", align_bytes=64, offset=offset)
             nc.sync.dma_start(raw[:], w3_rows[:, u])
             w3_raw.append(raw)
-        late = shared.tile([P, PACK * N + S], F32, name="late", align_bytes=64, offset=28480)
-        w2_raw = late[:, : PACK * N].rearrange("p (t n) -> p t n", t=PACK)
-        gate_sb = late[:, PACK * N :]
-        nc.sync.dma_start(w2_raw, w2.rearrange("(p t) n -> p t n", t=PACK))
-        nc.sync.dma_start(gate_sb, gate)
+        w2_raw = shared.tile([P, PACK, N], F32, name="w2_raw", align_bytes=64, offset=28480)
+        gate_sb = shared.tile([P, 3 * CHUNK], F32, name="gate_sb", align_bytes=64, offset=33664)
+        gate_col = shared.tile([P, PACK], F32, name="gate_col", align_bytes=64, offset=33600)
+        nc.sync.dma_start(w2_raw[:], w2.rearrange("(p t) n -> p t n", t=PACK))
+        nc.sync.dma_start(gate_sb[:], gate[:, : 3 * CHUNK])
+        with nc.allow_non_contiguous_dma(reason="one gate value a partition"):
+            nc.sync.dma_start(gate_col[:], gate[0, HALF:].rearrange("(c p) -> p c", p=P))
+        identity = keep.tile([P, P], F32, name="identity")
+        make_identity(nc, identity[:])
 
         def quantize(values, name):
             width = values.shape[1] // PACK
@@ -101,11 +108,18 @@ def tile_picked_route2_glusilu_p_kernel(
         )
         w1_q = quantize_first(w1_grouped, "w1", [(0, 4)])
 
+        def entries(j0, n):
+            e0 = (j0 + HALF) % S
+            return slice(e0, e0 + n)
+
+        def columns(j0, n):
+            e = entries(j0, n)
+            return slice(e.start // LIST, e.stop // LIST)
+
         x_codes = []
         for g in range(S // GATHER):
             picked = keep.tile([P, GATHER], U32, name=f"x_codes{g}", align_bytes=64)
-            cols = slice(g * GATHER // LIST, (g + 1) * GATHER // LIST)
-            nc.vector.tensor_copy(picked[:], words[:].bitcast(U32).indirect(offs_sb[:, cols]))
+            nc.vector.tensor_copy(picked[:], words[:].bitcast(U32).indirect(offs_sb[:, columns(g * GATHER, GATHER)]))
             x_codes.append(picked)
 
         w3_grouped = round_first(
@@ -117,78 +131,140 @@ def tile_picked_route2_glusilu_p_kernel(
         )
         w3_q = quantize_first(w3_grouped, "w3", [(0, 2), (2, 3), (3, 4)])
 
-        def first_product(w_q, k, tag):
-            bank = psum.tile([P, PACK, BANK_TOKENS], F32, name="up", tag=tag)
+        def bank(b, shape):
+            return psum.tile(shape, F32, name="bank", tag=f"bank{b}")
+
+        def first_product(w_q, k, b):
+            up = bank(b, [P, PACK, BANK_TOKENS])
             j0 = k * BANK_TOKENS
             picked = x_codes[j0 // GATHER]
             c0 = j0 % GATHER
             for t in range(PACK):
                 nc.tensor.matmul_mx(
-                    out=bank[:, t, :],
+                    out=up[:, t, :],
                     lhsT=w_q[t][0].bitcast(FP8X4),
                     lhsT_scale=w_q[t][1],
                     rhs=picked[:, c0 : c0 + BANK_TOKENS].bitcast(FP8X4),
-                    rhs_scale=x_planes[:, j0 : j0 + BANK_TOKENS],
+                    rhs_scale=x_planes[:, entries(j0, BANK_TOKENS)],
                     start=True,
                     stop=True,
                 )
-            return bank[:].rearrange("p t n -> p n t")
+            return up[:].rearrange("p t n -> p n t")
 
-        banks = S // BANK_TOKENS
-        acts = shared.tile([P, banks, BANK_TOKENS, PACK], F32, name="acts", align_bytes=64, offset=0)
-        rounded = keep.tile([P, S, PACK], BF16, name="rounded", align_bytes=64)
-        w2_grouped = rounded[:, :N, :]
-        h = [rounded[:, BANK_TOKENS : BANK_TOKENS + HALF, :], rounded[:, HALF:, :]]
+        acts = shared.tile([P, S, PACK], F32, name="acts", align_bytes=64, offset=0)
+        lins = keep.tile([P, 4, BANK_TOKENS * PACK], F32, name="lins")
+        lin_slot = {3: 0, 5: 1, 6: 2, 7: 3}
+        rounded = shared.tile([P, HALF + BANK_TOKENS, PACK], BF16, name="rounded", align_bytes=64, offset=28480)
+        w2_grouped = keep.tile([P, N, PACK], BF16, name="w2_grouped", align_bytes=64)
 
-        def hidden(k, turn, on_gpsimd):
-            nc.scalar.activation(acts[:, k], first_product(w1_q, k, f"act{turn % RING}"), SILU)
-            lin = first_product(w3_q, k, f"lin{turn % RING}")
-            c0 = k * BANK_TOKENS % HALF
-            h_part = h[k * BANK_TOKENS // HALF][:, c0 : c0 + BANK_TOKENS, :]
-            if on_gpsimd:
-                lin_sb = keep.tile([P, BANK_TOKENS, PACK], F32, name=f"lin_sb{k}")
-                nc.scalar.copy(lin_sb[:], lin)
-                nc.gpsimd.tensor_tensor(h_part, lin_sb[:], acts[:, k], MULT)
-            else:
-                nc.vector.tensor_tensor(h_part, lin, acts[:, k], MULT)
+        def h_part(j0, n):
+            c0 = j0 + BANK_TOKENS if j0 < HALF else j0 - HALF
+            return rounded[:, c0 : c0 + n, :]
 
-        def second_product(h_q, b, tag, name):
-            bank = psum.tile([P, HALF], F32, name="down", tag=tag)
+        def silu(k, b):
+            j0 = k * BANK_TOKENS
+            nc.scalar.activation(acts[:, j0 : j0 + BANK_TOKENS, :], first_product(w1_q, k, b), SILU)
+
+        def product_on_vector(lin, j0, n):
+            c0 = j0 % BANK_TOKENS
+            nc.vector.tensor_tensor(h_part(j0, n), lin[:, c0 : c0 + n, :], acts[:, j0 : j0 + n, :], MULT)
+
+        def lin_out(k, b):
+            nc.scalar.copy(lins[:, lin_slot[k], :].rearrange("p (n t) -> p n t", t=PACK), first_product(w3_q, k, b))
+
+        def product_on_gpsimd(k, n):
+            j0 = k * BANK_TOKENS
+            lin = lins[:, lin_slot[k], : n * PACK].rearrange("p (n t) -> p n t", t=PACK)
+            nc.gpsimd.tensor_tensor(h_part(j0, n), lin, acts[:, j0 : j0 + n, :], MULT)
+
+        def by_feature(h_q, c0, n, r, b):
+            down = bank(b, [P, n])
             nc.tensor.matmul_mx(
-                out=bank[:],
-                lhsT=w2_q[0][:, b * P : (b + 1) * P].bitcast(FP8X4),
-                lhsT_scale=w2_q[1][:, b * P : (b + 1) * P],
-                rhs=h_q[0][:].bitcast(FP8X4),
-                rhs_scale=h_q[1][:],
+                out=down[:],
+                lhsT=w2_q[0][:, r * P : (r + 1) * P].bitcast(FP8X4),
+                lhsT_scale=w2_q[1][:, r * P : (r + 1) * P],
+                rhs=h_q[0][:, c0 : c0 + n].bitcast(FP8X4),
+                rhs_scale=h_q[1][:, c0 : c0 + n],
                 start=True,
                 stop=True,
             )
-            y = keep.tile([P, HALF], F32, name=name)
-            nc.scalar.copy(y[:], bank[:])
-            return y
+            return down
 
-        def scatter(y, c, b):
-            places = dst_sb[:, c * HALF // LIST : (c + 1) * HALF // LIST]
-            nc.vector.tensor_tensor(windows[b][:].indirect(places), y[:], gate_sb[:, c * HALF : (c + 1) * HALF], MULT)
+        def by_token(h_q, c, m0, b):
+            width = N - m0
+            down = bank(b, [P, CHUNK // P, width])
+            gated = keep.tile([P, CHUNK // P, width], F32, name=f"gated{c}")
+            for i in range(CHUNK // P):
+                col = c * CHUNK // P + i
+                nc.tensor.matmul_mx(
+                    out=down[:, i, :],
+                    lhsT=h_q[0][:, col * P : (col + 1) * P].bitcast(FP8X4),
+                    lhsT_scale=h_q[1][:, col * P : (col + 1) * P],
+                    rhs=w2_q[0][:, m0:].bitcast(FP8X4),
+                    rhs_scale=w2_q[1][:, m0:],
+                    start=True,
+                    stop=True,
+                )
+            for i in range(CHUNK // P):
+                col = c * CHUNK // P + i
+                nc.scalar.activation(gated[:, i, :], down[:, i, :], COPY, scale=gate_col[:, col : col + 1])
+            return gated
 
-        nc.vector.tensor_copy(w2_grouped, w2_raw.rearrange("p t n -> p n t"))
-        hidden(1, 0, False)
-        w2_q = quantize(w2_grouped.rearrange("p n t -> p (n t)"), "w2")
-        hidden(0, 1, True)
-        hidden(2, 2, False)
-        hidden(3, 3, False)
-        hidden(5, 4, False)
-        h0_q = quantize(h[0].rearrange("p n t -> p (n t)"), "h0")
-        hidden(4, 5, True)
-        hidden(6, 6, False)
-        hidden(7, 7, False)
-        scatter(second_product(h0_q, 0, "down0", "y00"), 0, 0)
-        h1_q = quantize(h[1].rearrange("p n t -> p (n t)"), "h1")
-        y01 = second_product(h0_q, 1, f"lin{(banks - 2) % RING}", "y01")
-        y10 = second_product(h1_q, 0, "down1", "y10")
-        y11 = second_product(h1_q, 1, "down0", "y11")
-        scatter(y01, 0, 1)
-        scatter(y10, 1, 0)
+        def turn_back(gated, m0, b, y):
+            turned = bank(b, [P, CHUNK])
+            for i in range(CHUNK // P):
+                nc.tensor.transpose(turned[:, i * P : (i + 1) * P], gated[:, i, m0 : m0 + P], identity[:])
+            nc.scalar.copy(y, turned[:])
+
+        def scatter_plain(y, j0, r):
+            nc.vector.tensor_copy(windows[r][:].indirect(dst_sb[:, columns(j0, CHUNK)]), y)
+
+        def scatter_gated(y, r):
+            nc.vector.tensor_tensor(windows[r][:].indirect(dst_sb[:, columns(HALF, HALF)]), y, gate_sb[:, :HALF], MULT)
+
+        nc.vector.tensor_copy(w2_grouped[:], w2_raw[:].rearrange("p t n -> p n t"))
+        for b, k in enumerate((0, 1, 3, 2)):
+            silu(k, b)
+        for k in range(3):
+            product_on_vector(first_product(w3_q, k, 4 + k), k * BANK_TOKENS, BANK_TOKENS)
+        lin3 = first_product(w3_q, 3, 7)
+        nc.scalar.copy(lins[:, lin_slot[3], : SHARE * PACK].rearrange("p (n t) -> p n t", t=PACK), lin3[:, :SHARE, :])
+        product_on_gpsimd(3, SHARE)
+        product_on_vector(lin3, 3 * BANK_TOKENS + SHARE, BANK_TOKENS - SHARE)
+        silu(4, 4)
+        w2_q = quantize(w2_grouped[:].rearrange("p n t -> p (n t)"), "w2")
+        h0_q = quantize(h_part(0, HALF).rearrange("p n t -> p (n t)"), "h0")
+        product_on_vector(first_product(w3_q, 4, 7), HALF, BANK_TOKENS)
+        silu(5, 5)
+        lin_out(5, 6)
+        silu(6, 4)
+        ya0 = keep.tile([P, CHUNK], F32, name="ya0")
+        nc.vector.tensor_tensor(ya0[:], by_feature(h0_q, 0, CHUNK, 0, 0)[:], gate_sb[:, HALF:], MULT)
+        scatter_plain(ya0[:], 0, 0)
+        product_on_gpsimd(5, BANK_TOKENS)
+        gated_a = by_token(h0_q, 0, P, 1)
+        ya1 = keep.tile([P, CHUNK], F32, name="ya1")
+        turn_back(gated_a, 0, 3, ya1[:])
+        scatter_plain(ya1[:], 0, 1)
+        gated_b = by_token(h0_q, 1, 0, 2)
+        lin_out(6, 1)
+        product_on_gpsimd(6, BANK_TOKENS)
+        silu(7, 2)
+        yb0 = keep.tile([P, CHUNK], F32, name="yb0")
+        turn_back(gated_b, 0, 7, yb0[:])
+        scatter_plain(yb0[:], CHUNK, 0)
+        lin_out(7, 3)
+        product_on_gpsimd(7, BANK_TOKENS)
+        h1_q = quantize(h_part(HALF, HALF).rearrange("p n t -> p (n t)"), "h1")
+        yb1 = lins[:, lin_slot[7], :CHUNK]
+        turn_back(gated_b, P, 0, yb1)
+        scatter_plain(yb1, CHUNK, 1)
+        y10 = keep.tile([P, HALF], F32, name="y10")
+        for i in range(HALF // CHUNK):
+            nc.scalar.copy(y10[:, i * CHUNK : (i + 1) * CHUNK], by_feature(h1_q, i * CHUNK, CHUNK, 0, 5 + i)[:])
+        y11 = keep.tile([P, HALF], F32, name="y11")
+        nc.scalar.copy(y11[:], by_feature(h1_q, 0, HALF, 1, 4)[:])
+        scatter_gated(y10[:], 0)
         nc.sync.dma_start(out[0:P, :], windows[0][:])
-        scatter(y11, 1, 1)
+        scatter_gated(y11[:], 1)
         nc.sync.dma_start(out[P : 2 * P, :], windows[1][:])

@@ -16,6 +16,7 @@ FP8X4 = mybir.dt.float8_e4m3fn_x4
 SILU = mybir.ActivationFunctionType.Silu
 COPY = mybir.ActivationFunctionType.Copy
 MULT = mybir.AluOpType.mult
+ADD = mybir.AluOpType.add
 
 P = 128
 PACK = 4
@@ -25,7 +26,6 @@ GATHER = 512
 BANK_TOKENS = 128
 HALF = S // 2
 CHUNK = 256
-SHARE = 80
 
 
 def tile_picked_route2_glusilu_p_kernel(
@@ -45,7 +45,7 @@ def tile_picked_route2_glusilu_p_kernel(
 
         nc.sync.dma_start(planes[P - ROWS :, :].bitcast(I32), x_scales[0].bitcast(I32))
         nc.sync.dma_start(offs_sb[:], offs)
-        w1_raw = shared.tile([P, PACK, H], F32, name="w1_raw", align_bytes=64, offset=28480)
+        w1_raw = shared.tile([P, PACK, H], F32, name="w1_raw", align_bytes=64, offset=28672)
         nc.sync.dma_start(w1_raw[:], w1.rearrange("(p j) c -> p j c", j=PACK))
         words = keep.tile([P, T], I32, name="words")
         nc.sync.dma_start(words[:], x_words[0].rearrange("p c r -> p (c r)").bitcast(I32))
@@ -68,10 +68,12 @@ def tile_picked_route2_glusilu_p_kernel(
             raw = shared.tile([P, PACK, H // 2], F32, name=f"w3_raw{u}", align_bytes=64, offset=offset)
             nc.sync.dma_start(raw[:], w3_rows[:, u])
             w3_raw.append(raw)
-        w2_raw = shared.tile([P, PACK, N], F32, name="w2_raw", align_bytes=64, offset=28480)
-        gate_sb = shared.tile([P, 3 * CHUNK], F32, name="gate_sb", align_bytes=64, offset=33664)
-        gate_col = shared.tile([P, PACK], F32, name="gate_col", align_bytes=64, offset=33600)
-        nc.sync.dma_start(w2_raw[:], w2.rearrange("(p t) n -> p t n", t=PACK))
+        late = shared.tile([P, 2 * PACK * N], F32, name="late", align_bytes=64, offset=28480)
+        w2_raw = late[:, PACK * N :].rearrange("p (t n) -> p t n", t=PACK)
+        rounded = late[:].bitcast(BF16).rearrange("p (n t) -> p n t", t=PACK)
+        gate_sb = shared.tile([P, 3 * CHUNK], F32, name="gate_sb", align_bytes=64, offset=36736)
+        gate_col = shared.tile([P, PACK], F32, name="gate_col", align_bytes=64, offset=36672)
+        nc.sync.dma_start(w2_raw, w2.rearrange("(p t) n -> p t n", t=PACK))
         nc.sync.dma_start(gate_sb[:], gate[:, : 3 * CHUNK])
         with nc.allow_non_contiguous_dma(reason="one gate value a partition"):
             nc.sync.dma_start(gate_col[:], gate[0, HALF:].rearrange("(c p) -> p c", p=P))
@@ -152,10 +154,9 @@ def tile_picked_route2_glusilu_p_kernel(
             return up[:].rearrange("p t n -> p n t")
 
         acts = shared.tile([P, S, PACK], F32, name="acts", align_bytes=64, offset=0)
-        lins = keep.tile([P, 4, BANK_TOKENS * PACK], F32, name="lins")
-        lin_slot = {3: 0, 5: 1, 6: 2, 7: 3}
-        rounded = shared.tile([P, HALF + BANK_TOKENS, PACK], BF16, name="rounded", align_bytes=64, offset=28480)
-        w2_grouped = keep.tile([P, N, PACK], BF16, name="w2_grouped", align_bytes=64)
+        lins = keep.tile([P, 3, BANK_TOKENS * PACK], F32, name="lins")
+        lin_slot = {5: 0, 6: 1, 7: 2}
+        w2_grouped = w3_grouped[:, 2:].rearrange("p u m j -> p (u m) j")
 
         def h_part(j0, n):
             c0 = j0 + BANK_TOKENS if j0 < HALF else j0 - HALF
@@ -222,17 +223,13 @@ def tile_picked_route2_glusilu_p_kernel(
         def scatter_gated(y, r):
             nc.vector.tensor_tensor(windows[r][:].indirect(dst_sb[:, columns(HALF, HALF)]), y, gate_sb[:, :HALF], MULT)
 
-        nc.vector.tensor_copy(w2_grouped[:], w2_raw[:].rearrange("p t n -> p n t"))
-        for b, k in enumerate((0, 1, 3, 2)):
-            silu(k, b)
-        for k in range(3):
+        nc.gpsimd.tensor_scalar(w2_grouped, w2_raw.rearrange("p t n -> p n t"), 1.0, 0.0, MULT, ADD)
+        for k in range(4):
+            silu(k, k)
+        for k in range(4):
             product_on_vector(first_product(w3_q, k, 4 + k), k * BANK_TOKENS, BANK_TOKENS)
-        lin3 = first_product(w3_q, 3, 7)
-        nc.scalar.copy(lins[:, lin_slot[3], : SHARE * PACK].rearrange("p (n t) -> p n t", t=PACK), lin3[:, :SHARE, :])
-        product_on_gpsimd(3, SHARE)
-        product_on_vector(lin3, 3 * BANK_TOKENS + SHARE, BANK_TOKENS - SHARE)
         silu(4, 4)
-        w2_q = quantize(w2_grouped[:].rearrange("p n t -> p (n t)"), "w2")
+        w2_q = quantize(w2_grouped.rearrange("p n t -> p (n t)"), "w2")
         h0_q = quantize(h_part(0, HALF).rearrange("p n t -> p (n t)"), "h0")
         product_on_vector(first_product(w3_q, 4, 7), HALF, BANK_TOKENS)
         silu(5, 5)
@@ -250,10 +247,10 @@ def tile_picked_route2_glusilu_p_kernel(
         lin_out(6, 1)
         product_on_gpsimd(6, BANK_TOKENS)
         silu(7, 2)
+        lin_out(7, 3)
         yb0 = keep.tile([P, CHUNK], F32, name="yb0")
         turn_back(gated_b, 0, 7, yb0[:])
         scatter_plain(yb0[:], CHUNK, 0)
-        lin_out(7, 3)
         product_on_gpsimd(7, BANK_TOKENS)
         h1_q = quantize(h_part(HALF, HALF).rearrange("p n t -> p (n t)"), "h1")
         yb1 = lins[:, lin_slot[7], :CHUNK]

@@ -68,8 +68,8 @@ def tile_picked_route2_glusilu_p_kernel(
             raw = shared.tile([P, PACK, H // 2], F32, name=f"w3_raw{u}", align_bytes=64, offset=offset)
             nc.sync.dma_start(raw[:], w3_rows[:, u])
             w3_raw.append(raw)
-        late = shared.tile([P, 2 * PACK * N], F32, name="late", align_bytes=64, offset=28480)
-        w2_raw = late[:, PACK * N :].rearrange("p (t n) -> p t n", t=PACK)
+        late = shared.tile([P, 7 * CHUNK], F32, name="late", align_bytes=64, offset=28480)
+        w2_raw = late[:, : PACK * N].rearrange("p (t n) -> p t n", t=PACK)
         rounded = late[:].bitcast(BF16).rearrange("p (n t) -> p n t", t=PACK)
         gate_sb = shared.tile([P, 3 * CHUNK], F32, name="gate_sb", align_bytes=64, offset=36736)
         gate_col = shared.tile([P, PACK], F32, name="gate_col", align_bytes=64, offset=36672)
@@ -108,7 +108,8 @@ def tile_picked_route2_glusilu_p_kernel(
         w1_grouped = round_first(
             "w1", [(w1_raw[:], 0, slice(0, 2), nc.vector.tensor_copy), (w1_raw[:], 0, slice(2, 4), nc.scalar.copy)]
         )
-        w1_q = quantize_first(w1_grouped, "w1", [(0, 4)])
+        w1_codes, w1_scales = quantize(w1_grouped[:].rearrange("p t m j -> p (t m j)"), "w1")
+        w1_q = [(w1_codes[:, t * P : (t + 1) * P], w1_scales[:, t * P : (t + 1) * P]) for t in range(PACK)]
 
         def entries(j0, n):
             e0 = (j0 + HALF) % S
@@ -153,13 +154,25 @@ def tile_picked_route2_glusilu_p_kernel(
                 )
             return up[:].rearrange("p t n -> p n t")
 
+        unread = bank(4, [P, H])
+        for t in range(2):
+            nc.tensor.matmul_mx(
+                out=unread[:],
+                lhsT=w1_q[t][0].bitcast(FP8X4),
+                lhsT_scale=w1_q[t][1],
+                rhs=w1_codes[:].bitcast(FP8X4),
+                rhs_scale=x_planes[:, :H],
+                start=True,
+                stop=True,
+            )
+
         acts = shared.tile([P, S, PACK], F32, name="acts", align_bytes=64, offset=0)
         lins = keep.tile([P, 3, BANK_TOKENS * PACK], F32, name="lins")
         lin_slot = {5: 0, 6: 1, 7: 2}
         w2_grouped = w3_grouped[:, 2:].rearrange("p u m j -> p (u m) j")
 
         def h_part(j0, n):
-            c0 = j0 + BANK_TOKENS if j0 < HALF else j0 - HALF
+            c0 = j0 + (640 if j0 < CHUNK else 128 if j0 < HALF else -256)
             return rounded[:, c0 : c0 + n, :]
 
         def silu(k, b):
@@ -196,11 +209,10 @@ def tile_picked_route2_glusilu_p_kernel(
             down = bank(b, [P, CHUNK // P, width])
             gated = keep.tile([P, CHUNK // P, width], F32, name=f"gated{c}")
             for i in range(CHUNK // P):
-                col = c * CHUNK // P + i
                 nc.tensor.matmul_mx(
                     out=down[:, i, :],
-                    lhsT=h_q[0][:, col * P : (col + 1) * P].bitcast(FP8X4),
-                    lhsT_scale=h_q[1][:, col * P : (col + 1) * P],
+                    lhsT=h_q[0][:, i * P : (i + 1) * P].bitcast(FP8X4),
+                    lhsT_scale=h_q[1][:, i * P : (i + 1) * P],
                     rhs=w2_q[0][:, m0:].bitcast(FP8X4),
                     rhs_scale=w2_q[1][:, m0:],
                     start=True,
@@ -224,43 +236,45 @@ def tile_picked_route2_glusilu_p_kernel(
             nc.vector.tensor_tensor(windows[r][:].indirect(dst_sb[:, columns(HALF, HALF)]), y, gate_sb[:, :HALF], MULT)
 
         nc.gpsimd.tensor_scalar(w2_grouped, w2_raw.rearrange("p t n -> p n t"), 1.0, 0.0, MULT, ADD)
-        for k in range(4):
-            silu(k, k)
-        for k in range(4):
-            product_on_vector(first_product(w3_q, k, 4 + k), k * BANK_TOKENS, BANK_TOKENS)
-        silu(4, 4)
+        for b, k in enumerate((0, 1, 3, 2)):
+            silu(k, b)
+        for b, k in enumerate((0, 1, 3)):
+            product_on_vector(first_product(w3_q, k, 4 + b), k * BANK_TOKENS, BANK_TOKENS)
+        ha_q = quantize(h_part(0, CHUNK).rearrange("p n t -> p (n t)"), "ha")
         w2_q = quantize(w2_grouped.rearrange("p n t -> p (n t)"), "w2")
-        h0_q = quantize(h_part(0, HALF).rearrange("p n t -> p (n t)"), "h0")
-        product_on_vector(first_product(w3_q, 4, 7), HALF, BANK_TOKENS)
+        product_on_vector(first_product(w3_q, 2, 7), CHUNK, BANK_TOKENS)
+        lin_out(5, 3)
+        silu(4, 4)
         silu(5, 5)
-        lin_out(5, 6)
+        product_on_vector(first_product(w3_q, 4, 6), HALF, BANK_TOKENS)
         silu(6, 4)
         ya0 = keep.tile([P, CHUNK], F32, name="ya0")
-        nc.vector.tensor_tensor(ya0[:], by_feature(h0_q, 0, CHUNK, 0, 0)[:], gate_sb[:, HALF:], MULT)
+        nc.vector.tensor_tensor(ya0[:], by_feature(ha_q, 0, CHUNK, 0, 0)[:], gate_sb[:, HALF:], MULT)
+        hb_q = quantize(h_part(CHUNK, CHUNK).rearrange("p n t -> p (n t)"), "hb")
         scatter_plain(ya0[:], 0, 0)
+        gated_a = by_token(ha_q, 0, P, 1)
         product_on_gpsimd(5, BANK_TOKENS)
-        gated_a = by_token(h0_q, 0, P, 1)
-        ya1 = keep.tile([P, CHUNK], F32, name="ya1")
-        turn_back(gated_a, 0, 3, ya1[:])
-        scatter_plain(ya1[:], 0, 1)
-        gated_b = by_token(h0_q, 1, 0, 2)
-        lin_out(6, 1)
+        lin_out(6, 5)
         product_on_gpsimd(6, BANK_TOKENS)
-        silu(7, 2)
-        lin_out(7, 3)
+        ya1 = keep.tile([P, CHUNK], F32, name="ya1")
+        turn_back(gated_a, 0, 2, ya1[:])
+        scatter_plain(ya1[:], 0, 1)
+        silu(7, 7)
+        gated_b = by_token(hb_q, 1, 0, 3)
+        lin_out(7, 6)
         yb0 = keep.tile([P, CHUNK], F32, name="yb0")
-        turn_back(gated_b, 0, 7, yb0[:])
+        turn_back(gated_b, 0, 0, yb0[:])
         scatter_plain(yb0[:], CHUNK, 0)
         product_on_gpsimd(7, BANK_TOKENS)
         h1_q = quantize(h_part(HALF, HALF).rearrange("p n t -> p (n t)"), "h1")
         yb1 = lins[:, lin_slot[7], :CHUNK]
-        turn_back(gated_b, P, 0, yb1)
+        turn_back(gated_b, P, 1, yb1)
         scatter_plain(yb1, CHUNK, 1)
         y10 = keep.tile([P, HALF], F32, name="y10")
         for i in range(HALF // CHUNK):
-            nc.scalar.copy(y10[:, i * CHUNK : (i + 1) * CHUNK], by_feature(h1_q, i * CHUNK, CHUNK, 0, 5 + i)[:])
+            nc.scalar.copy(y10[:, i * CHUNK : (i + 1) * CHUNK], by_feature(h1_q, i * CHUNK, CHUNK, 0, 5 - i)[:])
         y11 = keep.tile([P, HALF], F32, name="y11")
-        nc.scalar.copy(y11[:], by_feature(h1_q, 0, HALF, 1, 4)[:])
+        nc.scalar.copy(y11[:], by_feature(h1_q, 0, HALF, 1, 7)[:])
         scatter_gated(y10[:], 0)
         nc.sync.dma_start(out[0:P, :], windows[0][:])
         scatter_gated(y11[:], 1)

@@ -16,7 +16,6 @@ FP8X4 = mybir.dt.float8_e4m3fn_x4
 SILU = mybir.ActivationFunctionType.Silu
 COPY = mybir.ActivationFunctionType.Copy
 MULT = mybir.AluOpType.mult
-ADD = mybir.AluOpType.add
 
 P = 128
 PACK = 4
@@ -26,6 +25,7 @@ GATHER = 512
 BANK_TOKENS = 128
 HALF = S // 2
 CHUNK = 256
+SHARE = 80
 
 
 def tile_picked_route2_glusilu_p_kernel(
@@ -68,12 +68,10 @@ def tile_picked_route2_glusilu_p_kernel(
             raw = shared.tile([P, PACK, H // 2], F32, name=f"w3_raw{u}", align_bytes=64, offset=offset)
             nc.sync.dma_start(raw[:], w3_rows[:, u])
             w3_raw.append(raw)
-        late = shared.tile([P, 7 * CHUNK], F32, name="late", align_bytes=64, offset=28480)
-        w2_raw = late[:, : PACK * N].rearrange("p (t n) -> p t n", t=PACK)
-        rounded = late[:].bitcast(BF16).rearrange("p (n t) -> p n t", t=PACK)
+        w2_raw = shared.tile([P, PACK, N], F32, name="w2_raw", align_bytes=64, offset=28480)
         gate_sb = shared.tile([P, 3 * CHUNK], F32, name="gate_sb", align_bytes=64, offset=36736)
         gate_col = shared.tile([P, PACK], F32, name="gate_col", align_bytes=64, offset=36672)
-        nc.sync.dma_start(w2_raw, w2.rearrange("(p t) n -> p t n", t=PACK))
+        nc.sync.dma_start(w2_raw[:], w2.rearrange("(p t) n -> p t n", t=PACK))
         nc.sync.dma_start(gate_sb[:], gate[:, : 3 * CHUNK])
         with nc.allow_non_contiguous_dma(reason="one gate value a partition"):
             nc.sync.dma_start(gate_col[:], gate[0, HALF:].rearrange("(c p) -> p c", p=P))
@@ -167,12 +165,13 @@ def tile_picked_route2_glusilu_p_kernel(
             )
 
         acts = shared.tile([P, S, PACK], F32, name="acts", align_bytes=64, offset=0)
-        lins = keep.tile([P, 3, BANK_TOKENS * PACK], F32, name="lins")
-        lin_slot = {5: 0, 6: 1, 7: 2}
-        w2_grouped = w3_grouped[:, 2:].rearrange("p u m j -> p (u m) j")
+        lins = keep.tile([P, 4, BANK_TOKENS * PACK], F32, name="lins")
+        lin_slot = {3: 0, 5: 1, 6: 2, 7: 3}
+        w2_grouped = keep.tile([P, N, PACK], BF16, name="w2_grouped", align_bytes=64)
+        rounded = shared.tile([P, 640, PACK], BF16, name="rounded", align_bytes=64, offset=28480)
 
         def h_part(j0, n):
-            c0 = j0 + (640 if j0 < CHUNK else 128 if j0 < HALF else -256)
+            c0 = j0 + (384 if j0 < CHUNK else -128 if j0 < HALF else -512)
             return rounded[:, c0 : c0 + n, :]
 
         def silu(k, b):
@@ -235,18 +234,21 @@ def tile_picked_route2_glusilu_p_kernel(
         def scatter_gated(y, r):
             nc.vector.tensor_tensor(windows[r][:].indirect(dst_sb[:, columns(HALF, HALF)]), y, gate_sb[:, :HALF], MULT)
 
-        nc.gpsimd.tensor_scalar(w2_grouped, w2_raw.rearrange("p t n -> p n t"), 1.0, 0.0, MULT, ADD)
+        nc.vector.tensor_copy(w2_grouped[:], w2_raw[:].rearrange("p t n -> p n t"))
         for b, k in enumerate((0, 1, 3, 2)):
             silu(k, b)
-        for b, k in enumerate((0, 1, 3)):
-            product_on_vector(first_product(w3_q, k, 4 + b), k * BANK_TOKENS, BANK_TOKENS)
+        lin3 = first_product(w3_q, 3, 7)
+        nc.scalar.copy(lins[:, lin_slot[3], : SHARE * PACK].rearrange("p (n t) -> p n t", t=PACK), lin3[:, :SHARE, :])
+        product_on_gpsimd(3, SHARE)
+        for k in range(3):
+            product_on_vector(first_product(w3_q, k, 4 + k), k * BANK_TOKENS, BANK_TOKENS)
+        w2_q = quantize(w2_grouped[:].rearrange("p n t -> p (n t)"), "w2")
         ha_q = quantize(h_part(0, CHUNK).rearrange("p n t -> p (n t)"), "ha")
-        w2_q = quantize(w2_grouped.rearrange("p n t -> p (n t)"), "w2")
-        product_on_vector(first_product(w3_q, 2, 7), CHUNK, BANK_TOKENS)
         lin_out(5, 3)
         silu(4, 4)
         silu(5, 5)
         product_on_vector(first_product(w3_q, 4, 6), HALF, BANK_TOKENS)
+        product_on_vector(lin3, 3 * BANK_TOKENS + SHARE, BANK_TOKENS - SHARE)
         silu(6, 4)
         ya0 = keep.tile([P, CHUNK], F32, name="ya0")
         nc.vector.tensor_tensor(ya0[:], by_feature(ha_q, 0, CHUNK, 0, 0)[:], gate_sb[:, HALF:], MULT)

@@ -21,11 +21,20 @@ P = 128
 PACK = 4
 LIST = 16
 ROWS = K // 32
-GATHER = 512
-BANK_TOKENS = 128
+GROUP = 128
 HALF = S // 2
-CHUNK = 256
+QUARTER = S // 4
 SHARE = 80
+
+OVERLAP = 64
+ACTS_AT = 0
+W3_FIRST_AT = ACTS_AT + S * PACK * 4 - OVERLAP
+PLANES_AT = W3_FIRST_AT + PACK * (H // 2) * 4 - OVERLAP
+W3_SECOND_AT = PLANES_AT + T - OVERLAP
+W2_AT = W3_SECOND_AT + PACK * (H // 2) * 4
+GATE_COLUMNS_AT = W2_AT + PACK * H * 4
+GATE_ROWS_AT = GATE_COLUMNS_AT + OVERLAP
+W1_AT = GATE_ROWS_AT + 2 * OVERLAP - PACK * H * 4
 
 
 def tile_picked_route2_glusilu_p_kernel(
@@ -39,44 +48,54 @@ def tile_picked_route2_glusilu_p_kernel(
 
         offs_sb = keep.tile([P, S // LIST], U16, name="offs_sb")
         dst_sb = keep.tile([P, S // LIST], U16, name="dst_sb")
-        planes = shared.tile([P, T], U8, name="planes", align_bytes=64, offset=20352)
-        windows = [keep.tile([P, U], F32, name=f"window{b}") for b in range(N // P)]
-        zeros = keep.tile([P, 8], F32, name="zeros")
+        planes = shared.tile([P, T], U8, name="planes", align_bytes=64, offset=PLANES_AT)
+        windows = [keep.tile([P, U], F32, name=f"window{r}") for r in range(N // P)]
+        zero = keep.tile([P, 1], F32, name="zero")
 
         nc.sync.dma_start(planes[P - ROWS :, :].bitcast(I32), x_scales[0].bitcast(I32))
         nc.sync.dma_start(offs_sb[:], offs)
-        w1_raw = shared.tile([P, PACK, H], F32, name="w1_raw", align_bytes=64, offset=28672)
+        w1_raw = shared.tile([P, PACK, H], F32, name="w1_raw", align_bytes=64, offset=W1_AT)
         nc.sync.dma_start(w1_raw[:], w1.rearrange("(p j) c -> p j c", j=PACK))
         words = keep.tile([P, T], I32, name="words")
         nc.sync.dma_start(words[:], x_words[0].rearrange("p c r -> p (c r)").bitcast(I32))
         nc.sync.dma_start(dst_sb[:], dst)
 
-        nc.vector.memset(zeros[:], 0.0)
+        nc.vector.memset(zero[:], 0.0)
         nc.vector.memset(planes[: P - ROWS, :].bitcast(I32), 0)
-        nc.scalar.activation(windows[1][:], zeros[:, 0:1].to_broadcast([P, U]), SILU)
+        nc.scalar.activation(windows[1][:], zero[:].to_broadcast([P, U]), SILU)
         nc.vector.memset(windows[0][:], 0.0)
 
         picked_planes = keep.tile([P, S], U8, name="picked_planes")
         nc.vector.tensor_copy(picked_planes[:], planes[:].indirect(offs_sb[:]))
         x_planes = keep.tile([P, S], U8, name="x_planes", align_bytes=64)
-        for q in range(4):
+        for q in range(ROWS // 4):
             r0 = P - ROWS + 4 * q
             nc.sync.dma_start(x_planes[32 * q : 32 * q + 4, :].bitcast(I32), picked_planes[r0 : r0 + 4, :].bitcast(I32))
+
         w3_rows = w3.rearrange("(p j) (u c) -> p u j c", j=PACK, u=2)
         w3_raw = []
-        for u, offset in enumerate((16320, 24384)):
+        for u, offset in enumerate((W3_FIRST_AT, W3_SECOND_AT)):
             raw = shared.tile([P, PACK, H // 2], F32, name=f"w3_raw{u}", align_bytes=64, offset=offset)
             nc.sync.dma_start(raw[:], w3_rows[:, u])
             w3_raw.append(raw)
-        w2_raw = shared.tile([P, PACK, N], F32, name="w2_raw", align_bytes=64, offset=28480)
-        gate_sb = shared.tile([P, 3 * CHUNK], F32, name="gate_sb", align_bytes=64, offset=36736)
-        gate_col = shared.tile([P, PACK], F32, name="gate_col", align_bytes=64, offset=36672)
+
+        w2_raw = shared.tile([P, PACK, N], F32, name="w2_raw", align_bytes=64, offset=W2_AT)
+        gate_rows = shared.tile([P, HALF + QUARTER], F32, name="gate_rows", align_bytes=64, offset=GATE_ROWS_AT)
+        gate_columns = shared.tile([P, HALF // P], F32, name="gate_columns", align_bytes=64, offset=GATE_COLUMNS_AT)
         nc.sync.dma_start(w2_raw[:], w2.rearrange("(p t) n -> p t n", t=PACK))
-        nc.sync.dma_start(gate_sb[:], gate[:, : 3 * CHUNK])
+        nc.sync.dma_start(gate_rows[:], gate[:, : HALF + QUARTER])
         with nc.allow_non_contiguous_dma(reason="one gate value a partition"):
-            nc.sync.dma_start(gate_col[:], gate[0, HALF:].rearrange("(c p) -> p c", p=P))
+            nc.sync.dma_start(gate_columns[:], gate[0, HALF:].rearrange("(c p) -> p c", p=P))
         identity = keep.tile([P, P], F32, name="identity")
         make_identity(nc, identity[:])
+
+        def entries(j0, n):
+            e0 = (j0 + HALF) % S
+            return slice(e0, e0 + n)
+
+        def list_columns(j0, n):
+            picked_entries = entries(j0, n)
+            return slice(picked_entries.start // LIST, picked_entries.stop // LIST)
 
         def quantize(values, name):
             width = values.shape[1] // PACK
@@ -95,189 +114,179 @@ def tile_picked_route2_glusilu_p_kernel(
                 )
             return grouped
 
-        def quantize_first(grouped, name, calls):
+        def quantize_first(grouped, name, slots_a_call):
             stationary = []
-            for t0, t1 in calls:
-                codes, scales = quantize(grouped[:, t0:t1].rearrange("p t m j -> p (t m j)"), f"{name}_{t0}")
-                for t in range(t1 - t0):
+            for t0 in range(0, PACK, slots_a_call):
+                values = grouped[:, t0 : t0 + slots_a_call].rearrange("p t m j -> p (t m j)")
+                codes, scales = quantize(values, f"{name}_{t0}")
+                for t in range(slots_a_call):
                     stationary.append((codes[:, t * P : (t + 1) * P], scales[:, t * P : (t + 1) * P]))
             return stationary
 
+        low, high, every = slice(0, 2), slice(2, 4), slice(0, 4)
         w1_grouped = round_first(
-            "w1", [(w1_raw[:], 0, slice(0, 2), nc.vector.tensor_copy), (w1_raw[:], 0, slice(2, 4), nc.scalar.copy)]
+            "w1", [(w1_raw[:], 0, low, nc.vector.tensor_copy), (w1_raw[:], 0, high, nc.scalar.copy)]
         )
-        w1_codes, w1_scales = quantize(w1_grouped[:].rearrange("p t m j -> p (t m j)"), "w1")
-        w1_q = [(w1_codes[:, t * P : (t + 1) * P], w1_scales[:, t * P : (t + 1) * P]) for t in range(PACK)]
-
-        def entries(j0, n):
-            e0 = (j0 + HALF) % S
-            return slice(e0, e0 + n)
-
-        def columns(j0, n):
-            e = entries(j0, n)
-            return slice(e.start // LIST, e.stop // LIST)
+        w1_q = quantize_first(w1_grouped, "w1", PACK)
 
         x_codes = []
-        for g in range(S // GATHER):
-            picked = keep.tile([P, GATHER], U32, name=f"x_codes{g}", align_bytes=64)
-            nc.vector.tensor_copy(picked[:], words[:].bitcast(U32).indirect(offs_sb[:, columns(g * GATHER, GATHER)]))
+        for g in range(S // HALF):
+            picked = keep.tile([P, HALF], U32, name=f"x_codes{g}", align_bytes=64)
+            nc.vector.tensor_copy(picked[:], words[:].bitcast(U32).indirect(offs_sb[:, list_columns(g * HALF, HALF)]))
             x_codes.append(picked)
 
         w3_grouped = round_first(
             "w3",
             [
-                (w3_raw[0][:], 0, slice(0, 4), nc.scalar.copy),
-                (w3_raw[1][:], P // 2, slice(0, 4), nc.vector.tensor_copy),
+                (w3_raw[0][:], 0, every, nc.scalar.copy),
+                (w3_raw[1][:], P // 2, low, nc.vector.tensor_copy),
+                (w3_raw[1][:], P // 2, high, nc.vector.tensor_copy),
             ],
         )
-        w3_q = quantize_first(w3_grouped, "w3", [(0, 2), (2, 3), (3, 4)])
+        w3_q = quantize_first(w3_grouped, "w3", 2)
 
         def bank(b, shape):
             return psum.tile(shape, F32, name="bank", tag=f"bank{b}")
 
         def first_product(w_q, k, b):
-            up = bank(b, [P, PACK, BANK_TOKENS])
-            j0 = k * BANK_TOKENS
-            picked = x_codes[j0 // GATHER]
-            c0 = j0 % GATHER
+            up = bank(b, [P, PACK, GROUP])
+            j0 = k * GROUP
+            picked = x_codes[j0 // HALF]
+            c0 = j0 % HALF
             for t in range(PACK):
                 nc.tensor.matmul_mx(
                     out=up[:, t, :],
                     lhsT=w_q[t][0].bitcast(FP8X4),
                     lhsT_scale=w_q[t][1],
-                    rhs=picked[:, c0 : c0 + BANK_TOKENS].bitcast(FP8X4),
-                    rhs_scale=x_planes[:, entries(j0, BANK_TOKENS)],
+                    rhs=picked[:, c0 : c0 + GROUP].bitcast(FP8X4),
+                    rhs_scale=x_planes[:, entries(j0, GROUP)],
                     start=True,
                     stop=True,
                 )
             return up[:].rearrange("p t n -> p n t")
 
-        unread = bank(4, [P, H])
-        for t in range(2):
-            nc.tensor.matmul_mx(
-                out=unread[:],
-                lhsT=w1_q[t][0].bitcast(FP8X4),
-                lhsT_scale=w1_q[t][1],
-                rhs=w1_codes[:].bitcast(FP8X4),
-                rhs_scale=x_planes[:, :H],
-                start=True,
-                stop=True,
-            )
-
-        acts = shared.tile([P, S, PACK], F32, name="acts", align_bytes=64, offset=0)
-        lins = keep.tile([P, 4, BANK_TOKENS * PACK], F32, name="lins")
-        lin_slot = {3: 0, 5: 1, 6: 2, 7: 3}
+        acts = shared.tile([P, S, PACK], F32, name="acts", align_bytes=64, offset=ACTS_AT)
+        on_gpsimd = (3, 5, 6, 7)
+        lins = keep.tile([P, len(on_gpsimd), GROUP * PACK], F32, name="lins")
         w2_grouped = keep.tile([P, N, PACK], BF16, name="w2_grouped", align_bytes=64)
-        rounded = shared.tile([P, 640, PACK], BF16, name="rounded", align_bytes=64, offset=28480)
+        rounded = shared.tile([P, GROUP + HALF, PACK], BF16, name="rounded", align_bytes=64, offset=W2_AT)
 
         def h_part(j0, n):
-            c0 = j0 + (384 if j0 < CHUNK else -128 if j0 < HALF else -512)
+            if j0 < QUARTER:
+                c0 = GROUP + QUARTER + j0
+            elif j0 < HALF:
+                c0 = GROUP + j0 - QUARTER
+            else:
+                c0 = j0 - HALF
             return rounded[:, c0 : c0 + n, :]
 
-        def silu(k, b):
-            j0 = k * BANK_TOKENS
-            nc.scalar.activation(acts[:, j0 : j0 + BANK_TOKENS, :], first_product(w1_q, k, b), SILU)
+        def lin_part(k, n):
+            return lins[:, on_gpsimd.index(k), : n * PACK].rearrange("p (n t) -> p n t", t=PACK)
 
-        def product_on_vector(lin, j0, n):
-            c0 = j0 % BANK_TOKENS
-            nc.vector.tensor_tensor(h_part(j0, n), lin[:, c0 : c0 + n, :], acts[:, j0 : j0 + n, :], MULT)
+        def silu(k, b):
+            j0 = k * GROUP
+            nc.scalar.activation(acts[:, j0 : j0 + GROUP, :], first_product(w1_q, k, b), SILU)
 
         def lin_out(k, b):
-            nc.scalar.copy(lins[:, lin_slot[k], :].rearrange("p (n t) -> p n t", t=PACK), first_product(w3_q, k, b))
+            nc.scalar.copy(lin_part(k, GROUP), first_product(w3_q, k, b))
+
+        def product_on_vector(lin, j0, n):
+            c0 = j0 % GROUP
+            nc.vector.tensor_tensor(h_part(j0, n), lin[:, c0 : c0 + n, :], acts[:, j0 : j0 + n, :], MULT)
 
         def product_on_gpsimd(k, n):
-            j0 = k * BANK_TOKENS
-            lin = lins[:, lin_slot[k], : n * PACK].rearrange("p (n t) -> p n t", t=PACK)
-            nc.gpsimd.tensor_tensor(h_part(j0, n), lin, acts[:, j0 : j0 + n, :], MULT)
+            j0 = k * GROUP
+            nc.gpsimd.tensor_tensor(h_part(j0, n), lin_part(k, n), acts[:, j0 : j0 + n, :], MULT)
 
-        def by_feature(h_q, c0, n, r, b):
-            down = bank(b, [P, n])
+        def quantize_h(j0, n):
+            return quantize(h_part(j0, n).rearrange("p n t -> p (n t)"), f"h{j0}")
+
+        def second_product(out_ap, stationary, s0, moving, m0, width):
             nc.tensor.matmul_mx(
-                out=down[:],
-                lhsT=w2_q[0][:, r * P : (r + 1) * P].bitcast(FP8X4),
-                lhsT_scale=w2_q[1][:, r * P : (r + 1) * P],
-                rhs=h_q[0][:, c0 : c0 + n].bitcast(FP8X4),
-                rhs_scale=h_q[1][:, c0 : c0 + n],
+                out=out_ap,
+                lhsT=stationary[0][:, s0 : s0 + P].bitcast(FP8X4),
+                lhsT_scale=stationary[1][:, s0 : s0 + P],
+                rhs=moving[0][:, m0 : m0 + width].bitcast(FP8X4),
+                rhs_scale=moving[1][:, m0 : m0 + width],
                 start=True,
                 stop=True,
             )
-            return down
 
-        def by_token(h_q, c, m0, b):
-            width = N - m0
-            down = bank(b, [P, CHUNK // P, width])
-            gated = keep.tile([P, CHUNK // P, width], F32, name=f"gated{c}")
-            for i in range(CHUNK // P):
-                nc.tensor.matmul_mx(
-                    out=down[:, i, :],
-                    lhsT=h_q[0][:, i * P : (i + 1) * P].bitcast(FP8X4),
-                    lhsT_scale=h_q[1][:, i * P : (i + 1) * P],
-                    rhs=w2_q[0][:, m0:].bitcast(FP8X4),
-                    rhs_scale=w2_q[1][:, m0:],
-                    start=True,
-                    stop=True,
-                )
-            for i in range(CHUNK // P):
-                col = c * CHUNK // P + i
-                nc.scalar.activation(gated[:, i, :], down[:, i, :], COPY, scale=gate_col[:, col : col + 1])
+        def rows_on_partitions(h_q, c0, n, r, b):
+            down = bank(b, [P, n])
+            second_product(down[:], w2_q, r * P, h_q, c0, n)
+            return down[:]
+
+        def gated_by_scalar(h_q, j0, r, b):
+            down = bank(b, [P, QUARTER // P, P])
+            gated = keep.tile([P, QUARTER // P, P], F32, name=f"gated{j0}_{r}")
+            for i in range(QUARTER // P):
+                second_product(down[:, i, :], h_q, i * P, w2_q, r * P, P)
+            for i in range(QUARTER // P):
+                c = j0 // P + i
+                nc.scalar.activation(gated[:, i, :], down[:, i, :], COPY, scale=gate_columns[:, c : c + 1])
             return gated
 
-        def turn_back(gated, m0, b, y):
-            turned = bank(b, [P, CHUNK])
-            for i in range(CHUNK // P):
-                nc.tensor.transpose(turned[:, i * P : (i + 1) * P], gated[:, i, m0 : m0 + P], identity[:])
+        def turn_back(gated, b, y):
+            turned = bank(b, [P, QUARTER])
+            for i in range(QUARTER // P):
+                nc.tensor.transpose(turned[:, i * P : (i + 1) * P], gated[:, i, :], identity[:])
             nc.scalar.copy(y, turned[:])
 
         def scatter_plain(y, j0, r):
-            nc.vector.tensor_copy(windows[r][:].indirect(dst_sb[:, columns(j0, CHUNK)]), y)
+            nc.vector.tensor_copy(windows[r][:].indirect(dst_sb[:, list_columns(j0, QUARTER)]), y)
 
         def scatter_gated(y, r):
-            nc.vector.tensor_tensor(windows[r][:].indirect(dst_sb[:, columns(HALF, HALF)]), y, gate_sb[:, :HALF], MULT)
+            places = dst_sb[:, list_columns(HALF, HALF)]
+            nc.vector.tensor_tensor(windows[r][:].indirect(places), y, gate_rows[:, :HALF], MULT)
 
         nc.vector.tensor_copy(w2_grouped[:], w2_raw[:].rearrange("p t n -> p n t"))
         for b, k in enumerate((0, 1, 3, 2)):
             silu(k, b)
         lin3 = first_product(w3_q, 3, 7)
-        nc.scalar.copy(lins[:, lin_slot[3], : SHARE * PACK].rearrange("p (n t) -> p n t", t=PACK), lin3[:, :SHARE, :])
+        nc.scalar.copy(lin_part(3, SHARE), lin3[:, :SHARE, :])
         product_on_gpsimd(3, SHARE)
         for k in range(3):
-            product_on_vector(first_product(w3_q, k, 4 + k), k * BANK_TOKENS, BANK_TOKENS)
+            product_on_vector(first_product(w3_q, k, 4 + k), k * GROUP, GROUP)
         w2_q = quantize(w2_grouped[:].rearrange("p n t -> p (n t)"), "w2")
-        ha_q = quantize(h_part(0, CHUNK).rearrange("p n t -> p (n t)"), "ha")
+        first_q = quantize_h(0, QUARTER)
         lin_out(5, 3)
         silu(4, 4)
         silu(5, 5)
-        product_on_vector(first_product(w3_q, 4, 6), HALF, BANK_TOKENS)
-        product_on_vector(lin3, 3 * BANK_TOKENS + SHARE, BANK_TOKENS - SHARE)
+        product_on_vector(first_product(w3_q, 4, 6), 4 * GROUP, GROUP)
+        product_on_vector(lin3, 3 * GROUP + SHARE, GROUP - SHARE)
         silu(6, 4)
-        ya0 = keep.tile([P, CHUNK], F32, name="ya0")
-        nc.vector.tensor_tensor(ya0[:], by_feature(ha_q, 0, CHUNK, 0, 0)[:], gate_sb[:, HALF:], MULT)
-        hb_q = quantize(h_part(CHUNK, CHUNK).rearrange("p n t -> p (n t)"), "hb")
-        scatter_plain(ya0[:], 0, 0)
-        gated_a = by_token(ha_q, 0, P, 1)
-        product_on_gpsimd(5, BANK_TOKENS)
+        y_first0 = keep.tile([P, QUARTER], F32, name="y_first0")
+        nc.vector.tensor_tensor(y_first0[:], rows_on_partitions(first_q, 0, QUARTER, 0, 0), gate_rows[:, HALF:], MULT)
+        second_q = quantize_h(QUARTER, QUARTER)
+
+        scatter_plain(y_first0[:], 0, 0)
+        gated_first1 = gated_by_scalar(first_q, 0, 1, 1)
+        product_on_gpsimd(5, GROUP)
         lin_out(6, 5)
-        product_on_gpsimd(6, BANK_TOKENS)
-        ya1 = keep.tile([P, CHUNK], F32, name="ya1")
-        turn_back(gated_a, 0, 2, ya1[:])
-        scatter_plain(ya1[:], 0, 1)
+        product_on_gpsimd(6, GROUP)
+        y_first1 = keep.tile([P, QUARTER], F32, name="y_first1")
+        turn_back(gated_first1, 2, y_first1[:])
+        scatter_plain(y_first1[:], 0, 1)
         silu(7, 7)
-        gated_b = by_token(hb_q, 1, 0, 3)
+        gated_second0 = gated_by_scalar(second_q, QUARTER, 0, 3)
         lin_out(7, 6)
-        yb0 = keep.tile([P, CHUNK], F32, name="yb0")
-        turn_back(gated_b, 0, 0, yb0[:])
-        scatter_plain(yb0[:], CHUNK, 0)
-        product_on_gpsimd(7, BANK_TOKENS)
-        h1_q = quantize(h_part(HALF, HALF).rearrange("p n t -> p (n t)"), "h1")
-        yb1 = lins[:, lin_slot[7], :CHUNK]
-        turn_back(gated_b, P, 1, yb1)
-        scatter_plain(yb1, CHUNK, 1)
-        y10 = keep.tile([P, HALF], F32, name="y10")
-        for i in range(HALF // CHUNK):
-            nc.scalar.copy(y10[:, i * CHUNK : (i + 1) * CHUNK], by_feature(h1_q, i * CHUNK, CHUNK, 0, 5 - i)[:])
-        y11 = keep.tile([P, HALF], F32, name="y11")
-        nc.scalar.copy(y11[:], by_feature(h1_q, 0, HALF, 1, 7)[:])
-        scatter_gated(y10[:], 0)
+        y_second0 = keep.tile([P, QUARTER], F32, name="y_second0")
+        turn_back(gated_second0, 0, y_second0[:])
+        scatter_plain(y_second0[:], QUARTER, 0)
+        gated_second1 = gated_by_scalar(second_q, QUARTER, 1, 0)
+        product_on_gpsimd(7, GROUP)
+
+        last_q = quantize_h(HALF, HALF)
+        y_second1 = lins[:, on_gpsimd.index(7), :QUARTER]
+        turn_back(gated_second1, 1, y_second1)
+        scatter_plain(y_second1, QUARTER, 1)
+        y_last0 = keep.tile([P, HALF], F32, name="y_last0")
+        for i, b in enumerate((5, 4)):
+            nc.scalar.copy(y_last0[:, i * QUARTER : (i + 1) * QUARTER], rows_on_partitions(last_q, i * QUARTER, QUARTER, 0, b))
+        y_last1 = keep.tile([P, HALF], F32, name="y_last1")
+        nc.scalar.copy(y_last1[:], rows_on_partitions(last_q, 0, HALF, 1, 7))
+        scatter_gated(y_last0[:], 0)
         nc.sync.dma_start(out[0:P, :], windows[0][:])
-        scatter_gated(y11[:], 1)
+        scatter_gated(y_last1[:], 1)
         nc.sync.dma_start(out[P : 2 * P, :], windows[1][:])

@@ -24,7 +24,7 @@ ROWS = K // 32
 GROUP = 128
 HALF = S // 2
 QUARTER = S // 4
-SHARE = 80
+SHARE = 64
 
 OVERLAP = 64
 ACTS_AT = 0
@@ -80,22 +80,17 @@ def tile_picked_route2_glusilu_p_kernel(
             w3_raw.append(raw)
 
         w2_raw = shared.tile([P, PACK, N], F32, name="w2_raw", align_bytes=64, offset=W2_AT)
-        gate_rows = shared.tile([P, HALF + QUARTER], F32, name="gate_rows", align_bytes=64, offset=GATE_ROWS_AT)
+        gate_rows = shared.tile([P, S], F32, name="gate_rows", align_bytes=64, offset=GATE_ROWS_AT)
         gate_columns = shared.tile([P, HALF // P], F32, name="gate_columns", align_bytes=64, offset=GATE_COLUMNS_AT)
         nc.sync.dma_start(w2_raw[:], w2.rearrange("(p t) n -> p t n", t=PACK))
-        nc.sync.dma_start(gate_rows[:], gate[:, : HALF + QUARTER])
+        nc.sync.dma_start(gate_rows[:], gate)
         with nc.allow_non_contiguous_dma(reason="one gate value a partition"):
-            nc.sync.dma_start(gate_columns[:], gate[0, HALF:].rearrange("(c p) -> p c", p=P))
+            nc.sync.dma_start(gate_columns[:], gate[0, :HALF].rearrange("(c p) -> p c", p=P))
         identity = keep.tile([P, P], F32, name="identity")
         make_identity(nc, identity[:])
 
-        def entries(j0, n):
-            e0 = (j0 + HALF) % S
-            return slice(e0, e0 + n)
-
         def list_columns(j0, n):
-            picked_entries = entries(j0, n)
-            return slice(picked_entries.start // LIST, picked_entries.stop // LIST)
+            return slice(j0 // LIST, (j0 + n) // LIST)
 
         def quantize(values, name):
             width = values.shape[1] // PACK
@@ -159,25 +154,21 @@ def tile_picked_route2_glusilu_p_kernel(
                     lhsT=w_q[t][0].bitcast(FP8X4),
                     lhsT_scale=w_q[t][1],
                     rhs=picked[:, c0 : c0 + GROUP].bitcast(FP8X4),
-                    rhs_scale=x_planes[:, entries(j0, GROUP)],
+                    rhs_scale=x_planes[:, j0 : j0 + GROUP],
                     start=True,
                     stop=True,
                 )
             return up[:].rearrange("p t n -> p n t")
 
         acts = shared.tile([P, S, PACK], F32, name="acts", align_bytes=64, offset=ACTS_AT)
-        on_gpsimd = (3, 5, 6, 7)
+        on_gpsimd = (4, 5, 6, 7)
         lins = keep.tile([P, len(on_gpsimd), GROUP * PACK], F32, name="lins")
         w2_grouped = keep.tile([P, N, PACK], BF16, name="w2_grouped", align_bytes=64)
-        rounded = shared.tile([P, GROUP + HALF, PACK], BF16, name="rounded", align_bytes=64, offset=W2_AT)
+        rounded_row = shared.tile([P, (GROUP + HALF) * PACK], BF16, name="rounded", align_bytes=64, offset=W2_AT)
+        rounded = rounded_row[:].rearrange("p (n t) -> p n t", t=PACK)
 
         def h_part(j0, n):
-            if j0 < QUARTER:
-                c0 = GROUP + QUARTER + j0
-            elif j0 < HALF:
-                c0 = GROUP + j0 - QUARTER
-            else:
-                c0 = j0 - HALF
+            c0 = j0 if j0 < HALF else j0 - HALF + GROUP
             return rounded[:, c0 : c0 + n, :]
 
         def lin_part(k, n):
@@ -217,15 +208,13 @@ def tile_picked_route2_glusilu_p_kernel(
             second_product(down[:], w2_q, r * P, h_q, c0, n)
             return down[:]
 
-        def gated_by_scalar(h_q, j0, r, b):
+        def gated_by_scalar(h_q, j0, r, b, gated):
             down = bank(b, [P, QUARTER // P, P])
-            gated = keep.tile([P, QUARTER // P, P], F32, name=f"gated{j0}_{r}")
             for i in range(QUARTER // P):
                 second_product(down[:, i, :], h_q, i * P, w2_q, r * P, P)
             for i in range(QUARTER // P):
                 c = j0 // P + i
                 nc.scalar.activation(gated[:, i, :], down[:, i, :], COPY, scale=gate_columns[:, c : c + 1])
-            return gated
 
         def turn_back(gated, b, y):
             turned = bank(b, [P, QUARTER])
@@ -236,57 +225,58 @@ def tile_picked_route2_glusilu_p_kernel(
         def scatter_plain(y, j0, r):
             nc.vector.tensor_copy(windows[r][:].indirect(dst_sb[:, list_columns(j0, QUARTER)]), y)
 
-        def scatter_gated(y, r):
-            places = dst_sb[:, list_columns(HALF, HALF)]
-            nc.vector.tensor_tensor(windows[r][:].indirect(places), y, gate_rows[:, :HALF], MULT)
+        def scatter_gated(y, j0, n, r):
+            places = dst_sb[:, list_columns(j0, n)]
+            nc.vector.tensor_tensor(windows[r][:].indirect(places), y, gate_rows[:, j0 : j0 + n], MULT)
 
         nc.vector.tensor_copy(w2_grouped[:], w2_raw[:].rearrange("p t n -> p n t"))
-        for b, k in enumerate((0, 1, 3, 2)):
+        for k, b in enumerate((0, 1, 2, 3, 7)):
             silu(k, b)
-        lin3 = first_product(w3_q, 3, 7)
-        nc.scalar.copy(lin_part(3, SHARE), lin3[:, :SHARE, :])
-        product_on_gpsimd(3, SHARE)
         for k in range(3):
             product_on_vector(first_product(w3_q, k, 4 + k), k * GROUP, GROUP)
         w2_q = quantize(w2_grouped[:].rearrange("p n t -> p (n t)"), "w2")
         first_q = quantize_h(0, QUARTER)
-        lin_out(5, 3)
-        silu(4, 4)
-        silu(5, 5)
-        product_on_vector(first_product(w3_q, 4, 6), 4 * GROUP, GROUP)
-        product_on_vector(lin3, 3 * GROUP + SHARE, GROUP - SHARE)
-        silu(6, 4)
+        product_on_vector(first_product(w3_q, 3, 0), 3 * GROUP, GROUP)
+        lin4 = first_product(w3_q, 4, 1)
+        nc.scalar.copy(lin_part(4, SHARE), lin4[:, :SHARE, :])
+        product_on_gpsimd(4, SHARE)
+        product_on_vector(lin4, 4 * GROUP + SHARE, GROUP - SHARE)
+        lin_out(5, 2)
+        silu(5, 4)
+        silu(6, 5)
+        lin_out(6, 6)
         y_first0 = keep.tile([P, QUARTER], F32, name="y_first0")
-        nc.vector.tensor_tensor(y_first0[:], rows_on_partitions(first_q, 0, QUARTER, 0, 0), gate_rows[:, HALF:], MULT)
+        nc.vector.tensor_tensor(y_first0[:], rows_on_partitions(first_q, 0, QUARTER, 0, 3), gate_rows[:, :QUARTER], MULT)
         second_q = quantize_h(QUARTER, QUARTER)
 
         scatter_plain(y_first0[:], 0, 0)
-        gated_first1 = gated_by_scalar(first_q, 0, 1, 1)
+        gated_first1 = keep.tile([P, QUARTER // P, P], F32, name="gated_first1")
+        gated_by_scalar(first_q, 0, 1, 7, gated_first1)
         product_on_gpsimd(5, GROUP)
-        lin_out(6, 5)
         product_on_gpsimd(6, GROUP)
         y_first1 = keep.tile([P, QUARTER], F32, name="y_first1")
         turn_back(gated_first1, 2, y_first1[:])
         scatter_plain(y_first1[:], 0, 1)
+        lin_out(7, 0)
+        gated_second0 = rounded_row[:, HALF * PACK :].bitcast(F32).rearrange("p (i m) -> p i m", m=P)
+        gated_by_scalar(second_q, QUARTER, 0, 4, gated_second0)
         silu(7, 7)
-        gated_second0 = gated_by_scalar(second_q, QUARTER, 0, 3)
-        lin_out(7, 6)
         y_second0 = keep.tile([P, QUARTER], F32, name="y_second0")
-        turn_back(gated_second0, 0, y_second0[:])
+        turn_back(gated_second0, 3, y_second0[:])
         scatter_plain(y_second0[:], QUARTER, 0)
-        gated_second1 = gated_by_scalar(second_q, QUARTER, 1, 0)
         product_on_gpsimd(7, GROUP)
 
         last_q = quantize_h(HALF, HALF)
         y_second1 = lins[:, on_gpsimd.index(7), :QUARTER]
-        turn_back(gated_second1, 1, y_second1)
-        scatter_plain(y_second1, QUARTER, 1)
+        nc.scalar.copy(y_second1, rows_on_partitions(second_q, 0, QUARTER, 1, 5))
+        scatter_gated(y_second1, QUARTER, QUARTER, 1)
         y_last0 = keep.tile([P, HALF], F32, name="y_last0")
-        for i, b in enumerate((5, 4)):
-            nc.scalar.copy(y_last0[:, i * QUARTER : (i + 1) * QUARTER], rows_on_partitions(last_q, i * QUARTER, QUARTER, 0, b))
+        for i, b in enumerate((1, 6)):
+            c0 = i * QUARTER
+            nc.scalar.copy(y_last0[:, c0 : c0 + QUARTER], rows_on_partitions(last_q, c0, QUARTER, 0, b))
         y_last1 = keep.tile([P, HALF], F32, name="y_last1")
-        nc.scalar.copy(y_last1[:], rows_on_partitions(last_q, 0, HALF, 1, 7))
-        scatter_gated(y_last0[:], 0)
+        nc.scalar.copy(y_last1[:], rows_on_partitions(last_q, 0, HALF, 1, 4))
+        scatter_gated(y_last0[:], HALF, HALF, 0)
         nc.sync.dma_start(out[0:P, :], windows[0][:])
-        scatter_gated(y_last1[:], 1)
+        scatter_gated(y_last1[:], HALF, HALF, 1)
         nc.sync.dma_start(out[P : 2 * P, :], windows[1][:])

@@ -24,17 +24,18 @@ ROWS = K // 32
 GROUP = 128
 HALF = S // 2
 QUARTER = S // 4
-SHARE = 64
+SHARE = 96
+SECOND_AT = QUARTER - SHARE
 
 OVERLAP = 64
-ACTS_AT = 0
-W3_FIRST_AT = ACTS_AT + S * PACK * 4 - OVERLAP
+W3_FIRST_AT = 0
 PLANES_AT = W3_FIRST_AT + PACK * (H // 2) * 4 - OVERLAP
 W3_SECOND_AT = PLANES_AT + T - OVERLAP
-W2_AT = W3_SECOND_AT + PACK * (H // 2) * 4
-GATE_COLUMNS_AT = W2_AT + PACK * H * 4
-GATE_ROWS_AT = GATE_COLUMNS_AT + OVERLAP
-W1_AT = GATE_ROWS_AT + 2 * OVERLAP - PACK * H * 4
+GATE_ROWS_AT = W3_SECOND_AT + PACK * (H // 2) * 4
+ZEROS = 64
+ZERO_AT = GATE_ROWS_AT + S * 4 - OVERLAP
+GATE_COLUMNS_AT = ZERO_AT + OVERLAP
+W2_AT = GATE_COLUMNS_AT + OVERLAP
 
 
 def tile_picked_route2_glusilu_p_kernel(
@@ -50,19 +51,27 @@ def tile_picked_route2_glusilu_p_kernel(
         dst_sb = keep.tile([P, S // LIST], U16, name="dst_sb")
         planes = shared.tile([P, T], U8, name="planes", align_bytes=64, offset=PLANES_AT)
         windows = [keep.tile([P, U], F32, name=f"window{r}") for r in range(N // P)]
-        zero = keep.tile([P, 1], F32, name="zero")
+        zero = shared.tile([P, ZEROS], F32, name="zero", align_bytes=64, offset=ZERO_AT)
 
         nc.sync.dma_start(planes[P - ROWS :, :].bitcast(I32), x_scales[0].bitcast(I32))
         nc.sync.dma_start(offs_sb[:], offs)
-        w1_raw = shared.tile([P, PACK, H], F32, name="w1_raw", align_bytes=64, offset=W1_AT)
-        nc.sync.dma_start(w1_raw[:], w1.rearrange("(p j) c -> p j c", j=PACK))
+        nc.sync.dma_start(dst_sb[:], dst)
         words = keep.tile([P, T], I32, name="words")
         nc.sync.dma_start(words[:], x_words[0].rearrange("p c r -> p (c r)").bitcast(I32))
-        nc.sync.dma_start(dst_sb[:], dst)
+        w1_rows = w1.rearrange("(p j) (u c) -> p u j c", j=PACK, u=2)
+        w1_raw = []
+        for u in range(2):
+            raw = keep.tile([P, PACK, H // 2], F32, name=f"w1_raw{u}", align_bytes=64)
+            nc.sync.dma_start(raw[:], w1_rows[:, u])
+            w1_raw.append(raw)
 
         nc.vector.memset(zero[:], 0.0)
         nc.vector.memset(planes[: P - ROWS, :].bitcast(I32), 0)
-        nc.scalar.activation(windows[1][:], zero[:].to_broadcast([P, U]), SILU)
+        nc.scalar.activation(
+            windows[1][:].rearrange("p (a b) -> p a b", b=ZEROS),
+            zero[:].unsqueeze(1).to_broadcast([P, U // ZEROS, ZEROS]),
+            SILU,
+        )
         nc.vector.memset(windows[0][:], 0.0)
 
         picked_planes = keep.tile([P, S], U8, name="picked_planes")
@@ -119,21 +128,26 @@ def tile_picked_route2_glusilu_p_kernel(
             return stationary
 
         low, high, every = slice(0, 2), slice(2, 4), slice(0, 4)
-        w1_grouped = round_first(
-            "w1", [(w1_raw[:], 0, low, nc.vector.tensor_copy), (w1_raw[:], 0, high, nc.scalar.copy)]
-        )
-        w1_q = quantize_first(w1_grouped, "w1", PACK)
-
         x_codes = []
         for g in range(S // HALF):
             picked = keep.tile([P, HALF], U32, name=f"x_codes{g}", align_bytes=64)
             nc.vector.tensor_copy(picked[:], words[:].bitcast(U32).indirect(offs_sb[:, list_columns(g * HALF, HALF)]))
             x_codes.append(picked)
 
+        w1_grouped = round_first(
+            "w1",
+            [
+                (w1_raw[0][:], 0, every, nc.scalar.copy),
+                (w1_raw[1][:], P // 2, low, nc.vector.tensor_copy),
+                (w1_raw[1][:], P // 2, high, nc.scalar.copy),
+            ],
+        )
+        w1_q = quantize_first(w1_grouped, "w1", 2)
+
         w3_grouped = round_first(
             "w3",
             [
-                (w3_raw[0][:], 0, every, nc.scalar.copy),
+                (w3_raw[0][:], 0, every, nc.vector.tensor_copy),
                 (w3_raw[1][:], P // 2, low, nc.vector.tensor_copy),
                 (w3_raw[1][:], P // 2, high, nc.vector.tensor_copy),
             ],
@@ -160,19 +174,19 @@ def tile_picked_route2_glusilu_p_kernel(
                 )
             return up[:].rearrange("p t n -> p n t")
 
-        acts = shared.tile([P, S, PACK], F32, name="acts", align_bytes=64, offset=ACTS_AT)
+        acts = keep.tile([P, S, PACK], F32, name="acts", align_bytes=64)
         on_gpsimd = (4, 5, 6, 7)
         lins = keep.tile([P, len(on_gpsimd), GROUP * PACK], F32, name="lins")
         w2_grouped = keep.tile([P, N, PACK], BF16, name="w2_grouped", align_bytes=64)
-        rounded_row = shared.tile([P, (GROUP + HALF) * PACK], BF16, name="rounded", align_bytes=64, offset=W2_AT)
+        rounded_row = shared.tile([P, (SECOND_AT + HALF) * PACK], BF16, name="rounded", align_bytes=64, offset=W2_AT)
         rounded = rounded_row[:].rearrange("p (n t) -> p n t", t=PACK)
 
         def h_part(j0, n):
-            c0 = j0 if j0 < HALF else j0 - HALF + GROUP
+            c0 = j0 if j0 < HALF else j0 - HALF + SECOND_AT
             return rounded[:, c0 : c0 + n, :]
 
-        def lin_part(k, n):
-            return lins[:, on_gpsimd.index(k), : n * PACK].rearrange("p (n t) -> p n t", t=PACK)
+        def lin_part(k, n, c0=0):
+            return lins[:, on_gpsimd.index(k), c0 * PACK : (c0 + n) * PACK].rearrange("p (n t) -> p n t", t=PACK)
 
         def silu(k, b):
             j0 = k * GROUP
@@ -185,9 +199,9 @@ def tile_picked_route2_glusilu_p_kernel(
             c0 = j0 % GROUP
             nc.vector.tensor_tensor(h_part(j0, n), lin[:, c0 : c0 + n, :], acts[:, j0 : j0 + n, :], MULT)
 
-        def product_on_gpsimd(k, n):
-            j0 = k * GROUP
-            nc.gpsimd.tensor_tensor(h_part(j0, n), lin_part(k, n), acts[:, j0 : j0 + n, :], MULT)
+        def product_on_gpsimd(k, n, c0=0):
+            j0 = k * GROUP + c0
+            nc.gpsimd.tensor_tensor(h_part(j0, n), lin_part(k, n, c0), acts[:, j0 : j0 + n, :], MULT)
 
         def quantize_h(j0, n):
             return quantize(h_part(j0, n).rearrange("p n t -> p (n t)"), f"h{j0}")
@@ -230,53 +244,57 @@ def tile_picked_route2_glusilu_p_kernel(
             nc.vector.tensor_tensor(windows[r][:].indirect(places), y, gate_rows[:, j0 : j0 + n], MULT)
 
         nc.vector.tensor_copy(w2_grouped[:], w2_raw[:].rearrange("p t n -> p n t"))
-        for k, b in enumerate((0, 1, 2, 3, 7)):
-            silu(k, b)
-        for k in range(3):
+        for k in range(4):
+            silu(k, k)
+        silu(4, 7)
+        for k in range(2):
             product_on_vector(first_product(w3_q, k, 4 + k), k * GROUP, GROUP)
+        lin_out(4, 1)
+        lin_out(5, 3)
+        silu(5, 4)
         w2_q = quantize(w2_grouped[:].rearrange("p n t -> p (n t)"), "w2")
         first_q = quantize_h(0, QUARTER)
+        product_on_vector(first_product(w3_q, 2, 6), 2 * GROUP, GROUP)
         product_on_vector(first_product(w3_q, 3, 0), 3 * GROUP, GROUP)
-        lin4 = first_product(w3_q, 4, 1)
-        nc.scalar.copy(lin_part(4, SHARE), lin4[:, :SHARE, :])
         product_on_gpsimd(4, SHARE)
-        product_on_vector(lin4, 4 * GROUP + SHARE, GROUP - SHARE)
-        lin_out(5, 2)
-        silu(5, 4)
-        silu(6, 5)
-        lin_out(6, 6)
         y_first0 = keep.tile([P, QUARTER], F32, name="y_first0")
-        nc.vector.tensor_tensor(y_first0[:], rows_on_partitions(first_q, 0, QUARTER, 0, 3), gate_rows[:, :QUARTER], MULT)
+        nc.vector.tensor_tensor(y_first0[:], rows_on_partitions(first_q, 0, QUARTER, 0, 7), gate_rows[:, :QUARTER], MULT)
         second_q = quantize_h(QUARTER, QUARTER)
 
         scatter_plain(y_first0[:], 0, 0)
-        gated_first1 = keep.tile([P, QUARTER // P, P], F32, name="gated_first1")
-        gated_by_scalar(first_q, 0, 1, 7, gated_first1)
+        product_on_gpsimd(4, GROUP - SHARE, SHARE)
         product_on_gpsimd(5, GROUP)
-        product_on_gpsimd(6, GROUP)
+        gated_first1 = keep.tile([P, QUARTER // P, P], F32, name="gated_first1")
+        gated_by_scalar(first_q, 0, 1, 2, gated_first1)
+        silu(6, 5)
         y_first1 = keep.tile([P, QUARTER], F32, name="y_first1")
-        turn_back(gated_first1, 2, y_first1[:])
+        turn_back(gated_first1, 6, y_first1[:])
         scatter_plain(y_first1[:], 0, 1)
-        lin_out(7, 0)
-        gated_second0 = rounded_row[:, HALF * PACK :].bitcast(F32).rearrange("p (i m) -> p i m", m=P)
-        gated_by_scalar(second_q, QUARTER, 0, 4, gated_second0)
-        silu(7, 7)
+        lin_out(6, 1)
+        product_on_gpsimd(6, GROUP)
+        gated_second0 = (
+            rounded_row[:, (SECOND_AT + 3 * GROUP) * PACK :].bitcast(F32).rearrange("p (i m) -> p i m", m=P)
+        )
+        gated_by_scalar(second_q, QUARTER, 0, 7, gated_second0)
+        silu(7, 3)
         y_second0 = keep.tile([P, QUARTER], F32, name="y_second0")
-        turn_back(gated_second0, 3, y_second0[:])
+        turn_back(gated_second0, 5, y_second0[:])
         scatter_plain(y_second0[:], QUARTER, 0)
+        lin_out(7, 0)
         product_on_gpsimd(7, GROUP)
 
         last_q = quantize_h(HALF, HALF)
         y_second1 = lins[:, on_gpsimd.index(7), :QUARTER]
-        nc.scalar.copy(y_second1, rows_on_partitions(second_q, 0, QUARTER, 1, 5))
+        nc.scalar.copy(y_second1, rows_on_partitions(second_q, 0, QUARTER, 1, 4))
         scatter_gated(y_second1, QUARTER, QUARTER, 1)
         y_last0 = keep.tile([P, HALF], F32, name="y_last0")
-        for i, b in enumerate((1, 6)):
+        for i, b in enumerate((1, 2)):
             c0 = i * QUARTER
             nc.scalar.copy(y_last0[:, c0 : c0 + QUARTER], rows_on_partitions(last_q, c0, QUARTER, 0, b))
         y_last1 = keep.tile([P, HALF], F32, name="y_last1")
-        nc.scalar.copy(y_last1[:], rows_on_partitions(last_q, 0, HALF, 1, 4))
+        nc.scalar.copy(y_last1[:], rows_on_partitions(last_q, 0, HALF, 1, 3))
         scatter_gated(y_last0[:], HALF, HALF, 0)
-        nc.sync.dma_start(out[0:P, :], windows[0][:])
+        for c0 in range(0, U, U // 8):
+            nc.sync.dma_start(out[0:P, c0 : c0 + U // 8], windows[0][:, c0 : c0 + U // 8])
         scatter_gated(y_last1[:], HALF, HALF, 1)
         nc.sync.dma_start(out[P : 2 * P, :], windows[1][:])

@@ -28,14 +28,14 @@ SHARE = 96
 SECOND_AT = QUARTER - SHARE
 
 OVERLAP = 64
-W3_FIRST_AT = 0
+ACTS_AT = 0
+W3_FIRST_AT = ACTS_AT + S * PACK * 4 - OVERLAP
 PLANES_AT = W3_FIRST_AT + PACK * (H // 2) * 4 - OVERLAP
 W3_SECOND_AT = PLANES_AT + T - OVERLAP
-GATE_ROWS_AT = W3_SECOND_AT + PACK * (H // 2) * 4
-ZEROS = 64
-ZERO_AT = GATE_ROWS_AT + S * 4 - OVERLAP
-GATE_COLUMNS_AT = ZERO_AT + OVERLAP
-W2_AT = GATE_COLUMNS_AT + OVERLAP
+W2_AT = W3_SECOND_AT + PACK * (H // 2) * 4
+GATE_COLUMNS_AT = W2_AT + PACK * H * 4
+GATE_ROWS_AT = GATE_COLUMNS_AT + OVERLAP
+W1_AT = GATE_ROWS_AT + 2 * OVERLAP - PACK * H * 4
 
 
 def tile_picked_route2_glusilu_p_kernel(
@@ -51,27 +51,19 @@ def tile_picked_route2_glusilu_p_kernel(
         dst_sb = keep.tile([P, S // LIST], U16, name="dst_sb")
         planes = shared.tile([P, T], U8, name="planes", align_bytes=64, offset=PLANES_AT)
         windows = [keep.tile([P, U], F32, name=f"window{r}") for r in range(N // P)]
-        zero = shared.tile([P, ZEROS], F32, name="zero", align_bytes=64, offset=ZERO_AT)
+        zero = keep.tile([P, 1], F32, name="zero")
 
         nc.sync.dma_start(planes[P - ROWS :, :].bitcast(I32), x_scales[0].bitcast(I32))
         nc.sync.dma_start(offs_sb[:], offs)
-        nc.sync.dma_start(dst_sb[:], dst)
+        w1_raw = shared.tile([P, PACK, H], F32, name="w1_raw", align_bytes=64, offset=W1_AT)
+        nc.sync.dma_start(w1_raw[:], w1.rearrange("(p j) c -> p j c", j=PACK))
         words = keep.tile([P, T], I32, name="words")
         nc.sync.dma_start(words[:], x_words[0].rearrange("p c r -> p (c r)").bitcast(I32))
-        w1_rows = w1.rearrange("(p j) (u c) -> p u j c", j=PACK, u=2)
-        w1_raw = []
-        for u in range(2):
-            raw = keep.tile([P, PACK, H // 2], F32, name=f"w1_raw{u}", align_bytes=64)
-            nc.sync.dma_start(raw[:], w1_rows[:, u])
-            w1_raw.append(raw)
+        nc.sync.dma_start(dst_sb[:], dst)
 
         nc.vector.memset(zero[:], 0.0)
         nc.vector.memset(planes[: P - ROWS, :].bitcast(I32), 0)
-        nc.scalar.activation(
-            windows[1][:].rearrange("p (a b) -> p a b", b=ZEROS),
-            zero[:].unsqueeze(1).to_broadcast([P, U // ZEROS, ZEROS]),
-            SILU,
-        )
+        nc.scalar.activation(windows[1][:], zero[:].to_broadcast([P, U]), SILU)
         nc.vector.memset(windows[0][:], 0.0)
 
         picked_planes = keep.tile([P, S], U8, name="picked_planes")
@@ -128,26 +120,21 @@ def tile_picked_route2_glusilu_p_kernel(
             return stationary
 
         low, high, every = slice(0, 2), slice(2, 4), slice(0, 4)
+        w1_grouped = round_first(
+            "w1", [(w1_raw[:], 0, low, nc.vector.tensor_copy), (w1_raw[:], 0, high, nc.scalar.copy)]
+        )
+        w1_q = quantize_first(w1_grouped, "w1", PACK)
+
         x_codes = []
         for g in range(S // HALF):
             picked = keep.tile([P, HALF], U32, name=f"x_codes{g}", align_bytes=64)
             nc.vector.tensor_copy(picked[:], words[:].bitcast(U32).indirect(offs_sb[:, list_columns(g * HALF, HALF)]))
             x_codes.append(picked)
 
-        w1_grouped = round_first(
-            "w1",
-            [
-                (w1_raw[0][:], 0, every, nc.scalar.copy),
-                (w1_raw[1][:], P // 2, low, nc.vector.tensor_copy),
-                (w1_raw[1][:], P // 2, high, nc.scalar.copy),
-            ],
-        )
-        w1_q = quantize_first(w1_grouped, "w1", 2)
-
         w3_grouped = round_first(
             "w3",
             [
-                (w3_raw[0][:], 0, every, nc.vector.tensor_copy),
+                (w3_raw[0][:], 0, every, nc.scalar.copy),
                 (w3_raw[1][:], P // 2, low, nc.vector.tensor_copy),
                 (w3_raw[1][:], P // 2, high, nc.vector.tensor_copy),
             ],
@@ -174,7 +161,7 @@ def tile_picked_route2_glusilu_p_kernel(
                 )
             return up[:].rearrange("p t n -> p n t")
 
-        acts = keep.tile([P, S, PACK], F32, name="acts", align_bytes=64)
+        acts = shared.tile([P, S, PACK], F32, name="acts", align_bytes=64, offset=ACTS_AT)
         on_gpsimd = (4, 5, 6, 7)
         lins = keep.tile([P, len(on_gpsimd), GROUP * PACK], F32, name="lins")
         w2_grouped = keep.tile([P, N, PACK], BF16, name="w2_grouped", align_bytes=64)
@@ -294,7 +281,6 @@ def tile_picked_route2_glusilu_p_kernel(
         y_last1 = keep.tile([P, HALF], F32, name="y_last1")
         nc.scalar.copy(y_last1[:], rows_on_partitions(last_q, 0, HALF, 1, 3))
         scatter_gated(y_last0[:], HALF, HALF, 0)
-        for c0 in range(0, U, U // 8):
-            nc.sync.dma_start(out[0:P, c0 : c0 + U // 8], windows[0][:, c0 : c0 + U // 8])
+        nc.sync.dma_start(out[0:P, :], windows[0][:])
         scatter_gated(y_last1[:], HALF, HALF, 1)
         nc.sync.dma_start(out[P : 2 * P, :], windows[1][:])

@@ -230,14 +230,16 @@ def tile_picked_route2_glusilu_p_kernel(
             places = dst_sb[:, list_columns(j0, n)]
             nc.vector.tensor_tensor(windows[r][:].indirect(places), y, gate_rows[:, j0 : j0 + n], MULT)
 
-        nc.vector.tensor_copy(w2_grouped[:], w2_raw[:].rearrange("p t n -> p n t"))
+        nc.vector.tensor_copy(
+            w2_grouped[:].rearrange("p (c i) t -> p c t i", i=PACK), w2_raw[:].rearrange("p t (c i) -> p c t i", i=PACK)
+        )
         for k in range(4):
             silu(k, k)
-        silu(4, 7)
         for k in range(2):
             product_on_vector(first_product(w3_q, k, 4 + k), k * GROUP, GROUP)
-        lin_out(4, 1)
-        lin_out(5, 3)
+        silu(4, 2)
+        lin_out(4, 7)
+        lin_out(5, 1)
         silu(5, 4)
         w2_q = quantize(w2_grouped[:].rearrange("p n t -> p (n t)"), "w2")
         first_q = quantize_h(0, QUARTER)
@@ -245,14 +247,14 @@ def tile_picked_route2_glusilu_p_kernel(
         product_on_vector(first_product(w3_q, 3, 0), 3 * GROUP, GROUP)
         product_on_gpsimd(4, SHARE)
         y_first0 = keep.tile([P, QUARTER], F32, name="y_first0")
-        nc.vector.tensor_tensor(y_first0[:], rows_on_partitions(first_q, 0, QUARTER, 0, 7), gate_rows[:, :QUARTER], MULT)
+        nc.vector.tensor_tensor(y_first0[:], rows_on_partitions(first_q, 0, QUARTER, 0, 3), gate_rows[:, :QUARTER], MULT)
         second_q = quantize_h(QUARTER, QUARTER)
 
         scatter_plain(y_first0[:], 0, 0)
         product_on_gpsimd(4, GROUP - SHARE, SHARE)
         product_on_gpsimd(5, GROUP)
         gated_first1 = keep.tile([P, QUARTER // P, P], F32, name="gated_first1")
-        gated_by_scalar(first_q, 0, 1, 2, gated_first1)
+        gated_by_scalar(first_q, 0, 1, 7, gated_first1)
         silu(6, 5)
         y_first1 = keep.tile([P, QUARTER], F32, name="y_first1")
         turn_back(gated_first1, 6, y_first1[:])
@@ -262,8 +264,8 @@ def tile_picked_route2_glusilu_p_kernel(
         gated_second0 = (
             rounded_row[:, (SECOND_AT + 3 * GROUP) * PACK :].bitcast(F32).rearrange("p (i m) -> p i m", m=P)
         )
-        gated_by_scalar(second_q, QUARTER, 0, 7, gated_second0)
-        silu(7, 3)
+        gated_by_scalar(second_q, QUARTER, 0, 3, gated_second0)
+        silu(7, 2)
         y_second0 = keep.tile([P, QUARTER], F32, name="y_second0")
         turn_back(gated_second0, 5, y_second0[:])
         scatter_plain(y_second0[:], QUARTER, 0)

@@ -24,16 +24,19 @@ ROWS = K // 32
 GROUP = 128
 HALF = S // 2
 QUARTER = S // 4
-SHARE = 96
+SHARE = 80
+
 SECOND_AT = QUARTER - SHARE
+H_ROW = (SECOND_AT + HALF) * PACK
 
 OVERLAP = 64
 ACTS_AT = 0
 W3_FIRST_AT = ACTS_AT + S * PACK * 4 - OVERLAP
 PLANES_AT = W3_FIRST_AT + PACK * (H // 2) * 4 - OVERLAP
 W3_SECOND_AT = PLANES_AT + T - OVERLAP
-W2_AT = W3_SECOND_AT + PACK * (H // 2) * 4
-GATE_COLUMNS_AT = W2_AT + PACK * H * 4
+H_ROW_AT = W3_SECOND_AT + PACK * (H // 2) * 4
+W2_FROM = GROUP * PACK - OVERLAP // 2
+GATE_COLUMNS_AT = H_ROW_AT + PACK * H * 4
 GATE_ROWS_AT = GATE_COLUMNS_AT + OVERLAP
 W1_AT = GATE_ROWS_AT + 2 * OVERLAP - PACK * H * 4
 
@@ -80,10 +83,11 @@ def tile_picked_route2_glusilu_p_kernel(
             nc.sync.dma_start(raw[:], w3_rows[:, u])
             w3_raw.append(raw)
 
-        w2_raw = shared.tile([P, PACK, N], F32, name="w2_raw", align_bytes=64, offset=W2_AT)
+        h_row = shared.tile([P, H_ROW], BF16, name="h_row", align_bytes=64, offset=H_ROW_AT)
+        w2_raw = h_row[:, W2_FROM : W2_FROM + 2 * PACK * N].bitcast(F32).rearrange("p (t n) -> p t n", t=PACK)
         gate_rows = shared.tile([P, S], F32, name="gate_rows", align_bytes=64, offset=GATE_ROWS_AT)
         gate_columns = shared.tile([P, HALF // P], F32, name="gate_columns", align_bytes=64, offset=GATE_COLUMNS_AT)
-        nc.sync.dma_start(w2_raw[:], w2.rearrange("(p t) n -> p t n", t=PACK))
+        nc.sync.dma_start(w2_raw, w2.rearrange("(p t) n -> p t n", t=PACK))
         nc.sync.dma_start(gate_rows[:], gate)
         with nc.allow_non_contiguous_dma(reason="one gate value a partition"):
             nc.sync.dma_start(gate_columns[:], gate[0, :HALF].rearrange("(c p) -> p c", p=P))
@@ -162,33 +166,31 @@ def tile_picked_route2_glusilu_p_kernel(
             return up[:].rearrange("p t n -> p n t")
 
         acts = shared.tile([P, S, PACK], F32, name="acts", align_bytes=64, offset=ACTS_AT)
-        on_gpsimd = (4, 5, 6, 7)
-        lins = keep.tile([P, len(on_gpsimd), GROUP * PACK], F32, name="lins")
+        lins_row = keep.tile([P, HALF * PACK], F32, name="lins")
+        lins = lins_row[:].rearrange("p (n t) -> p n t", t=PACK)
         w2_grouped = keep.tile([P, N, PACK], BF16, name="w2_grouped", align_bytes=64)
-        rounded_row = shared.tile([P, (SECOND_AT + HALF) * PACK], BF16, name="rounded", align_bytes=64, offset=W2_AT)
-        rounded = rounded_row[:].rearrange("p (n t) -> p n t", t=PACK)
+        rounded = h_row[:].rearrange("p (n t) -> p n t", t=PACK)
 
         def h_part(j0, n):
             c0 = j0 if j0 < HALF else j0 - HALF + SECOND_AT
             return rounded[:, c0 : c0 + n, :]
 
-        def lin_part(k, n, c0=0):
-            return lins[:, on_gpsimd.index(k), c0 * PACK : (c0 + n) * PACK].rearrange("p (n t) -> p n t", t=PACK)
+        def lin_part(j0, n):
+            return lins[:, j0 - HALF : j0 - HALF + n, :]
 
         def silu(k, b):
             j0 = k * GROUP
             nc.scalar.activation(acts[:, j0 : j0 + GROUP, :], first_product(w1_q, k, b), SILU)
 
         def lin_out(k, b):
-            nc.scalar.copy(lin_part(k, GROUP), first_product(w3_q, k, b))
+            nc.scalar.copy(lin_part(k * GROUP, GROUP), first_product(w3_q, k, b))
 
-        def product_on_vector(lin, j0, n):
-            c0 = j0 % GROUP
-            nc.vector.tensor_tensor(h_part(j0, n), lin[:, c0 : c0 + n, :], acts[:, j0 : j0 + n, :], MULT)
+        def product_on_vector(k, b):
+            j0 = k * GROUP
+            nc.vector.tensor_tensor(h_part(j0, GROUP), first_product(w3_q, k, b), acts[:, j0 : j0 + GROUP, :], MULT)
 
-        def product_on_gpsimd(k, n, c0=0):
-            j0 = k * GROUP + c0
-            nc.gpsimd.tensor_tensor(h_part(j0, n), lin_part(k, n, c0), acts[:, j0 : j0 + n, :], MULT)
+        def product_on_gpsimd(j0, n):
+            nc.gpsimd.tensor_tensor(h_part(j0, n), lin_part(j0, n), acts[:, j0 : j0 + n, :], MULT)
 
         def quantize_h(j0, n):
             return quantize(h_part(j0, n).rearrange("p n t -> p (n t)"), f"h{j0}")
@@ -230,29 +232,30 @@ def tile_picked_route2_glusilu_p_kernel(
             places = dst_sb[:, list_columns(j0, n)]
             nc.vector.tensor_tensor(windows[r][:].indirect(places), y, gate_rows[:, j0 : j0 + n], MULT)
 
-        nc.vector.tensor_copy(
-            w2_grouped[:].rearrange("p (c i) t -> p c t i", i=PACK), w2_raw[:].rearrange("p t (c i) -> p c t i", i=PACK)
-        )
+        for r in range(N // P):
+            nc.vector.tensor_copy(
+                w2_grouped[:, r * P : (r + 1) * P, :].rearrange("p (c i) t -> p c t i", i=PACK),
+                w2_raw[:, :, r * P : (r + 1) * P].rearrange("p t (c i) -> p c t i", i=PACK),
+            )
         for k in range(4):
             silu(k, k)
         for k in range(2):
-            product_on_vector(first_product(w3_q, k, 4 + k), k * GROUP, GROUP)
+            product_on_vector(k, 4 + k)
         silu(4, 2)
         lin_out(4, 7)
         lin_out(5, 1)
         silu(5, 4)
         w2_q = quantize(w2_grouped[:].rearrange("p n t -> p (n t)"), "w2")
         first_q = quantize_h(0, QUARTER)
-        product_on_vector(first_product(w3_q, 2, 6), 2 * GROUP, GROUP)
-        product_on_vector(first_product(w3_q, 3, 0), 3 * GROUP, GROUP)
-        product_on_gpsimd(4, SHARE)
+        product_on_vector(2, 6)
+        product_on_vector(3, 0)
+        product_on_gpsimd(HALF, SHARE)
         y_first0 = keep.tile([P, QUARTER], F32, name="y_first0")
         nc.vector.tensor_tensor(y_first0[:], rows_on_partitions(first_q, 0, QUARTER, 0, 3), gate_rows[:, :QUARTER], MULT)
         second_q = quantize_h(QUARTER, QUARTER)
 
         scatter_plain(y_first0[:], 0, 0)
-        product_on_gpsimd(4, GROUP - SHARE, SHARE)
-        product_on_gpsimd(5, GROUP)
+        product_on_gpsimd(HALF + SHARE, 2 * GROUP - SHARE)
         gated_first1 = keep.tile([P, QUARTER // P, P], F32, name="gated_first1")
         gated_by_scalar(first_q, 0, 1, 7, gated_first1)
         silu(6, 5)
@@ -260,20 +263,18 @@ def tile_picked_route2_glusilu_p_kernel(
         turn_back(gated_first1, 6, y_first1[:])
         scatter_plain(y_first1[:], 0, 1)
         lin_out(6, 1)
-        product_on_gpsimd(6, GROUP)
-        gated_second0 = (
-            rounded_row[:, (SECOND_AT + 3 * GROUP) * PACK :].bitcast(F32).rearrange("p (i m) -> p i m", m=P)
-        )
+        product_on_gpsimd(6 * GROUP, GROUP)
+        gated_second0 = h_row[:, H_ROW - GROUP * PACK :].bitcast(F32).rearrange("p (i m) -> p i m", m=P)
         gated_by_scalar(second_q, QUARTER, 0, 3, gated_second0)
         silu(7, 2)
         y_second0 = keep.tile([P, QUARTER], F32, name="y_second0")
         turn_back(gated_second0, 5, y_second0[:])
         scatter_plain(y_second0[:], QUARTER, 0)
         lin_out(7, 0)
-        product_on_gpsimd(7, GROUP)
+        product_on_gpsimd(7 * GROUP, GROUP)
 
         last_q = quantize_h(HALF, HALF)
-        y_second1 = lins[:, on_gpsimd.index(7), :QUARTER]
+        y_second1 = lins_row[:, (HALF - GROUP) * PACK :][:, :QUARTER]
         nc.scalar.copy(y_second1, rows_on_partitions(second_q, 0, QUARTER, 1, 4))
         scatter_gated(y_second1, QUARTER, QUARTER, 1)
         y_last0 = keep.tile([P, HALF], F32, name="y_last0")

@@ -1,7 +1,6 @@
 from contextlib import ExitStack
 
 import concourse.mybir as mybir
-from concourse.masks import make_identity
 
 K, T, S, H, N, U = 512, 4096, 1024, 512, 256, 2048
 FLOPS = 2 * K * H * S * 2 + 2 * H * N * S
@@ -22,12 +21,8 @@ PACK = 4
 LIST = 16
 ROWS = K // 32
 GROUP = 128
-HALF = S // 2
-QUARTER = S // 4
-SHARE = 80
-
-SECOND_AT = QUARTER - SHARE
-H_ROW = (SECOND_AT + HALF) * PACK
+GATHERS = ((0, 512), (512, 512))
+CHUNKS = ((0, 256), (256, 384), (640, 384))
 
 OVERLAP = 64
 ACTS_AT = 0
@@ -36,9 +31,8 @@ PLANES_AT = W3_FIRST_AT + PACK * (H // 2) * 4 - OVERLAP
 W3_SECOND_AT = PLANES_AT + T - OVERLAP
 H_ROW_AT = W3_SECOND_AT + PACK * (H // 2) * 4
 W2_FROM = GROUP * PACK - OVERLAP // 2
-GATE_COLUMNS_AT = H_ROW_AT + PACK * H * 4
-GATE_ROWS_AT = GATE_COLUMNS_AT + OVERLAP
-W1_AT = GATE_ROWS_AT + 2 * OVERLAP - PACK * H * 4
+GATE_AT = H_ROW_AT + S * PACK * 2
+W1_AT = GATE_AT + OVERLAP - PACK * H * 4
 
 
 def tile_picked_route2_glusilu_p_kernel(
@@ -83,16 +77,11 @@ def tile_picked_route2_glusilu_p_kernel(
             nc.sync.dma_start(raw[:], w3_rows[:, u])
             w3_raw.append(raw)
 
-        h_row = shared.tile([P, H_ROW], BF16, name="h_row", align_bytes=64, offset=H_ROW_AT)
+        h_row = shared.tile([P, S * PACK], BF16, name="h_row", align_bytes=64, offset=H_ROW_AT)
         w2_raw = h_row[:, W2_FROM : W2_FROM + 2 * PACK * N].bitcast(F32).rearrange("p (t n) -> p t n", t=PACK)
-        gate_rows = shared.tile([P, S], F32, name="gate_rows", align_bytes=64, offset=GATE_ROWS_AT)
-        gate_columns = shared.tile([P, HALF // P], F32, name="gate_columns", align_bytes=64, offset=GATE_COLUMNS_AT)
+        gate_rows = shared.tile([P, S], F32, name="gate_rows", align_bytes=64, offset=GATE_AT)
         nc.sync.dma_start(w2_raw, w2.rearrange("(p t) n -> p t n", t=PACK))
         nc.sync.dma_start(gate_rows[:], gate)
-        with nc.allow_non_contiguous_dma(reason="one gate value a partition"):
-            nc.sync.dma_start(gate_columns[:], gate[0, :HALF].rearrange("(c p) -> p c", p=P))
-        identity = keep.tile([P, P], F32, name="identity")
-        make_identity(nc, identity[:])
 
         def list_columns(j0, n):
             return slice(j0 // LIST, (j0 + n) // LIST)
@@ -130,10 +119,10 @@ def tile_picked_route2_glusilu_p_kernel(
         w1_q = quantize_first(w1_grouped, "w1", PACK)
 
         x_codes = []
-        for g in range(S // HALF):
-            picked = keep.tile([P, HALF], U32, name=f"x_codes{g}", align_bytes=64)
-            nc.vector.tensor_copy(picked[:], words[:].bitcast(U32).indirect(offs_sb[:, list_columns(g * HALF, HALF)]))
-            x_codes.append(picked)
+        for j0, n in GATHERS:
+            picked = keep.tile([P, n], U32, name=f"x_codes{j0}", align_bytes=64)
+            nc.vector.tensor_copy(picked[:], words[:].bitcast(U32).indirect(offs_sb[:, list_columns(j0, n)]))
+            x_codes.extend((picked, c0) for c0 in range(0, n, GROUP))
 
         w3_grouped = round_first(
             "w3",
@@ -150,87 +139,57 @@ def tile_picked_route2_glusilu_p_kernel(
 
         def first_product(w_q, k, b):
             up = bank(b, [P, PACK, GROUP])
-            j0 = k * GROUP
-            picked = x_codes[j0 // HALF]
-            c0 = j0 % HALF
+            picked, c0 = x_codes[k]
             for t in range(PACK):
                 nc.tensor.matmul_mx(
                     out=up[:, t, :],
                     lhsT=w_q[t][0].bitcast(FP8X4),
                     lhsT_scale=w_q[t][1],
                     rhs=picked[:, c0 : c0 + GROUP].bitcast(FP8X4),
-                    rhs_scale=x_planes[:, j0 : j0 + GROUP],
+                    rhs_scale=x_planes[:, k * GROUP : (k + 1) * GROUP],
                     start=True,
                     stop=True,
                 )
             return up[:].rearrange("p t n -> p n t")
 
         acts = shared.tile([P, S, PACK], F32, name="acts", align_bytes=64, offset=ACTS_AT)
-        lins_row = keep.tile([P, HALF * PACK], F32, name="lins")
-        lins = lins_row[:].rearrange("p (n t) -> p n t", t=PACK)
         w2_grouped = keep.tile([P, N, PACK], BF16, name="w2_grouped", align_bytes=64)
         rounded = h_row[:].rearrange("p (n t) -> p n t", t=PACK)
 
-        def h_part(j0, n):
-            c0 = j0 if j0 < HALF else j0 - HALF + SECOND_AT
-            return rounded[:, c0 : c0 + n, :]
-
-        def lin_part(j0, n):
-            return lins[:, j0 - HALF : j0 - HALF + n, :]
-
         def silu(k, b):
-            j0 = k * GROUP
-            nc.scalar.activation(acts[:, j0 : j0 + GROUP, :], first_product(w1_q, k, b), SILU)
+            nc.scalar.activation(acts[:, k * GROUP : (k + 1) * GROUP, :], first_product(w1_q, k, b), SILU)
 
-        def lin_out(k, b):
-            nc.scalar.copy(lin_part(k * GROUP, GROUP), first_product(w3_q, k, b))
+        def product(k, b):
+            tokens = slice(k * GROUP, (k + 1) * GROUP)
+            nc.vector.tensor_tensor(rounded[:, tokens, :], first_product(w3_q, k, b), acts[:, tokens, :], MULT)
 
-        def product_on_vector(k, b):
-            j0 = k * GROUP
-            nc.vector.tensor_tensor(h_part(j0, GROUP), first_product(w3_q, k, b), acts[:, j0 : j0 + GROUP, :], MULT)
+        def quantize_h(c):
+            j0, n = CHUNKS[c]
+            return quantize(h_row[:, j0 * PACK : (j0 + n) * PACK], f"h{c}")
 
-        def product_on_gpsimd(j0, n):
-            nc.gpsimd.tensor_tensor(h_part(j0, n), lin_part(j0, n), acts[:, j0 : j0 + n, :], MULT)
-
-        def quantize_h(j0, n):
-            return quantize(h_part(j0, n).rearrange("p n t -> p (n t)"), f"h{j0}")
-
-        def second_product(out_ap, stationary, s0, moving, m0, width):
-            nc.tensor.matmul_mx(
-                out=out_ap,
-                lhsT=stationary[0][:, s0 : s0 + P].bitcast(FP8X4),
-                lhsT_scale=stationary[1][:, s0 : s0 + P],
-                rhs=moving[0][:, m0 : m0 + width].bitcast(FP8X4),
-                rhs_scale=moving[1][:, m0 : m0 + width],
-                start=True,
-                stop=True,
-            )
-
-        def rows_on_partitions(h_q, c0, n, r, b):
+        def gated(h_q, c, r, b):
+            j0, n = CHUNKS[c]
             down = bank(b, [P, n])
-            second_product(down[:], w2_q, r * P, h_q, c0, n)
-            return down[:]
+            for c0 in range(0, n, 2 * GROUP):
+                width = min(2 * GROUP, n - c0)
+                nc.tensor.matmul_mx(
+                    out=down[:, c0 : c0 + width],
+                    lhsT=w2_q[0][:, r * P : (r + 1) * P].bitcast(FP8X4),
+                    lhsT_scale=w2_q[1][:, r * P : (r + 1) * P],
+                    rhs=h_q[0][:, c0 : c0 + width].bitcast(FP8X4),
+                    rhs_scale=h_q[1][:, c0 : c0 + width],
+                    start=True,
+                    stop=True,
+                )
+            y = keep.tile([P, n], F32, name=f"y{c}_{r}")
+            nc.vector.tensor_tensor(y[:], down[:], gate_rows[:, j0 : j0 + n], MULT)
+            return y
 
-        def gated_by_scalar(h_q, j0, r, b, gated):
-            down = bank(b, [P, QUARTER // P, P])
-            for i in range(QUARTER // P):
-                second_product(down[:, i, :], h_q, i * P, w2_q, r * P, P)
-            for i in range(QUARTER // P):
-                c = j0 // P + i
-                nc.scalar.activation(gated[:, i, :], down[:, i, :], COPY, scale=gate_columns[:, c : c + 1])
+        def places(c, r):
+            return windows[r][:].indirect(dst_sb[:, list_columns(*CHUNKS[c])])
 
-        def turn_back(gated, b, y):
-            turned = bank(b, [P, QUARTER])
-            for i in range(QUARTER // P):
-                nc.tensor.transpose(turned[:, i * P : (i + 1) * P], gated[:, i, :], identity[:])
-            nc.scalar.copy(y, turned[:])
-
-        def scatter_plain(y, j0, r):
-            nc.vector.tensor_copy(windows[r][:].indirect(dst_sb[:, list_columns(j0, QUARTER)]), y)
-
-        def scatter_gated(y, j0, n, r):
-            places = dst_sb[:, list_columns(j0, n)]
-            nc.vector.tensor_tensor(windows[r][:].indirect(places), y, gate_rows[:, j0 : j0 + n], MULT)
+        def scatter_on_scalar(y, c, r):
+            nc.scalar.activation(places(c, r), y[:], COPY)
 
         for r in range(N // P):
             nc.vector.tensor_copy(
@@ -239,51 +198,33 @@ def tile_picked_route2_glusilu_p_kernel(
             )
         for k in range(4):
             silu(k, k)
-        for k in range(2):
-            product_on_vector(k, 4 + k)
-        silu(4, 2)
-        lin_out(4, 7)
-        lin_out(5, 1)
-        silu(5, 4)
+        silu(4, 0)
+        product(0, 4)
+        product(1, 5)
         w2_q = quantize(w2_grouped[:].rearrange("p n t -> p (n t)"), "w2")
-        first_q = quantize_h(0, QUARTER)
-        product_on_vector(2, 6)
-        product_on_vector(3, 0)
-        product_on_gpsimd(HALF, SHARE)
-        y_first0 = keep.tile([P, QUARTER], F32, name="y_first0")
-        nc.vector.tensor_tensor(y_first0[:], rows_on_partitions(first_q, 0, QUARTER, 0, 3), gate_rows[:, :QUARTER], MULT)
-        second_q = quantize_h(QUARTER, QUARTER)
-
-        scatter_plain(y_first0[:], 0, 0)
-        product_on_gpsimd(HALF + SHARE, 2 * GROUP - SHARE)
-        gated_first1 = keep.tile([P, QUARTER // P, P], F32, name="gated_first1")
-        gated_by_scalar(first_q, 0, 1, 7, gated_first1)
-        silu(6, 5)
-        y_first1 = keep.tile([P, QUARTER], F32, name="y_first1")
-        turn_back(gated_first1, 6, y_first1[:])
-        scatter_plain(y_first1[:], 0, 1)
-        lin_out(6, 1)
-        product_on_gpsimd(6 * GROUP, GROUP)
-        gated_second0 = h_row[:, H_ROW - GROUP * PACK :].bitcast(F32).rearrange("p (i m) -> p i m", m=P)
-        gated_by_scalar(second_q, QUARTER, 0, 3, gated_second0)
-        silu(7, 2)
-        y_second0 = keep.tile([P, QUARTER], F32, name="y_second0")
-        turn_back(gated_second0, 5, y_second0[:])
-        scatter_plain(y_second0[:], QUARTER, 0)
-        lin_out(7, 0)
-        product_on_gpsimd(7 * GROUP, GROUP)
-
-        last_q = quantize_h(HALF, HALF)
-        y_second1 = lins_row[:, (HALF - GROUP) * PACK :][:, :QUARTER]
-        nc.scalar.copy(y_second1, rows_on_partitions(second_q, 0, QUARTER, 1, 4))
-        scatter_gated(y_second1, QUARTER, QUARTER, 1)
-        y_last0 = keep.tile([P, HALF], F32, name="y_last0")
-        for i, b in enumerate((1, 2)):
-            c0 = i * QUARTER
-            nc.scalar.copy(y_last0[:, c0 : c0 + QUARTER], rows_on_partitions(last_q, c0, QUARTER, 0, b))
-        y_last1 = keep.tile([P, HALF], F32, name="y_last1")
-        nc.scalar.copy(y_last1[:], rows_on_partitions(last_q, 0, HALF, 1, 3))
-        scatter_gated(y_last0[:], HALF, HALF, 0)
+        h_q = quantize_h(0)
+        y_00 = gated(h_q, 0, 0, 7)
+        y_01 = gated(h_q, 0, 1, 4)
+        product(2, 6)
+        product(3, 1)
+        silu(5, 2)
+        silu(6, 3)
+        silu(7, 0)
+        scatter_on_scalar(y_00, 0, 0)
+        scatter_on_scalar(y_01, 0, 1)
+        product(4, 5)
+        h_q = quantize_h(1)
+        y_10 = gated(h_q, 1, 0, 2)
+        product(5, 6)
+        product(6, 1)
+        product(7, 0)
+        last_q = quantize_h(2)
+        y_11 = gated(h_q, 1, 1, 3)
+        scatter_on_scalar(y_10, 1, 0)
+        scatter_on_scalar(y_11, 1, 1)
+        y_20 = gated(last_q, 2, 0, 7)
+        y_21 = gated(last_q, 2, 1, 4)
+        nc.vector.tensor_copy(places(2, 0), y_20[:])
         nc.sync.dma_start(out[0:P, :], windows[0][:])
-        scatter_gated(y_last1[:], HALF, HALF, 1)
+        scatter_on_scalar(y_21, 2, 1)
         nc.sync.dma_start(out[P : 2 * P, :], windows[1][:])

@@ -15,24 +15,29 @@ FP8X4 = mybir.dt.float8_e4m3fn_x4
 SILU = mybir.ActivationFunctionType.Silu
 COPY = mybir.ActivationFunctionType.Copy
 MULT = mybir.AluOpType.mult
+ADD = mybir.AluOpType.add
 
 P = 128
 PACK = 4
 LIST = 16
 ROWS = K // 32
 GROUP = 128
-GATHERS = ((0, 512), (512, 512))
+GATHERS = ((0, 512), (512, 256), (768, 256))
 CHUNKS = ((0, 256), (256, 384), (640, 384))
+ON_VECTOR = 448
 
 OVERLAP = 64
 ACTS_AT = 0
 W3_FIRST_AT = ACTS_AT + S * PACK * 4 - OVERLAP
 PLANES_AT = W3_FIRST_AT + PACK * (H // 2) * 4 - OVERLAP
 W3_SECOND_AT = PLANES_AT + T - OVERLAP
-H_ROW_AT = W3_SECOND_AT + PACK * (H // 2) * 4
-W2_FROM = GROUP * PACK - OVERLAP // 2
-GATE_AT = H_ROW_AT + S * PACK * 2
-W1_AT = GATE_AT + OVERLAP - PACK * H * 4
+LAST_CODES_AT = W3_SECOND_AT + T // 2
+W3_GROUPED_AT = W3_SECOND_AT + PACK * (H // 2) * 4
+H_ROW_AT = W3_GROUPED_AT + PACK * H * 2 - OVERLAP
+W2_FROM = 3 * GROUP * PACK - OVERLAP // 2
+W2_AT = H_ROW_AT + S * PACK * 2
+GATE_AT = W2_AT + PACK * N * 4
+W1_AT = GATE_AT - OVERLAP
 
 
 def tile_picked_route2_glusilu_p_kernel(
@@ -78,9 +83,9 @@ def tile_picked_route2_glusilu_p_kernel(
             w3_raw.append(raw)
 
         h_row = shared.tile([P, S * PACK], BF16, name="h_row", align_bytes=64, offset=H_ROW_AT)
-        w2_raw = h_row[:, W2_FROM : W2_FROM + 2 * PACK * N].bitcast(F32).rearrange("p (t n) -> p t n", t=PACK)
+        w2_raw = shared.tile([P, PACK, N], F32, name="w2_raw", align_bytes=64, offset=W2_AT)
         gate_rows = shared.tile([P, S], F32, name="gate_rows", align_bytes=64, offset=GATE_AT)
-        nc.sync.dma_start(w2_raw, w2.rearrange("(p t) n -> p t n", t=PACK))
+        nc.sync.dma_start(w2_raw[:], w2.rearrange("(p t) n -> p t n", t=PACK))
         nc.sync.dma_start(gate_rows[:], gate)
 
         def list_columns(j0, n):
@@ -93,15 +98,13 @@ def tile_picked_route2_glusilu_p_kernel(
             nc.vector.quantize_mx(out=codes[:].bitcast(FP8X4), scales=scales[:], in_=values)
             return codes, scales
 
-        def round_first(name, pieces):
-            grouped = keep.tile([P, PACK, P, PACK], BF16, name=f"{name}_grouped", align_bytes=64)
+        def round_first(grouped, pieces):
             for raw, m0, slots, copy in pieces:
                 m = slice(m0, m0 + raw.shape[2] // PACK)
                 copy(
                     grouped[:, slots, m, :].rearrange("p t m j -> p m j t"),
                     raw.rearrange("p j (m t) -> p m j t", t=PACK)[:, :, :, slots],
                 )
-            return grouped
 
         def quantize_first(grouped, name, slots_a_call):
             stationary = []
@@ -113,19 +116,22 @@ def tile_picked_route2_glusilu_p_kernel(
             return stationary
 
         low, high, every = slice(0, 2), slice(2, 4), slice(0, 4)
-        w1_grouped = round_first(
-            "w1", [(w1_raw[:], 0, low, nc.vector.tensor_copy), (w1_raw[:], 0, high, nc.scalar.copy)]
-        )
+        w1_grouped = keep.tile([P, PACK, P, PACK], BF16, name="w1_grouped", align_bytes=64)
+        round_first(w1_grouped, [(w1_raw[:], 0, low, nc.vector.tensor_copy), (w1_raw[:], 0, high, nc.scalar.copy)])
         w1_q = quantize_first(w1_grouped, "w1", PACK)
 
         x_codes = []
-        for j0, n in GATHERS:
-            picked = keep.tile([P, n], U32, name=f"x_codes{j0}", align_bytes=64)
+
+        def gather_words(picked, j0, n):
             nc.vector.tensor_copy(picked[:], words[:].bitcast(U32).indirect(offs_sb[:, list_columns(j0, n)]))
             x_codes.extend((picked, c0) for c0 in range(0, n, GROUP))
 
-        w3_grouped = round_first(
-            "w3",
+        for j0, n in GATHERS[:-1]:
+            gather_words(keep.tile([P, n], U32, name=f"x_codes{j0}", align_bytes=64), j0, n)
+
+        w3_grouped = shared.tile([P, PACK, P, PACK], BF16, name="w3_grouped", align_bytes=64, offset=W3_GROUPED_AT)
+        round_first(
+            w3_grouped,
             [
                 (w3_raw[0][:], 0, every, nc.scalar.copy),
                 (w3_raw[1][:], P // 2, low, nc.vector.tensor_copy),
@@ -133,6 +139,8 @@ def tile_picked_route2_glusilu_p_kernel(
             ],
         )
         w3_q = quantize_first(w3_grouped, "w3", 2)
+        last_codes = shared.tile([P, GATHERS[-1][1]], U32, name="last_codes", align_bytes=64, offset=LAST_CODES_AT)
+        gather_words(last_codes, *GATHERS[-1])
 
         def bank(b, shape):
             return psum.tile(shape, F32, name="bank", tag=f"bank{b}")
@@ -153,7 +161,7 @@ def tile_picked_route2_glusilu_p_kernel(
             return up[:].rearrange("p t n -> p n t")
 
         acts = shared.tile([P, S, PACK], F32, name="acts", align_bytes=64, offset=ACTS_AT)
-        w2_grouped = keep.tile([P, N, PACK], BF16, name="w2_grouped", align_bytes=64)
+        w2_grouped = h_row[:, W2_FROM : W2_FROM + N * PACK]
         rounded = h_row[:].rearrange("p (n t) -> p n t", t=PACK)
 
         def silu(k, b):
@@ -163,11 +171,16 @@ def tile_picked_route2_glusilu_p_kernel(
             tokens = slice(k * GROUP, (k + 1) * GROUP)
             nc.vector.tensor_tensor(rounded[:, tokens, :], first_product(w3_q, k, b), acts[:, tokens, :], MULT)
 
-        def quantize_h(c):
-            j0, n = CHUNKS[c]
-            return quantize(h_row[:, j0 * PACK : (j0 + n) * PACK], f"h{c}")
+        h_q = {}
 
-        def gated(h_q, c, r, b):
+        def quantize_h(j0, n):
+            codes, scales = quantize(h_row[:, j0 * PACK : (j0 + n) * PACK], f"h{j0}")
+            for c0 in range(0, n, 2 * GROUP):
+                h_q[j0 + c0] = (codes[:, c0 : min(n, c0 + 2 * GROUP)], scales[:, c0 : min(n, c0 + 2 * GROUP)])
+
+        y = [keep.tile([P, S], F32, name=f"y{r}") for r in range(N // P)]
+
+        def gated(c, r, b):
             j0, n = CHUNKS[c]
             down = bank(b, [P, n])
             for c0 in range(0, n, 2 * GROUP):
@@ -176,55 +189,57 @@ def tile_picked_route2_glusilu_p_kernel(
                     out=down[:, c0 : c0 + width],
                     lhsT=w2_q[0][:, r * P : (r + 1) * P].bitcast(FP8X4),
                     lhsT_scale=w2_q[1][:, r * P : (r + 1) * P],
-                    rhs=h_q[0][:, c0 : c0 + width].bitcast(FP8X4),
-                    rhs_scale=h_q[1][:, c0 : c0 + width],
+                    rhs=h_q[j0 + c0][0].bitcast(FP8X4),
+                    rhs_scale=h_q[j0 + c0][1],
                     start=True,
                     stop=True,
                 )
-            y = keep.tile([P, n], F32, name=f"y{c}_{r}")
-            nc.vector.tensor_tensor(y[:], down[:], gate_rows[:, j0 : j0 + n], MULT)
-            return y
+            nc.vector.tensor_tensor(y[r][:, j0 : j0 + n], down[:], gate_rows[:, j0 : j0 + n], MULT)
 
-        def places(c, r):
-            return windows[r][:].indirect(dst_sb[:, list_columns(*CHUNKS[c])])
+        def places(j0, n, r):
+            return windows[r][:].indirect(dst_sb[:, list_columns(j0, n)])
 
-        def scatter_on_scalar(y, c, r):
-            nc.scalar.activation(places(c, r), y[:], COPY)
+        def scatter_on_scalar(j0, n, r):
+            nc.scalar.activation(places(j0, n, r), y[r][:, j0 : j0 + n], COPY)
 
-        for r in range(N // P):
-            nc.vector.tensor_copy(
-                w2_grouped[:, r * P : (r + 1) * P, :].rearrange("p (c i) t -> p c t i", i=PACK),
-                w2_raw[:, :, r * P : (r + 1) * P].rearrange("p t (c i) -> p c t i", i=PACK),
-            )
+        nc.gpsimd.tensor_scalar(
+            w2_grouped.rearrange("p (n t) -> p n t", t=PACK),
+            w2_raw[:].rearrange("p t n -> p n t"),
+            1.0,
+            0.0,
+            op0=MULT,
+            op1=ADD,
+        )
         for k in range(4):
             silu(k, k)
         silu(4, 0)
         product(0, 4)
         product(1, 5)
-        w2_q = quantize(w2_grouped[:].rearrange("p n t -> p (n t)"), "w2")
-        h_q = quantize_h(0)
-        y_00 = gated(h_q, 0, 0, 7)
-        y_01 = gated(h_q, 0, 1, 4)
-        product(2, 6)
-        product(3, 1)
+        w2_q = quantize(w2_grouped, "w2")
+        quantize_h(*CHUNKS[0])
+        gated(0, 0, 4)
+        product(2, 7)
+        product(3, 6)
         silu(5, 2)
         silu(6, 3)
         silu(7, 0)
-        scatter_on_scalar(y_00, 0, 0)
-        scatter_on_scalar(y_01, 0, 1)
-        product(4, 5)
-        h_q = quantize_h(1)
-        y_10 = gated(h_q, 1, 0, 2)
-        product(5, 6)
-        product(6, 1)
-        product(7, 0)
-        last_q = quantize_h(2)
-        y_11 = gated(h_q, 1, 1, 3)
-        scatter_on_scalar(y_10, 1, 0)
-        scatter_on_scalar(y_11, 1, 1)
-        y_20 = gated(last_q, 2, 0, 7)
-        y_21 = gated(last_q, 2, 1, 4)
-        nc.vector.tensor_copy(places(2, 0), y_20[:])
+        scatter_on_scalar(*CHUNKS[0], 0)
+        product(4, 1)
+        gated(0, 1, 5)
+        scatter_on_scalar(*CHUNKS[0], 1)
+        quantize_h(*CHUNKS[1])
+        gated(1, 0, 2)
+        product(5, 7)
+        product(6, 6)
+        product(7, 1)
+        quantize_h(CHUNKS[2][0], 2 * GROUP)
+        quantize_h(S - GROUP, GROUP)
+        gated(1, 1, 3)
+        scatter_on_scalar(CHUNKS[1][0], S - ON_VECTOR - CHUNKS[1][0], 0)
+        scatter_on_scalar(*CHUNKS[1], 1)
+        gated(2, 0, 4)
+        gated(2, 1, 5)
+        nc.vector.tensor_copy(places(S - ON_VECTOR, ON_VECTOR, 0), y[0][:, S - ON_VECTOR :])
         nc.sync.dma_start(out[0:P, :], windows[0][:])
-        scatter_on_scalar(y_21, 2, 1)
+        scatter_on_scalar(*CHUNKS[2], 1)
         nc.sync.dma_start(out[P : 2 * P, :], windows[1][:])

@@ -15,29 +15,25 @@ FP8X4 = mybir.dt.float8_e4m3fn_x4
 SILU = mybir.ActivationFunctionType.Silu
 COPY = mybir.ActivationFunctionType.Copy
 MULT = mybir.AluOpType.mult
-ADD = mybir.AluOpType.add
 
 P = 128
 PACK = 4
 LIST = 16
 ROWS = K // 32
 GROUP = 128
-GATHERS = ((0, 512), (512, 256), (768, 256))
+GATHERS = ((0, 512), (512, 512))
 CHUNKS = ((0, 256), (256, 384), (640, 384))
-ON_VECTOR = 448
+ON_VECTOR = 416
 
 OVERLAP = 64
 ACTS_AT = 0
 W3_FIRST_AT = ACTS_AT + S * PACK * 4 - OVERLAP
 PLANES_AT = W3_FIRST_AT + PACK * (H // 2) * 4 - OVERLAP
 W3_SECOND_AT = PLANES_AT + T - OVERLAP
-LAST_CODES_AT = W3_SECOND_AT + T // 2
-W3_GROUPED_AT = W3_SECOND_AT + PACK * (H // 2) * 4
-H_ROW_AT = W3_GROUPED_AT + PACK * H * 2 - OVERLAP
-W2_FROM = 3 * GROUP * PACK - OVERLAP // 2
-W2_AT = H_ROW_AT + S * PACK * 2
-GATE_AT = W2_AT + PACK * N * 4
-W1_AT = GATE_AT - OVERLAP
+H_ROW_AT = W3_SECOND_AT + PACK * (H // 2) * 4
+W2_FROM = GROUP * PACK - OVERLAP // 2
+GATE_AT = H_ROW_AT + S * PACK * 2
+W1_AT = GATE_AT + OVERLAP - PACK * H * 4
 
 
 def tile_picked_route2_glusilu_p_kernel(
@@ -83,9 +79,9 @@ def tile_picked_route2_glusilu_p_kernel(
             w3_raw.append(raw)
 
         h_row = shared.tile([P, S * PACK], BF16, name="h_row", align_bytes=64, offset=H_ROW_AT)
-        w2_raw = shared.tile([P, PACK, N], F32, name="w2_raw", align_bytes=64, offset=W2_AT)
+        w2_raw = h_row[:, W2_FROM : W2_FROM + 2 * PACK * N].bitcast(F32).rearrange("p (t n) -> p t n", t=PACK)
         gate_rows = shared.tile([P, S], F32, name="gate_rows", align_bytes=64, offset=GATE_AT)
-        nc.sync.dma_start(w2_raw[:], w2.rearrange("(p t) n -> p t n", t=PACK))
+        nc.sync.dma_start(w2_raw, w2.rearrange("(p t) n -> p t n", t=PACK))
         nc.sync.dma_start(gate_rows[:], gate)
 
         def list_columns(j0, n):
@@ -98,13 +94,15 @@ def tile_picked_route2_glusilu_p_kernel(
             nc.vector.quantize_mx(out=codes[:].bitcast(FP8X4), scales=scales[:], in_=values)
             return codes, scales
 
-        def round_first(grouped, pieces):
+        def round_first(name, pieces):
+            grouped = keep.tile([P, PACK, P, PACK], BF16, name=f"{name}_grouped", align_bytes=64)
             for raw, m0, slots, copy in pieces:
                 m = slice(m0, m0 + raw.shape[2] // PACK)
                 copy(
                     grouped[:, slots, m, :].rearrange("p t m j -> p m j t"),
                     raw.rearrange("p j (m t) -> p m j t", t=PACK)[:, :, :, slots],
                 )
+            return grouped
 
         def quantize_first(grouped, name, slots_a_call):
             stationary = []
@@ -116,22 +114,19 @@ def tile_picked_route2_glusilu_p_kernel(
             return stationary
 
         low, high, every = slice(0, 2), slice(2, 4), slice(0, 4)
-        w1_grouped = keep.tile([P, PACK, P, PACK], BF16, name="w1_grouped", align_bytes=64)
-        round_first(w1_grouped, [(w1_raw[:], 0, low, nc.vector.tensor_copy), (w1_raw[:], 0, high, nc.scalar.copy)])
+        w1_grouped = round_first(
+            "w1", [(w1_raw[:], 0, low, nc.vector.tensor_copy), (w1_raw[:], 0, high, nc.scalar.copy)]
+        )
         w1_q = quantize_first(w1_grouped, "w1", PACK)
 
         x_codes = []
-
-        def gather_words(picked, j0, n):
+        for j0, n in GATHERS:
+            picked = keep.tile([P, n], U32, name=f"x_codes{j0}", align_bytes=64)
             nc.vector.tensor_copy(picked[:], words[:].bitcast(U32).indirect(offs_sb[:, list_columns(j0, n)]))
             x_codes.extend((picked, c0) for c0 in range(0, n, GROUP))
 
-        for j0, n in GATHERS[:-1]:
-            gather_words(keep.tile([P, n], U32, name=f"x_codes{j0}", align_bytes=64), j0, n)
-
-        w3_grouped = shared.tile([P, PACK, P, PACK], BF16, name="w3_grouped", align_bytes=64, offset=W3_GROUPED_AT)
-        round_first(
-            w3_grouped,
+        w3_grouped = round_first(
+            "w3",
             [
                 (w3_raw[0][:], 0, every, nc.scalar.copy),
                 (w3_raw[1][:], P // 2, low, nc.vector.tensor_copy),
@@ -139,8 +134,6 @@ def tile_picked_route2_glusilu_p_kernel(
             ],
         )
         w3_q = quantize_first(w3_grouped, "w3", 2)
-        last_codes = shared.tile([P, GATHERS[-1][1]], U32, name="last_codes", align_bytes=64, offset=LAST_CODES_AT)
-        gather_words(last_codes, *GATHERS[-1])
 
         def bank(b, shape):
             return psum.tile(shape, F32, name="bank", tag=f"bank{b}")
@@ -161,7 +154,7 @@ def tile_picked_route2_glusilu_p_kernel(
             return up[:].rearrange("p t n -> p n t")
 
         acts = shared.tile([P, S, PACK], F32, name="acts", align_bytes=64, offset=ACTS_AT)
-        w2_grouped = h_row[:, W2_FROM : W2_FROM + N * PACK]
+        w2_grouped = keep.tile([P, N, PACK], BF16, name="w2_grouped", align_bytes=64)
         rounded = h_row[:].rearrange("p (n t) -> p n t", t=PACK)
 
         def silu(k, b):
@@ -170,6 +163,11 @@ def tile_picked_route2_glusilu_p_kernel(
         def product(k, b):
             tokens = slice(k * GROUP, (k + 1) * GROUP)
             nc.vector.tensor_tensor(rounded[:, tokens, :], first_product(w3_q, k, b), acts[:, tokens, :], MULT)
+
+        w2_q = []
+
+        def quantize_w2(r):
+            w2_q.append(quantize(w2_grouped[:, r * P : (r + 1) * P, :].rearrange("p n t -> p (n t)"), f"w2_{r}"))
 
         h_q = {}
 
@@ -180,15 +178,14 @@ def tile_picked_route2_glusilu_p_kernel(
 
         y = [keep.tile([P, S], F32, name=f"y{r}") for r in range(N // P)]
 
-        def gated(c, r, b):
-            j0, n = CHUNKS[c]
+        def gated(j0, n, r, b):
             down = bank(b, [P, n])
             for c0 in range(0, n, 2 * GROUP):
                 width = min(2 * GROUP, n - c0)
                 nc.tensor.matmul_mx(
                     out=down[:, c0 : c0 + width],
-                    lhsT=w2_q[0][:, r * P : (r + 1) * P].bitcast(FP8X4),
-                    lhsT_scale=w2_q[1][:, r * P : (r + 1) * P],
+                    lhsT=w2_q[r][0][:].bitcast(FP8X4),
+                    lhsT_scale=w2_q[r][1][:],
                     rhs=h_q[j0 + c0][0].bitcast(FP8X4),
                     rhs_scale=h_q[j0 + c0][1],
                     start=True,
@@ -202,44 +199,46 @@ def tile_picked_route2_glusilu_p_kernel(
         def scatter_on_scalar(j0, n, r):
             nc.scalar.activation(places(j0, n, r), y[r][:, j0 : j0 + n], COPY)
 
-        nc.gpsimd.tensor_scalar(
-            w2_grouped.rearrange("p (n t) -> p n t", t=PACK),
-            w2_raw[:].rearrange("p t n -> p n t"),
-            1.0,
-            0.0,
-            op0=MULT,
-            op1=ADD,
-        )
+        for r in range(N // P):
+            nc.vector.tensor_copy(
+                w2_grouped[:, r * P : (r + 1) * P, :].rearrange("p (c i) t -> p c t i", i=PACK),
+                w2_raw[:, :, r * P : (r + 1) * P].rearrange("p t (c i) -> p c t i", i=PACK),
+            )
+        first, second, third = CHUNKS
+        third_a, third_b = (third[0], 2 * GROUP), (S - GROUP, GROUP)
+        quantize_w2(0)
         for k in range(4):
             silu(k, k)
         silu(4, 0)
         product(0, 4)
         product(1, 5)
-        w2_q = quantize(w2_grouped, "w2")
-        quantize_h(*CHUNKS[0])
-        gated(0, 0, 4)
+        quantize_w2(1)
+        quantize_h(*first)
         product(2, 7)
         product(3, 6)
+        gated(*first, 0, 4)
         silu(5, 2)
         silu(6, 3)
         silu(7, 0)
-        scatter_on_scalar(*CHUNKS[0], 0)
+        scatter_on_scalar(*first, 0)
         product(4, 1)
-        gated(0, 1, 5)
-        scatter_on_scalar(*CHUNKS[0], 1)
-        quantize_h(*CHUNKS[1])
-        gated(1, 0, 2)
+        gated(*first, 1, 5)
+        scatter_on_scalar(*first, 1)
+        quantize_h(*second)
         product(5, 7)
         product(6, 6)
+        gated(*second, 0, 2)
+        scatter_on_scalar(second[0], S - ON_VECTOR - second[0], 0)
+        quantize_h(*third_a)
         product(7, 1)
-        quantize_h(CHUNKS[2][0], 2 * GROUP)
-        quantize_h(S - GROUP, GROUP)
-        gated(1, 1, 3)
-        scatter_on_scalar(CHUNKS[1][0], S - ON_VECTOR - CHUNKS[1][0], 0)
-        scatter_on_scalar(*CHUNKS[1], 1)
-        gated(2, 0, 4)
-        gated(2, 1, 5)
+        gated(*second, 1, 3)
+        scatter_on_scalar(*second, 1)
+        quantize_h(*third_b)
+        gated(*third_a, 0, 4)
+        gated(*third_a, 1, 5)
+        gated(*third_b, 0, 0)
+        gated(*third_b, 1, 7)
         nc.vector.tensor_copy(places(S - ON_VECTOR, ON_VECTOR, 0), y[0][:, S - ON_VECTOR :])
         nc.sync.dma_start(out[0:P, :], windows[0][:])
-        scatter_on_scalar(*CHUNKS[2], 1)
+        scatter_on_scalar(*third, 1)
         nc.sync.dma_start(out[P : 2 * P, :], windows[1][:])

from contextlib import ExitStack

import concourse.mybir as mybir

K, T, S, H, N, U = 512, 4096, 1024, 512, 256, 2048
FLOPS = 2 * K * H * S * 2 + 2 * H * N * S

F32 = mybir.dt.float32
BF16 = mybir.dt.bfloat16
I32 = mybir.dt.int32
U32 = mybir.dt.uint32
U16 = mybir.dt.uint16
U8 = mybir.dt.uint8
FP8X4 = mybir.dt.float8_e4m3fn_x4
SILU = mybir.ActivationFunctionType.Silu
COPY = mybir.ActivationFunctionType.Copy
MULT = mybir.AluOpType.mult

P = 128
PACK = 4
LIST = 16
ROWS = K // 32
GROUP = 128
GATHERS = ((0, 512), (512, 512))
CHUNKS = ((0, 256), (256, 384), (640, 384))
ON_VECTOR = 416

OVERLAP = 64
ACTS_AT = 0
W3_FIRST_AT = ACTS_AT + S * PACK * 4 - OVERLAP
PLANES_AT = W3_FIRST_AT + PACK * (H // 2) * 4 - OVERLAP
W3_SECOND_AT = PLANES_AT + T - OVERLAP
H_ROW_AT = W3_SECOND_AT + PACK * (H // 2) * 4
W2_FROM = GROUP * PACK - OVERLAP // 2
GATE_AT = H_ROW_AT + S * PACK * 2
W1_AT = GATE_AT + OVERLAP - PACK * H * 4


def tile_picked_route2_glusilu_p_kernel(
    tc, x_words, x_scales, gate, w1, w3, w2, offs, dst, out
):
    nc = tc.nc
    with ExitStack() as ctx:
        keep = ctx.enter_context(tc.tile_pool(name="keep", bufs=1))
        shared = ctx.enter_context(tc.tile_pool(name="shared", bufs=1))
        psum = ctx.enter_context(tc.psum_pool(name="psum", bufs=1))

        offs_sb = keep.tile([P, S // LIST], U16, name="offs_sb")
        dst_sb = keep.tile([P, S // LIST], U16, name="dst_sb")
        planes = shared.tile([P, T], U8, name="planes", align_bytes=64, offset=PLANES_AT)
        windows = [keep.tile([P, U], F32, name=f"window{r}") for r in range(N // P)]
        zero = keep.tile([P, 1], F32, name="zero")

        nc.sync.dma_start(planes[P - ROWS :, :].bitcast(I32), x_scales[0].bitcast(I32))
        nc.sync.dma_start(offs_sb[:], offs)
        w1_raw = shared.tile([P, PACK, H], F32, name="w1_raw", align_bytes=64, offset=W1_AT)
        nc.sync.dma_start(w1_raw[:], w1.rearrange("(p j) c -> p j c", j=PACK))
        words = keep.tile([P, T], I32, name="words")
        nc.sync.dma_start(words[:], x_words[0].rearrange("p c r -> p (c r)").bitcast(I32))
        nc.sync.dma_start(dst_sb[:], dst)

        nc.vector.memset(zero[:], 0.0)
        nc.vector.memset(planes[: P - ROWS, :].bitcast(I32), 0)
        nc.scalar.activation(windows[1][:], zero[:].to_broadcast([P, U]), SILU)
        nc.vector.memset(windows[0][:], 0.0)

        picked_planes = keep.tile([P, S], U8, name="picked_planes")
        nc.vector.tensor_copy(picked_planes[:], planes[:].indirect(offs_sb[:]))
        x_planes = keep.tile([P, S], U8, name="x_planes", align_bytes=64)
        for q in range(ROWS // 4):
            r0 = P - ROWS + 4 * q
            nc.sync.dma_start(x_planes[32 * q : 32 * q + 4, :].bitcast(I32), picked_planes[r0 : r0 + 4, :].bitcast(I32))

        w3_rows = w3.rearrange("(p j) (u c) -> p u j c", j=PACK, u=2)
        w3_raw = []
        for u, offset in enumerate((W3_FIRST_AT, W3_SECOND_AT)):
            raw = shared.tile([P, PACK, H // 2], F32, name=f"w3_raw{u}", align_bytes=64, offset=offset)
            nc.sync.dma_start(raw[:], w3_rows[:, u])
            w3_raw.append(raw)

        h_row = shared.tile([P, S * PACK], BF16, name="h_row", align_bytes=64, offset=H_ROW_AT)
        w2_raw = h_row[:, W2_FROM : W2_FROM + 2 * PACK * N].bitcast(F32).rearrange("p (t n) -> p t n", t=PACK)
        gate_rows = shared.tile([P, S], F32, name="gate_rows", align_bytes=64, offset=GATE_AT)
        nc.sync.dma_start(w2_raw, w2.rearrange("(p t) n -> p t n", t=PACK))
        nc.sync.dma_start(gate_rows[:], gate)

        def list_columns(j0, n):
            return slice(j0 // LIST, (j0 + n) // LIST)

        def quantize(values, name):
            width = values.shape[1] // PACK
            codes = keep.tile([P, width], U32, name=f"{name}_codes", align_bytes=64)
            scales = keep.tile([P, width], U8, name=f"{name}_scales", align_bytes=64)
            nc.vector.quantize_mx(out=codes[:].bitcast(FP8X4), scales=scales[:], in_=values)
            return codes, scales

        def round_first(name, pieces):
            grouped = keep.tile([P, PACK, P, PACK], BF16, name=f"{name}_grouped", align_bytes=64)
            for raw, m0, slots, copy in pieces:
                m = slice(m0, m0 + raw.shape[2] // PACK)
                copy(
                    grouped[:, slots, m, :].rearrange("p t m j -> p m j t"),
                    raw.rearrange("p j (m t) -> p m j t", t=PACK)[:, :, :, slots],
                )
            return grouped

        def quantize_first(grouped, name, slots_a_call):
            stationary = []
            for t0 in range(0, PACK, slots_a_call):
                values = grouped[:, t0 : t0 + slots_a_call].rearrange("p t m j -> p (t m j)")
                codes, scales = quantize(values, f"{name}_{t0}")
                for t in range(slots_a_call):
                    stationary.append((codes[:, t * P : (t + 1) * P], scales[:, t * P : (t + 1) * P]))
            return stationary

        low, high, every = slice(0, 2), slice(2, 4), slice(0, 4)
        w1_grouped = round_first(
            "w1", [(w1_raw[:], 0, low, nc.vector.tensor_copy), (w1_raw[:], 0, high, nc.scalar.copy)]
        )
        w1_q = quantize_first(w1_grouped, "w1", PACK)

        x_codes = []
        for j0, n in GATHERS:
            picked = keep.tile([P, n], U32, name=f"x_codes{j0}", align_bytes=64)
            nc.vector.tensor_copy(picked[:], words[:].bitcast(U32).indirect(offs_sb[:, list_columns(j0, n)]))
            x_codes.extend((picked, c0) for c0 in range(0, n, GROUP))

        w3_grouped = round_first(
            "w3",
            [
                (w3_raw[0][:], 0, every, nc.scalar.copy),
                (w3_raw[1][:], P // 2, low, nc.vector.tensor_copy),
                (w3_raw[1][:], P // 2, high, nc.vector.tensor_copy),
            ],
        )
        w3_q = quantize_first(w3_grouped, "w3", 2)

        def bank(b, shape):
            return psum.tile(shape, F32, name="bank", tag=f"bank{b}")

        def first_product(w_q, k, b):
            up = bank(b, [P, PACK, GROUP])
            picked, c0 = x_codes[k]
            for t in range(PACK):
                nc.tensor.matmul_mx(
                    out=up[:, t, :],
                    lhsT=w_q[t][0].bitcast(FP8X4),
                    lhsT_scale=w_q[t][1],
                    rhs=picked[:, c0 : c0 + GROUP].bitcast(FP8X4),
                    rhs_scale=x_planes[:, k * GROUP : (k + 1) * GROUP],
                    start=True,
                    stop=True,
                )
            return up[:].rearrange("p t n -> p n t")

        acts = shared.tile([P, S, PACK], F32, name="acts", align_bytes=64, offset=ACTS_AT)
        w2_grouped = keep.tile([P, N, PACK], BF16, name="w2_grouped", align_bytes=64)
        rounded = h_row[:].rearrange("p (n t) -> p n t", t=PACK)

        def silu(k, b):
            nc.scalar.activation(acts[:, k * GROUP : (k + 1) * GROUP, :], first_product(w1_q, k, b), SILU)

        def product(k, b):
            tokens = slice(k * GROUP, (k + 1) * GROUP)
            nc.vector.tensor_tensor(rounded[:, tokens, :], first_product(w3_q, k, b), acts[:, tokens, :], MULT)

        w2_q = []

        def quantize_w2(r):
            w2_q.append(quantize(w2_grouped[:, r * P : (r + 1) * P, :].rearrange("p n t -> p (n t)"), f"w2_{r}"))

        h_q = {}

        def quantize_h(j0, n):
            codes, scales = quantize(h_row[:, j0 * PACK : (j0 + n) * PACK], f"h{j0}")
            for c0 in range(0, n, 2 * GROUP):
                h_q[j0 + c0] = (codes[:, c0 : min(n, c0 + 2 * GROUP)], scales[:, c0 : min(n, c0 + 2 * GROUP)])

        y = [keep.tile([P, S], F32, name=f"y{r}") for r in range(N // P)]

        def gated(j0, n, r, b):
            down = bank(b, [P, n])
            for c0 in range(0, n, 2 * GROUP):
                width = min(2 * GROUP, n - c0)
                nc.tensor.matmul_mx(
                    out=down[:, c0 : c0 + width],
                    lhsT=w2_q[r][0][:].bitcast(FP8X4),
                    lhsT_scale=w2_q[r][1][:],
                    rhs=h_q[j0 + c0][0].bitcast(FP8X4),
                    rhs_scale=h_q[j0 + c0][1],
                    start=True,
                    stop=True,
                )
            nc.vector.tensor_tensor(y[r][:, j0 : j0 + n], down[:], gate_rows[:, j0 : j0 + n], MULT)

        def places(j0, n, r):
            return windows[r][:].indirect(dst_sb[:, list_columns(j0, n)])

        def scatter_on_scalar(j0, n, r):
            nc.scalar.activation(places(j0, n, r), y[r][:, j0 : j0 + n], COPY)

        for r in range(N // P):
            nc.vector.tensor_copy(
                w2_grouped[:, r * P : (r + 1) * P, :].rearrange("p (c i) t -> p c t i", i=PACK),
                w2_raw[:, :, r * P : (r + 1) * P].rearrange("p t (c i) -> p c t i", i=PACK),
            )
        first, second, third = CHUNKS
        third_a, third_b = (third[0], 2 * GROUP), (S - GROUP, GROUP)
        quantize_w2(0)
        for k in range(4):
            silu(k, k)
        silu(4, 0)
        product(0, 4)
        product(1, 5)
        quantize_w2(1)
        quantize_h(*first)
        product(2, 7)
        product(3, 6)
        gated(*first, 0, 4)
        silu(5, 2)
        silu(6, 3)
        silu(7, 0)
        scatter_on_scalar(*first, 0)
        product(4, 1)
        gated(*first, 1, 5)
        scatter_on_scalar(*first, 1)
        quantize_h(*second)
        product(5, 7)
        product(6, 6)
        gated(*second, 0, 2)
        scatter_on_scalar(second[0], S - ON_VECTOR - second[0], 0)
        quantize_h(*third_a)
        product(7, 1)
        gated(*second, 1, 3)
        scatter_on_scalar(*second, 1)
        quantize_h(*third_b)
        gated(*third_a, 0, 4)
        gated(*third_a, 1, 5)
        gated(*third_b, 0, 0)
        gated(*third_b, 1, 7)
        nc.vector.tensor_copy(places(S - ON_VECTOR, ON_VECTOR, 0), y[0][:, S - ON_VECTOR :])
        nc.sync.dma_start(out[0:P, :], windows[0][:])
        scatter_on_scalar(*third, 1)
        nc.sync.dma_start(out[P : 2 * P, :], windows[1][:])
